import numpy as np, ml_dtypes
CORES = [1,5,17,21,33,37,49,53]
N = 8
BF = ml_dtypes.bfloat16
def gentries(a):
    return np.ascontiguousarray(a.reshape(8, 16, -1).transpose(0, 2, 1)).reshape(8, -1)
def gtable(e):
    e = np.asarray(e); return np.ascontiguousarray(e.reshape(8, -1, 16).transpose(0, 2, 1)).reshape(128, -1).astype(np.int32)
W, B, L, S, RO, ST = 4096, 1024, 128, 32, 4, 3
def parts(rng):
    X = rng.integers(0, 201, (N, 8, 1, W)) + rng.integers(0, 56, (N, 8, 16, W))
    c = rng.integers(0, 101, (N, 8, 1, L)) + rng.integers(0, 56, (N, 8, 16, L))
    return X, rng.integers(0, W, (N, 8, 16, B)), rng.integers(0, W, (N, 8, 16, L)), c, rng.integers(0, B, (N, 8, L))
def pack(X, TT, T, c, b):
    return {"clk": X.reshape(N, 128, W).astype(np.float32).astype(BF), "ttab": TT.reshape(N, 128, B).astype(np.int32), "trav": T.reshape(N, 128, L).astype(np.int32),
            "last": c.reshape(N, 128, L).astype(np.float32).astype(BF), "slot": np.stack([gtable(a) for a in b])}
def setup_inputs(rng):
    return pack(*parts(rng))
def setup_inputs_spread(rng):
    pw = rng.choice(np.array([0.25, 0.5, 1.0, 2.0, 4.0]), (N, 8, 1, 1))
    sz = np.exp2(rng.integers(0, 8, (N, 8, 1, W)))
    X = np.clip(np.floor(256 * rng.random((N, 8, 1, W)) ** pw + sz * (rng.random((N, 8, 16, W)) - 0.5)), 0, 255).astype(np.int64)
    c = np.minimum(np.floor(256 * rng.random((N, 8, 1, L)) ** 2 * rng.random((N, 8, 16, L))), 255).astype(np.int64)
    pt = rng.choice(np.array([0.5, 1.0, 3.0]), (N, 8, 16, 1))
    T = np.minimum(np.floor(W * rng.random((N, 8, 16, L)) ** pt), W - 1).astype(np.int64)
    TT = np.minimum(np.floor(W * rng.random((N, 8, 16, B)) ** pt[::-1]), W - 1).astype(np.int64)
    b = np.minimum(np.floor(B * rng.random((N, 8, L)) ** 2), B - 1).astype(np.int64)
    return pack(X, TT, T, c, b)
def setup_inputs_ends(rng):
    X = 255 * rng.integers(0, 2, (N, 8, 16, W)); TT = (W - 1) * rng.integers(0, 2, (N, 8, 16, B)); T = (W - 1) * rng.integers(0, 2, (N, 8, 16, L))
    c = 255 * rng.integers(0, 2, (N, 8, 16, L)); b = (B - 1) * rng.integers(0, 2, (N, 8, L))
    for q in range(N):
        for g, size in ((3, 1), (7, 4)):
            P = np.sort(np.append(rng.permutation(15)[:size - 1], 15)); v = np.zeros(16, np.int64); v[P] = 255
            X[q, g] = (255 - v)[:, None]
            if size > 1:
                for t in (0, W - 1):
                    for s in (0, B - 1): X[q, g, int(np.argmin(v)), (((t * 511) >> 3) + 613 * int(P[0]) + 37 * s) & (W - 1)] = 254
            X[q, g, :, 0] = v; X[q, g, :, W - 1] = v
            c[q, g, P] = 255 * (np.arange(L) % 4 == 1)
            T[q, g, :, L - 1] = W - 1; b[q, g, L - 1] = B - 1
        X[q, 5] = 255; c[q, 5] = 0
        X[q, 6] = 255; c[q, 6] = 255
        if q % 2: c[q, 6, 15, L - 1] = 0
    return pack(X, TT, T, c, b)
def setup_inputs_corners(rng):
    X, TT, T, c, b = parts(rng); j = np.arange(W); i = np.arange(L)
    T[:, 0] = np.where(i % 2 == 0, 0, W - 1); b[:, 0] = np.where(i % 3 == 0, 0, B - 1)
    T[:, 1] = rng.integers(0, W, (N, 1, L))
    same = rng.integers(0, W, (N, 16, 1)); T[:, 2] = same; TT[:, 2] = same
    c[:, 3] = 255; b[:, 3] = (B - 99 + rng.integers(0, 100, (N, L))) & (B - 1)
    X[:, 4] = np.maximum(X[:, 4], 1); c[:, 4] = 0
    r = rng.integers(1, 255, (N, 16, 1)); X[:, 5] = r; c[:, 5] = r + rng.integers(-1, 2, (N, 16, L))
    o = np.argsort(rng.random((N, 16, W)), axis=1)
    X[:, 6] = np.where(j % 4 == 0, 100, np.where(j % 4 == 2, np.where(o < rng.integers(11, 13, (N, 1, W)), 120, 50), np.where(o < rng.integers(8, 11, (N, 1, W)), 101, 99)))
    T[:, 6] = 4 * rng.integers(0, W // 4, (N, 16, L)); TT[:, 6] = 2 * rng.integers(0, W // 2, (N, 16, B)) + 1; c[:, 6] = 0
    T[:, 7] = np.where(rng.random((N, 16, L)) < 0.5, (W - 1) * rng.integers(0, 2, (N, 16, L)), T[:, 7]); b[:, 7] = np.where(rng.random((N, L)) < 0.5, B - 1, b[:, 7])
    for a in (X, TT, T, c, b):
        for q in range(N): a[q] = np.roll(a[q], q, axis=0)
    return pack(X, TT, T, c, b)
def setup_inputs_crowd(rng):
    X, TT, T, c, b = parts(rng); one = rng.integers(0, B, (N, 8)); i = np.arange(L)
    for g in (0, 1, 2, 7): b[:, g] = one[:, g, None]
    b[:, 1, 0] = (one[:, 1] + 1) & (B - 1); b[:, 2, L - 1] = (one[:, 2] + 1) & (B - 1)
    b[:, 3] = one[:, 3, None] ^ rng.integers(0, 4, (N, L))
    b[:, 4] = B - 1; T[:, 4] = T[:, 4, :, :1].copy(); c[:, 4] = 255
    b[:, 5] = np.where(i % 2 == 0, one[:, 5, None], B - 1 - one[:, 5, None])
    b[:, 6] = 0; T[:, 6] = T[:, 6, :, :1].copy(); c[:, 6] = 255; c[:, 6, :, L - 1] = 0; X[:, 6] = np.maximum(X[:, 6], 1)
    for q in range(N):
        z = int(rng.integers(0, W)); X[q, 6, :, z] = 1; T[q, 6, :, L - 1] = z; TT[q, 6, :, 0] = z
    T[:, 7] = T[:, 7, :, :1].copy(); c[:, 7] = 0
    return pack(X, TT, T, c, b)
def high(rng, X, TT, T, c, g):
    o = np.argsort(rng.random((N, 16, W)), axis=1)
    X[:, g] = 255 - ((o < rng.integers(3, 7, (N, 1, W))) & (np.arange(W) % 2 == 1))
    T[:, g] = 2 * rng.integers(0, W // 2, (N, 16, L)); TT[:, g] = 2 * rng.integers(0, W // 2, (N, 16, B)); c[:, g] = rng.integers(253, 256, (N, 16, L))
def near(rng, X, TT, T, c, b, g):
    t = np.arange(W); v = np.zeros(16, np.int64); v[0] = 255; v[15] = 255
    for q in range(N):
        s = rng.permutation(B)[:L]; two = []
        for p, lo, hi in ((0, W - 8, W - 1), (15, 0, 8)):
            n = (((t * 511) >> 3)[None, :] + 613 * p + 37 * s[:, None]) & (W - 1)
            ok = (n >= lo) & (n <= hi) & (t > 8) & (t < W - 8)
            two.append(np.argmax(ok * rng.random((L, W)), axis=1))
        X[q, g] = (255 - v)[:, None]; X[q, g, 1, W - 8:] = 254
        for a in two: X[q, g][:, a] = v[:, None]
        T[q, g, :8] = two[0]; T[q, g, 8:] = two[1]; TT[q, g][:, s] = T[q, g]; b[q, g] = s
        c[q, g, 0] = rng.integers(0, 255, L); c[q, g, 15] = rng.integers(0, 255, L)
def setup_inputs_ties(rng):
    X, TT, T, c, b = parts(rng); o = rng.permutation(8)
    base = np.array([0, 0, 1, 64, 127, 127, 252, 252])[o].reshape(1, 8, 1, 1)
    X = base + rng.integers(0, 3, (N, 8, 1, W)) + (rng.random((N, 8, 16, W)) < 0.25)
    c = base + rng.integers(0, 2, (N, 8, 16, L))
    few = rng.integers(0, W, 8); T[:, ::2] = few[rng.integers(0, 8, (N, 4, 16, L))]
    high(rng, X, TT, T, c, int(np.argmax(o == 7))); near(rng, X, TT, T, c, b, int(np.argmax(o == 5)))
    return pack(X, TT, T, c, b)
def check_inputs(d):
    bad = []
    for k, lo, hi in (("clk", 0, 255), ("ttab", 0, W - 1), ("trav", 0, W - 1), ("last", 0, 255), ("slot", 0, B - 1)):
        a = np.asarray(d[k]).astype(np.float64)
        if not (np.min(a) >= lo and np.max(a) <= hi): bad.append("range of " + k)
        if np.any(a != np.floor(a)): bad.append("whole numbers in " + k)
    return bad
def pick(X, n):
    return np.take_along_axis(X, n.reshape(N, 8, 1, 16 * L), 3).reshape(N, 8, 16, 16, L)
def reference(clk, ttab, trav, last, slot):
    X = clk.astype(np.float32).astype(np.int32).reshape(N, 8, 16, W); TT = ttab.astype(np.int32).reshape(N, 8, 16, B)
    T = trav.astype(np.int32).reshape(N, 8, 16, L); c = last.astype(np.float32).astype(np.int32).reshape(N, 8, 16, L)
    b = np.stack([gentries(a) for a in slot]).astype(np.int32)
    bound = np.full((N, 8), 9, np.int32); row = np.arange(16, dtype=np.int32)[None, None, :, None]; lane = np.arange(L, dtype=np.int32)
    for v in range(RO):
        if v > 0:
            T = np.roll(T, ST, axis=0); c = np.roll(c, ST, axis=0); b = np.roll(b, ST, axis=0)
        at = np.broadcast_to(b[:, :, None, :], (N, 8, 16, L))
        H = np.take_along_axis(TT, at, 3); x = pick(X, T); y = pick(X, H)
        take = np.sum(y >= x, axis=2) >= bound[:, :, None, None]
        T = np.where(take, H, T); z = np.where(take[:, :, None], y, x)
        m = np.min(z, axis=3); M = np.max(z, axis=3)
        free = m > c; c = m
        n = (((T * (2 * m + 1)) >> 3) + 613 * row + 37 * at) & (W - 1)
        e = pick(X, n)
        ready = free & (np.sum(e >= m[:, :, :, None], axis=2) >= 12)
        T = np.where(ready, n, T)
        score = np.where(ready, np.sum(np.abs(e - M[:, :, :, None]), axis=2), -1)
        best = np.argmax(score, axis=2)
        has = np.any(ready, axis=2)
        low = np.argmax(b[:, :, :, None] == b[:, :, None, :], axis=3)
        np.put_along_axis(TT, at, np.take_along_axis(T, np.broadcast_to(low[:, :, None, :], (N, 8, 16, L)), 3), 3)
        col = np.broadcast_to((S * lane + (np.sum(M, axis=2) & (S - 1)))[:, :, None, :], (N, 8, 16, L))
        np.put_along_axis(X, col, (np.take_along_axis(X, col, 3) + M) >> 1, 3)
        b = np.where(has, np.take_along_axis(n, best[:, :, None, :], 2)[:, :, 0] & (B - 1), (b + 97) & (B - 1)).astype(np.int32)
        bound = 9 + (np.sum(~has, axis=2) & 1)
    return {"yclk": X.reshape(N, 128, W).astype(np.float32).astype(BF), "yttab": TT.reshape(N, 128, B).astype(np.float32), "ytrav": T.reshape(N, 128, L).astype(np.float32),
            "ylast": c.reshape(N, 128, L).astype(np.float32).astype(BF), "yslot": np.stack([gtable(a) for a in b]).astype(np.float32)}

@@ -1,0 +1,559 @@
+from concourse.mybir import AluOpType as A, AxisListType, ActivationFunctionType as F
+
+N, STEP, VISITS = 8, 3, 4
+W, B, L, H = 4096, 1024, 128, 64
+RW = 2 * H
+F16 = "float16"
+
+SCRATCH = {
+    "X": ("sbuf", [128, W], "bfloat16"), "X2": ("sbuf", [128, W], "bfloat16"),
+    "tt32": ("sbuf", [128, B], "int32"), "TT": ("sbuf", [128, B + L], "float32"),
+    "trav0": ("sbuf", [128, L], "int32"), "last0": ("sbuf", [128, L], "bfloat16"), "slot0": ("sbuf", [128, 8], "int32"),
+    "mS": ("sbuf", [128, 16 * L], "bfloat16"), "MS": ("sbuf", [128, 16 * L], "bfloat16"),
+    "bB": ("sbuf", [128, L], F16), "eq0": ("sbuf", [128, 256], F16), "eq1": ("sbuf", [128, 512], F16),
+    "es0": ("sbuf", [128, 256], F16), "es1": ("sbuf", [128, 512], F16),
+    "If": ("sbuf", [128, 128], "float32"), "Ig": ("sbuf", [128, 128], "float32"), "Ih": ("sbuf", [128, 128], "bfloat16"),
+    "mh": ("sbuf", [128, 128], "bfloat16"), "xo": ("sbuf", [128, L], "bfloat16"),
+    "Ik": ("sbuf", [128, 128], "bfloat16"), "ui": ("sbuf", [128, 8], "int32"), "uj": ("sbuf", [128, 8], "int32"),
+    "uk": ("sbuf", [128, 8], "int32"), "ju": ("sbuf", [128, 8], "uint16"),
+    "xs": ("sbuf", [128, L], "int32"), "xt": ("sbuf", [128, L], "int32"),
+    "par": ("sbuf", [128, 1], "float32"), "yl": ("sbuf", [128, L], "bfloat16"),
+    "pi": ("sbuf", [128, 1], "int32"), "pj": ("sbuf", [128, 2], "int32"), "col": ("sbuf", [128, 12], "float32"),
+    "BT": ("sbuf", [128, B], "float32"), "i144": ("sbuf", [128, 144], "float32"), "iog": ("sbuf", [128, 128], "float32"),
+    "iom": ("sbuf", [128, H], "float32"), "i16": ("sbuf", [128, 8], "float32"),
+    "id0": ("sbuf", [128, 256], "float32"), "id1": ("sbuf", [128, 512], "float32"),
+    "S1": ("sbuf", [128, 144], "bfloat16"), "S2": ("sbuf", [128, 144], "bfloat16"), "S16": ("sbuf", [128, 144], "bfloat16"),
+    "I1": ("sbuf", [128, 128], "bfloat16"), "In": ("sbuf", [128, 128], "bfloat16"), "I32": ("sbuf", [128, 128], "bfloat16"),
+    "BOf": ("sbuf", [128, 128], "float32"),
+    "lb": ("sbuf", [128, 16 * VISITS], "uint16"), "sb": ("sbuf", [128, 16 * VISITS], "uint16"),
+    "DF": ("sbuf", [128, B], "float32"), "BOh": ("sbuf", [128, 128], F16), "BOm": ("sbuf", [128, 128], "bfloat16"),
+    "MK": ("sbuf", [128, H], "bfloat16"), "PC": ("sbuf", [128, H], "bfloat16"), "ones": ("sbuf", [128, H], "bfloat16"),
+    "RS": ("sbuf", [128, 512], "bfloat16"), "RM": ("sbuf", [128, 512], "bfloat16"), "RK": ("sbuf", [128, H], "float32"),
+    "L32": ("sbuf", [128, 8], "float32"), "DS": ("sbuf", [128, 8], "float32"), "OB": ("sbuf", [128, 4], "uint16"),
+    "D0": ("sbuf", [128, 256], F16), "D1": ("sbuf", [128, 512], F16),
+}
+for _h in range(2):
+    for _n, _w, _d in (("U", H, "uint16"), ("Hu", H, "uint16"), ("dH", H, "float32"), ("A8", H, "float32"),
+                       ("x", 16 * H, "bfloat16"), ("cy", 16 * H, "bfloat16"), ("z", 16 * H, "bfloat16"),
+                       ("e", 16 * H, "bfloat16"), ("cm", 16 * H, "bfloat16"), ("ab", 16 * H, "bfloat16"),
+                       ("Tu", H, "uint16"), ("s", H, "int32"), ("n", H, "int32"), ("nu", H, "uint16"),
+                       ("rel", H, "bfloat16"), ("rdy", H, "bfloat16"), ("td", H, "float32"), ("tk", H, "float32"),
+                       ("kT", H, "float32"), ("kr", H, "float32"), ("qT", H, "bfloat16"), ("oh", H, "bfloat16"),
+                       ("sel", H, F16), ("ex", H, "float32"), ("nm", H, "int32"), ("df", H, "float32"),
+                       ("bl", 4, "float32"), ("of", 4, "float32"), ("ou", 4, "uint16")):
+        SCRATCH["h" + _n] = ("sbuf", [128, 2 * _w], _d)
+    for _v in range(VISITS):
+        SCRATCH["land%d_%d" % (_v, _h)] = ("sbuf", [128, RW], "float32")
+        SCRATCH["send%d_%d" % (_v, _h)] = ("sbuf", [128, RW], "float32")
+for _b in range(8):
+    SCRATCH["pb%d" % _b] = ("psum", [128, 512], "float32")
+
+DMAS = ["slot", "trav", "last", "tt", "clk", "cp", "yclk", "ytt", "ytr0", "ytr1", "ysl0", "ysl1", "yla"]
+SEMAPHORES = ["cV", "cS", "cP", "cG", "sent"] + ["d" + d for d in DMAS] + \
+             ["arr%d_%d_%d" % (v, h, k) for v in range(1, VISITS) for h in range(2) for k in range(2)]
+
+MODEL = {"cyc": 0.83e-3 * 1.25, "pe": 0.6e-3, "g": 1.56, "sc": 3.8, "fix": 0.03, "same": 0.06, "cross": 0.1,
+         "rem": 3.0, "dma0": 2.0, "bw": 250e3}
+CONFIG = {"seed": 0, "noise": 0.0, "bias": 0.3, "slack": 0.1, "pre": True, "split": True, "dh": False, "rel": False, "xs": False, "clk1": True}
+
+
+def build(T, send):
+    ops, now = [], {}
+
+    def ap(name, a=0, b=None, step=None):
+        b = T[name].shape[1] if b is None else b
+        return (name, a, b, T[name][:, a:b] if step is None else T[name][:, a:b:step])
+
+    def slot(name, v, h):
+        return ap(name, 16 * v + 8 * h, 16 * v + 8 * h + 4)
+
+    def val(x):
+        return x[3] if isinstance(x, tuple) else x
+
+    def aps(*xs):
+        return [x for x in xs if isinstance(x, tuple)]
+
+    def two(*xs):
+        return all(SCRATCH[x[0]][2] in ("bfloat16", "float16", "uint16") for x in xs)
+
+    def cnt(x):
+        return x[3].shape[1]
+
+    def add(eng, fn, rd, wr, kind, n, **kw):
+        ops.append(dict(eng=eng, fn=fn, rd=rd, wr=wr, kind=kind, n=n, **kw, **now))
+        return ops[-1]
+
+    def ind(win, off):
+        return win[3].indirect(off[3])
+
+    def tt(out, a, b, op):
+        both = SCRATCH[a[0]][0] == "sbuf" and SCRATCH[b[0]][0] == "sbuf"
+        return add("V", lambda q, e: [q.tensor_tensor(out[3], a[3], b[3], op)], [a, b], [out], "v", cnt(out) * (2 if both else 1))
+
+    def ts(out, a, s1, s2, op0, op1=None):
+        def fn(q, e):
+            if op1 is None:
+                return [q.tensor_scalar(out[3], a[3], val(s1), None, op0)]
+            return [q.tensor_scalar(out[3], a[3], val(s1), val(s2), op0, op1)]
+        return add("V", fn, [a] + aps(s1, s2), [out], "v", cnt(out) * (0.5 if two(out, a) else 1))
+
+    def cp(out, a):
+        return add("V", lambda q, e: [q.tensor_copy(out[3], a[3])], [a], [out], "v", cnt(out) * (0.5 if two(out, a) else 1))
+
+    def aff(out, a, mul, plus, eng="VS"):
+        def fn(q, e):
+            if e == "V":
+                return [q.tensor_scalar(out[3], a[3], float(mul), float(plus), A.mult, A.add)]
+            return [q.activation(out[3], a[3], F.Identity, bias=float(plus), scale=float(mul))]
+        return add(eng, fn, [a], [out], "v", cnt(out))
+
+    def ms(out, c):
+        return add("V", lambda q, e: [q.memset(out[3], c)], [], [out], "v", cnt(out) * (0.5 if two(out) else 1))
+
+    def scan(out, d0, d1, init, op0, op1):
+        return add("V", lambda q, e: [q.tensor_tensor_scan(out[3], d0[3], d1[3], init, op0, op1)], [d0, d1], [out], "v",
+                   cnt(out) * (0.5 if two(out, d0, d1) else 1))
+
+    def vt(out, a):
+        return add("V", lambda q, e: [q.transpose(out[3], a[3])], [a], [out], "v", cnt(out) * (0.5 if two(out, a) else 1))
+
+    def gat(out, win, off, eng):
+        def fn(q, e):
+            if e == "V":
+                return [q.tensor_copy(out[3], ind(win, off))]
+            return [q.activation(out[3], ind(win, off), F.Copy)]
+        return add(eng, fn, [win, off], [out], "g", cnt(out))
+
+    def gtt(out, win, off, b, op):
+        return add("V", lambda q, e: [q.tensor_tensor(out[3], ind(win, off), b[3], op)], [win, off, b], [out], "g", cnt(out))
+
+    def sct(win, off, a):
+        return add("V", lambda q, e: [q.tensor_copy(ind(win, off), a[3])], [off, a], [win], "sc", cnt(a))
+
+    def mm(groups, part=None):
+        rd, n = [], 0
+        for out, terms in groups:
+            for l, r in terms:
+                rd += (l if isinstance(l, list) else [l]) + [r]
+                n += max(64, cnt(r)) * (4 if SCRATCH[r[0]][2] == "float32" else 1)
+        rd = [x for x in rd if isinstance(x, tuple)]
+
+        def fn(q, e):
+            res = []
+            for k, (out, terms) in enumerate(groups):
+                for i, (l, r) in enumerate(terms):
+                    lt = l[l[0]()] if isinstance(l, list) else l
+                    st, sp = i == 0, i == len(terms) - 1
+                    if part == "open":
+                        st, sp = k == 0, False
+                    elif part == "begin":
+                        sp = False
+                    elif part == "more":
+                        st = sp = False
+                    elif part == "end":
+                        st = False
+                    elif part == "close":
+                        st, sp = False, k == len(groups) - 1
+                    ins = q.matmul(out[3], lt[3], r[3], st, sp)
+                res.append(ins)
+            return res
+        return add("P", fn, rd, [o for o, t in groups], "pe", n)
+
+    def iota(out, pattern, base, ch):
+        def fn(q, e):
+            if SCRATCH[out[0]][2] == "int32":
+                return [q.iota(out[3], pattern, base, ch)]
+            return [q.iota(out[3], pattern, base, ch, allow_small_or_imprecise_dtypes=True)]
+        return add("G", fn, [], [out], "io", cnt(out))
+
+    def dma(eng, sem, out, a, rd, wr, nbytes):
+        return add(eng, lambda q, e: [q.dma_start(out, a)], rd, wr, "dma", nbytes, sem="d" + sem)
+
+    dma("S", "slot", T.slot0[:], T.slot[:], [], [ap("slot0")], 4096)
+    dma("S", "trav", T.trav0[:], T.trav[:], [], [ap("trav0")], 65536)
+    if CONFIG["clk1"]:
+        first = dma("Y", "clk", T.X[:], T.clk[:], [], [ap("X")], 1048576)
+        dma("Y", "tt", T.tt32[:], T.ttab[:], [], [ap("tt32")], 1572864)["behind"] = first
+    else:
+        first = dma("Y", "tt", T.tt32[:], T.ttab[:], [], [ap("tt32")], 524288)
+        dma("Y", "clk", T.X[:], T.clk[:], [], [ap("X")], 1572864)["behind"] = first
+    dma("S", "last", T.last0[:], T.last[:], [], [ap("last0")], 1572864)
+
+    def col(i):
+        return ap("col", i, i + 1)
+    P, G, BA, PC, HI, TH = col(0), col(1), col(2), col(3), col(4), 5
+    iota(ap("pi"), [[0, 1]], 0, 1)
+    iota(ap("i144"), [[1, 144]], 0, -1)
+    iota(ap("BT"), [[1, B]], 0, 0)
+    iota(ap("iog"), [[1, 8], [0, 16]], 0, 0)
+    iota(ap("iom"), [[0, 4], [1, 16]], 0, 0)
+    iota(ap("i16"), [[16, 8]], 0, 0)
+    iota(ap("id0"), [[-16, 4], [1, 64]], 0, 0)
+    iota(ap("id1"), [[-16, 4], [1, 128]], -64, 0)
+    ts(ap("pj", 0, 1), ap("pi"), 15, None, A.bitwise_and)
+    ts(ap("pj", 1, 2), ap("pi"), 4, None, A.logical_shift_right)
+    cp(ap("col", 0, 2), ap("pj"))
+    aff(BA, P, 8 * 613, 0)
+    aff(PC, P, -1, 16)
+    ts(HI, P, 8.0, 16.0, A.is_ge, A.mult)
+    ms(col(TH), 56.0)
+    aff(col(TH + 1), HI, 1, 40)
+    aff(col(TH + 2), HI, -1, 56)
+    ms(col(TH + 3), 40.0)
+    ts(ap("S1"), ap("i144"), P, 15.0, A.add, A.is_equal)
+    aff(ap("S2"), ap("S1"), 2, 0)
+    aff(ap("S16"), ap("S1"), 16, 0)
+    ts(ap("I1"), ap("i144", 0, 128), 0.0, None, A.is_equal)
+    aff(ap("In"), ap("I1"), -1, 0)
+    aff(ap("I32"), ap("I1"), 32, 0)
+    ts(ap("BOf"), ap("iog"), G, None, A.is_equal)
+    cp(ap("BOh"), ap("BOf"))
+    iota(ap("DF", 0, B - 97), [[1, B - 97]], 97, 0)
+    iota(ap("DF", B - 97, B), [[1, 97]], 0, 0)
+    aff(ap("BOm"), ap("BOf"), -2, 0)
+    ts(ap("MK"), ap("iom"), P, 16384.0, A.not_equal, A.mult)
+    ts(ap("PC"), ap("iom"), 0.0, PC, A.mult, A.add)
+    ms(ap("ones"), 1.0)
+    ms(ap("RS"), 0.0)
+    ms(ap("RS", 0, 512, 16), 65536.0)
+    ms(ap("RM"), 1.0)
+    ms(ap("RM", 0, 512, 16), 0.0)
+    ms(ap("RK"), 1048576.0)
+    ms(ap("RK", 0, H, 16), 65536.0)
+    aff(ap("Ik"), ap("I1"), 65536, 0)
+    aff(ap("If"), ap("I1"), 1, 0)
+    if CONFIG["dh"] or CONFIG["rel"]:
+        aff(ap("Ig"), ap("I1"), -1, 0)
+    if CONFIG["xs"]:
+        aff(ap("Ih"), ap("I1"), 0.5, 0)
+        aff(ap("mh"), ap("I1"), 0, -0.5)
+    ts(ap("L32"), ap("i16"), P, 32.0, A.add, A.mult)
+    aff(ap("DS"), ap("L32"), 2.0 ** -18, 0.125)
+    ts(ap("OB"), ap("i16", 0, 4), 15.0, None, A.add)
+    for h in range(2):
+        d, w = "D%d" % h, H * (h + 1)
+        ts(ap(d), ap("id%d" % h), P, 8191.0, A.is_equal, A.mult)
+        ts(ap(d), ap(d), 1.0, None, A.add)
+        ms(ap(d, 0, 4 * w, w), 0.0)
+    ms(ap("par"), 1.0)
+    for h in range(2):
+        r = "land0_%d" % h
+        cp(ap(r, 0, H), ap("trav0", H * h, H * h + H))
+        cp(slot("lb", 0, h), ap("slot0", 4 * h, 4 * h + 4))
+        aff(ap(r, H, RW), ap("last0", H * h, H * h + H), 2, 1)
+    for q in range(4):
+        cp(ap("TT", 256 * q, 256 * q + 256), ap("tt32", 256 * q, 256 * q + 256))
+
+    X, TT = ap("X"), ap("TT", 0, B)
+
+    def smat(name, k):
+        return ap(name, 15 - k, 143 - k)
+
+    for v in range(VISITS):
+        last = v == VISITS - 1
+        now["visit"] = v
+
+        def b(name, h, a=0, z=None, step=None):
+            w = SCRATCH["h" + name][1][1] // 2
+            return ap("h" + name, w * h + a, w * h + (w if z is None else z), step)
+
+        def land(h, *r):
+            return ap("land%d_%d" % (v, h), *r)
+
+        def snd(h, *r):
+            return ap("send%d_%d" % (v, h), *r)
+
+        def pv(i):
+            return ap("pb7", H * i, H * i + H)
+
+        def mrow(name, h):
+            return ap(name, 1024 * h + 15, 1024 * h + 1024, 16)
+
+        for h in range(2):
+            if v:
+                for k, r in enumerate((land(h), slot("lb", v, h))):
+                    add("R", None, [], [r], "arr", 0, sem="arr%d_%d_%d" % (v, h, k), after=("send", v - 1, h, k))
+            cp(b("U", h), land(h, 0, H))
+            bo = slot("lb", v, h)
+            tab = ap("tt32") if v == 0 and CONFIG["clk1"] else TT
+            gat(b("Hu", h), tab, bo, "V")
+            for q in range(2):
+                gat(b("x", h, 512 * q, 512 * q + 512), X, b("U", h, 32 * q, 32 * q + 32), "VS")
+                gtt(b("cy", h, 512 * q, 512 * q + 512), X, b("Hu", h, 32 * q, 32 * q + 32), b("x", h, 512 * q, 512 * q + 512), A.is_ge)
+            if CONFIG["dh"]:
+                gat(b("dH", h), TT, bo, "VS")
+                mm([(ap("pb%d" % (4 + h), H, 2 * H), [(ap("If"), b("dH", h)), (ap("Ig"), land(h, 0, H))])])
+            else:
+                gtt(b("dH", h), tab, bo, land(h, 0, H), A.subtract)
+            add("S", lambda q, e, o=b("A8", h), bo=bo: [q.activation(o[3], ind(ap("BT"), bo), F.Identity, bias=BA[3], scale=296.0)],
+                [ap("BT"), bo, BA], [b("A8", h)], "g", H)
+            gat(b("df", h), ap("DF"), bo, "VS")
+            cp(b("bl", h), bo)
+            gat(ap("bB", H * h, H * h + H), ap("BT"), bo, "V")
+        for h in range(2):
+            c1 = ap("pb%d" % (4 + h), 3 * H, 4 * H)
+            mm([(c1, [(smat("S2", k), b("cy", h, k, 1024, 16)) for k in range(16)])])
+            if CONFIG["dh"]:
+                ts(b("tk", h), c1, ap("par"), 19.0, A.add, A.is_ge)
+                tt(pv(5), b("tk", h), ap("pb%d" % (4 + h), H, 2 * H), A.mult)
+            else:
+                ts(pv(4), c1, ap("par"), 19.0, A.add, A.is_ge)
+                tt(pv(5), pv(4), b("dH", h), A.mult)
+            tt(pv(h), pv(5), land(h, 0, H), A.add)
+            cp(b("Tu", h), pv(h))
+        for h in range(2):
+            w = H * (h + 1)
+            for c in range(4):
+                ts(ap("eq%d" % h, w * c, w * c + w), ap("bB", 0, w), b("bl", h, c, c + 1), ap("DS", 4 * h + c, 4 * h + c + 1), A.is_equal, A.mult)
+            scan(ap("es%d" % h), ap("D%d" % h), ap("eq%d" % h), 0.0, A.mult, A.max)
+            tt(b("of", h), ap("es%d" % h, w - 1, 4 * w, w), b("bl", h), A.max)
+            cp(b("ou", h), b("of", h))
+        for h in range(2):
+            for q in range(2):
+                z = b("z", h, 512 * q, 512 * q + 512)
+                gat(z, X, b("Tu", h, 32 * q, 32 * q + 32), "VS")
+                o = 1024 * h + 512 * q
+                scan(ap("mS", o, o + 512), ap("RS"), z, 0.0, A.max, A.min)
+                scan(ap("MS", o, o + 512), ap("RM"), z, 0.0, A.mult, A.max)
+            m2 = snd(h, H, RW)
+            aff(m2, mrow("mS", h), 2, 1)
+            tt(pv(6 + h), pv(h), m2, A.mult)
+            tt(b("s", h), pv(6 + h), b("A8", h), A.add)
+            ts(b("n", h), b("s", h), 3, W - 1, A.logical_shift_right, A.bitwise_and)
+            cp(b("nu", h), b("n", h))
+            ts(b("nm", h), b("s", h), 3, B - 1, A.logical_shift_right, A.bitwise_and)
+            tt(pv(6 + h), b("nm", h), b("df", h), A.subtract)
+            if CONFIG["rel"]:
+                d, o = ap("pb%d" % (4 + h), 7 * H, 8 * H), b("rel", h)
+                mm([(d, [(ap("If"), m2), (ap("Ig"), land(h, H, RW))])])
+                add("S", lambda qq, e, d=d, o=o: [qq.activation(o[3], d[3], F.Sign)], [d], [o], "v", H)
+            else:
+                tt(b("rel", h), m2, land(h, H, RW), A.is_gt)
+            tt(pv(2 + h), b("n", h), pv(h), A.subtract)
+            if last:
+                aff(ap("yl", H * h, H * h + H), mrow("mS", h), 1, 0)
+        mm([(ap("pb5", 6 * H, 6 * H + 8), [(smat("S1", a), ap("MS", 16 * a + 15, 16 * L, 256)) for a in range(16)])])
+        cp(ap("ui"), ap("pb5", 6 * H, 6 * H + 8))
+        ts(ap("uj"), ap("ui"), 31, None, A.bitwise_and)
+        tt(ap("uk"), ap("uj"), ap("L32"), A.add)
+        cp(ap("ju"), ap("uk"))
+        if CONFIG["xs"]:
+            gat(ap("xo"), X, ap("ju"), "VS")
+            mm([(ap("pb5", 4 * H, 6 * H), [(ap("Ih"), ap("xo")), (ap("Ih"), ap("MS", 15, 16 * L, 16)), (ap("Ih"), ap("mh"))])])
+            cp(ap("xt"), ap("pb5", 4 * H, 6 * H))
+        else:
+            gtt(ap("xs"), X, ap("ju"), ap("MS", 15, 16 * L, 16), A.add)
+            ts(ap("xt"), ap("xs"), 1, None, A.logical_shift_right)
+        if last:
+            dma("Y", "cp", T.X2[:], T.X[:], [X, land(1, 0, H)], [ap("X2")], 1048576)
+            sct(ap("X2"), ap("ju"), ap("xt"))
+            dma("Y", "yclk", T.yclk[:], T.X2[:], [ap("X2")], [], 1048576)
+            dma("Y", "yla", T.ylast[:], T.yl[:], [ap("yl")], [], 32768)
+        for h in range(2):
+            for q in range(2):
+                gat(b("e", h, 512 * q, 512 * q + 512), X, b("nu", h, 32 * q, 32 * q + 32), "VS")
+            cmps = []
+            for q in range(2):
+                for bank, name in ((q, "mS"), (2 + q, "MS")):
+                    if CONFIG["pre"]:
+                        mm([(ap("pb%d" % bank, H * j, H * j + H), [(ap("In"), mrow(name, h))]) for j in range(8)], "open")
+                        mm([(ap("pb%d" % bank, H * j, H * j + H), [(ap("I1"), b("e", h, 8 * q + j, 1024, 16))]) for j in range(8)], "close")
+                    else:
+                        mm([(ap("pb%d" % bank, H * j, H * j + H), [(ap("I1"), b("e", h, 8 * q + j, 1024, 16)), (ap("In"), mrow(name, h))])
+                            for j in range(8)])
+                d, o = ap("pb%d" % q), b("cm", h, 512 * q, 512 * q + 512)
+
+                def fn(qq, e, d=d, o=o):
+                    if e == "V":
+                        return [qq.tensor_scalar(o[3], d[3], 0.0, None, A.is_ge)]
+                    return [qq.activation(o[3], d[3], F.Sign, bias=0.5, scale=1.0)]
+                cmps.append(add("VS", fn, [d], [o], "v", 512))
+                d, o = ap("pb%d" % (2 + q)), b("ab", h, 512 * q, 512 * q + 512)
+                add("S", lambda qq, e, d=d, o=o: [qq.activation(o[3], d[3], F.Abs)], [d], [o], "v", 512)
+            c2, zz = ap("pb%d" % (4 + h), 0, H), ap("pb6", H * h, H * h + H)
+            for q in range(2):
+                mm([(c2, [(ap("I32"), b("rel", h))] * (1 - q) +
+                     [([lambda c=cmps[q]: 1 if c["on"] == "V" else 2, smat("S2", p), smat("S1", p)], b("cm", h, H * p, H * p + H))
+                      for p in range(8 * q, 8 * q + 8)])], "end" if q else "begin")
+            rdy = b("rdy", h)
+            add("V", lambda q, e, c2=c2, rdy=rdy, cs=cmps: [q.tensor_scalar(
+                rdy[3], c2[3], col(TH + (cs[0]["on"] == "S") + 2 * (cs[1]["on"] == "S"))[3], None, A.is_ge)],
+                [c2, ap("col", TH, TH + 4)], [rdy], "v", H)
+            tt(b("td", h), rdy, pv(2 + h), A.mult)
+            tt(snd(h, 0, H), b("td", h), pv(h), A.add)
+            sct(ap("TT"), b("ou", h), snd(h, 0, H))
+            nb = ap("pb%d" % (4 + h), 2 * H, 3 * H)
+            mm([(nb, [(ap("If"), b("df", h)), (ap("I1"), ap("MK"))])], "begin")
+            for q in range(2):
+                mm([(zz, [(ap("I1"), ap("PC"))] * (1 - q) + [(smat("S16", p), b("ab", h, H * p, H * p + H)) for p in range(8 * q, 8 * q + 8)])],
+                   "more" if q else "begin")
+            mm([(zz, [(ap("Ik"), rdy)])], "close")
+            vt(b("kT", h), zz)
+            scan(b("kr", h), ap("RK"), b("kT", h), 65536.0, A.min, A.max)
+            gtt(b("qT", h), b("kr", h), ap("OB"), b("kT", h), A.is_equal)
+            vt(b("oh", h), b("qT", h))
+            tt(b("sel", h), b("oh", h), pv(6 + h), A.mult)
+            sg = ap("pb4", 4 * H + H * h, 5 * H + H * h)
+            mm([(nb, [(ap("BOh"), b("sel", h))])], "end")
+            scan(b("ex", h), ap("RS", 0, H), nb, 0.0, A.max, A.min)
+            if not last:
+                cp(slot("sb", v, h), b("ex", h, 15, H, 16))
+                for k, (src, dst) in enumerate(((snd(h), "land%d_%d" % (v + 1, h)), (slot("sb", v, h), "lb"))):
+                    dst = ap(dst) if k == 0 else slot("lb", v + 1, h)
+                    add("G", lambda q, e, s=src, d=dst, sem="arr%d_%d_%d" % (v + 1, h, k): [send(d[3], s[3], sem)], [src], [], "send", 0,
+                        tag=("send", v, h, k), sem="sent")
+                mm([(sg, [(ap("BOm"), b("oh", h)), (ap("I1"), ap("ones"))])])
+            else:
+                aff(b("bl", h), b("ex", h, 15, H, 16), 1, 0)
+                dma("Y", "ytr%d" % h, T.ytrav[:, H * h:H * h + H], snd(h, 0, H)[3], [snd(h, 0, H)], [], 32768)
+                dma("Y", "ysl%d" % h, T.yslot[:, 4 * h:4 * h + 4], b("bl", h)[3], [b("bl", h)], [], 2048)
+        if not last:
+            sct(X, ap("ju"), ap("xt"))
+            sg = ap("pb4", 4 * H, 6 * H)
+            add("V", lambda q, e, sg=sg: [q.tensor_reduce(T.par[:], sg[3], AxisListType.X, A.mult)], [sg], [ap("par")], "v", L)
+        else:
+            dma("Y", "ytt", T.yttab[:], TT[3], [TT], [], 524288)
+
+    hist, tags = {}, {}
+    for i, o in enumerate(ops):
+        dep = set()
+        for acc, isw in [(x, False) for x in o["rd"]] + [(x, True) for x in o["wr"]]:
+            bank = SCRATCH[acc[0]][0] == "psum"
+            for j, a, bb, w in hist.get(acc[0], ()):
+                if j == i:
+                    continue
+                if (isw or w) and a < acc[2] and acc[1] < bb:
+                    dep.add(j)
+                elif bank and (ops[j]["eng"] != o["eng"] or o["eng"] != "V"):
+                    dep.add(j)
+        for acc, isw in [(x, False) for x in o["rd"]] + [(x, True) for x in o["wr"]]:
+            hist.setdefault(acc[0], []).append((i, acc[1], acc[2], isw))
+        if o["kind"] == "arr":
+            dep = {tags[o["after"]]}
+        if "tag" in o:
+            tags[o["tag"]] = i
+        o["dep"] = sorted(dep)
+    return ops
+
+
+def cost(o, e, m):
+    k, n = o["kind"], o["n"]
+    if k == "v":
+        t = max(64, n) * m["cyc"] + m["fix"]
+    elif k == "g":
+        t = (0.05 if e == "V" else 0.065) + n * m["g"] * m["cyc"]
+    elif k == "sc":
+        t = 0.05 + n * m["sc"] * m["cyc"]
+    elif k == "pe":
+        t = n * m["pe"] + m["fix"]
+    elif k == "io":
+        t = 0.13 + 2 * n * m["cyc"]
+    elif k == "dma":
+        return 0.05, m["dma0"] + n / m["bw"]
+    elif k == "send":
+        return 0.5, 0.5
+    else:
+        return 0.0, m["rem"]
+    return t, t
+
+
+def schedule(ops, cfg, m):
+    n = len(ops)
+    rnd = [cfg["seed"] * 7919 + 1]
+
+    def rand():
+        rnd[0] = (rnd[0] * 1103515245 + 12345) % 2147483648
+        return rnd[0] / 2147483648.0
+    succ = [[] for _ in ops]
+    for i, o in enumerate(ops):
+        for j in o["dep"]:
+            succ[j].append(i)
+    prio = [0.0] * n
+    for i in range(n - 1, -1, -1):
+        prio[i] = cost(ops[i], ops[i]["eng"][-1], m)[1] + max([prio[j] + m["cross"] for j in succ[i]] + [0.0])
+    prio = [p + cfg["noise"] * rand() for p in prio]
+    left = [len(o["dep"]) for o in ops]
+    ready = [i for i in range(n) if left[i] == 0]
+    free, done, order = {}, [0.0] * n, []
+    while ready:
+        cand = []
+        for i in ready:
+            o, best = ops[i], None
+            for e in o["eng"]:
+                s = max([free.get(e, 0.0)] + [done[j] + (m["same"] if ops[j]["on"] == e else m["cross"]) for j in o["dep"]])
+                f = s + cost(o, e, m)[0] + (cfg["bias"] if e == "V" and len(o["eng"]) > 1 else 0.0)
+                if best is None or f < best[0]:
+                    best = (f, s, e)
+            cand.append((best[1], i, best[2]))
+        t0 = min(c[0] for c in cand)
+        s, i, e = max([c for c in cand if c[0] <= t0 + cfg["slack"]], key=lambda c: prio[c[1]])
+        hold, lat = cost(ops[i], e, m)
+        ops[i]["on"] = e
+        free[e], done[i] = s + hold, s + lat
+        order.append(i)
+        ready.remove(i)
+        for j in succ[i]:
+            left[j] -= 1
+            if left[j] == 0:
+                ready.append(j)
+    return order, max(done)
+
+
+ORDER = [int(x) for x in """
+42 55 5 10 38 13 0 1 4 2 3 22 14 15 16 17 8 6 48 23 29 18 20 40 31 43 46 25 24 12 34 30 47 7 19 60 56 57 26 39 21 52 66 41 53 44 27 28 75 54 59 76 101 99 86 100 11 49 87 50 98 33 9 51 108 102 77 106 107 105 103 37 36 109 84 73 32 45 70 68 104 110 35 67 71 69 58 74 81 61 79 88 62 65 72 78 89 85 111 90 91 92 80 82 112 115 113 93 116 63 118 151 119 120 157 121 122 83 94 126 95 117 96 114 150 149 159 153 152 158 160 154 97 127 64 -130 155 125 132 128 131 123 161 163 186 -133 124 129 156 134 164 135 142 165 138 162 136 166 137 167 170 181 143 168 171 144 221 172 140 145 173 184 185 174 175 176 146 177 169 192 194 188 147 141 148 178 187 179 180 139 193 189 190 -196 182 195 191 219 198 222 197 199 223 200 201 205 225 206 202 203 216 207 204 208 183 209 227 210 234 211 212 218 213 214 215 217 224 220 230 226 233 235 228 236 232 231 247 240 238 258 260 259 257 229 248 249 250 261 251 237 274 271 241 243 239 275 252 272 276 277 278 244 310 279 280 316 281 245 246 308 309 253 242 265 254 284 273 255 318 312 311 313 317 319 262 256 286 264 -289 285 290 288 266 282 314 287 291 267 320 322 345 323 -292 268 315 293 324 294 295 321 296 325 263 326 297 283 344 343 301 302 303 329 328 330 331 353 347 351 340 327 380 299 332 304 333 305 334 335 336 298 306 346 337 352 348 338 349 339 307 -355 341 354 357 350 300 381 378 356 358 364 359 382 384 360 361 365 269 375 366 363 270 367 368 369 370 342 386 393 371 377 362 372 373 374 379 376 383 389 390 394 385 387 395 391 406 392 399 388 417 419 416 418 407 408 397 409 420 410 396 400 430 398 433 431 411 402 434 403 435 436 469 437 438 475 439 440 432 401 404 412 405 467 468 413 421 424 477 414 443 471 415 444 441 -448 445 470 476 472 478 449 425 446 473 504 481 447 450 -451 442 426 479 452 423 453 482 460 474 480 483 454 455 427 484 461 422 462 485 456 488 489 490 510 506 512 487 502 503 505 463 499 491 539 492 464 486 493 465 494 495 496 466 458 497 498 511 507 508 457 -514 500 513 509 516 540 537 459 517 518 515 523 428 519 520 524 534 429 525 522 541 526 527 501 528 543 545 552 529 530 536 521 531 532 533 535 538 542 548 544 546 549 553 628 554 565 551 550 558 577 547 578 576 566 575 567 556 568 579 569 555 559 589 592 557 590 570 561 593 562 595 634 594 596 563 597 571 598 599 604 633 632 640 564 560 583 572 584 573 603 574 591 642 636 605 -608 582 602 585 610 580 635 637 641 643 638 644 646 600 609 606 586 607 611 -620 612 613 639 645 581 616 601 668 647 621 653 614 648 615 622 649 623 650 624 666 667 631 664 618 625 651 626 627 629 674 654 670 652 676 669 655 656 657 658 659 660 675 671 677 661 672 662 678 630 680 617 -663 673 679 681 619 587 665 588 682 687 683 688 684 685 698 689 686 690 700 691 692 693 694 695 696 -697 699
+""".split() if x != "30"]
+ORDER = [x - (x > 30) + (x < -30) for x in ORDER]
+
+
+def rank_program(g, core, T, topo):
+    rank = T.rank_of(core)
+    if rank is None:
+        return
+    nxt, prv = T.cores[(rank + STEP) % N], T.cores[(rank - STEP) % N]
+    rid, pid, _ = topo.addr(nxt)
+    n_out, n_in = len(topo.engines(core, nxt)), len(topo.engines(prv, core))
+
+    def send(dst, src, sem):
+        return g.remote_dma(dst, src, T.sem[sem],
+                            T.sem.sent, pid, rid, topo.mask(core, nxt))
+
+    ops = build(T, send)
+    order = [abs(x) for x in ORDER]
+    for x in ORDER:
+        ops[abs(x)]["on"] = "V" if x < 0 else ops[abs(x)]["eng"][-1]
+    queue = {"V": g.vector, "S": g.scalar, "P": g.tensor, "G": g, "Y": g.sync}
+    total = {}
+    known = {e: {} for e in queue}
+    for i in order:
+        o = ops[i]
+        e = o["on"]
+        if o["kind"] == "arr":
+            o["sig"], o["seen"] = (o["sem"], n_in), {}
+            total[o["sem"]] = n_in
+            continue
+        need = {}
+        for j in o["dep"]:
+            if e == "P" and ops[j]["on"] == "P":
+                continue
+            s, c = ops[j]["sig"]
+            if c > need.get(s, (0, 0))[0]:
+                need[s] = (c, j)
+        for s, (c, j) in sorted(need.items(), key=lambda x: -ops[x[1][1]]["pos"] if "pos" in ops[x[1][1]] else 0):
+            if known[e].get(s, 0) >= c:
+                continue
+            queue[e].wait_ge(T.sem[s], c)
+            known[e][s] = c
+            for s2, c2 in ops[j]["seen"].items():
+                if c2 > known[e].get(s2, 0):
+                    known[e][s2] = c2
+        ins = o["fn"](queue[e], e)
+        if o["kind"] == "send":
+            total["sent"] = total.get("sent", 0) + n_out
+            continue
+        s, step = (o["sem"], 16) if o["kind"] == "dma" else ("c" + e, 1)
+        for x in ins:
+            x.then_inc(T.sem[s], step)
+            total[s] = total.get(s, 0) + step
+        o["sig"], o["seen"], o["pos"] = (s, total[s]), dict(known[e]), len(total) + sum(total.values())
+    for s, c in total.items():
+        g.wait_ge(T.sem[s], c)

@@ -145,7 +145,7 @@ def build(T, send):
                     lt = l[l[0]()] if isinstance(l, list) else l
                     st, sp = i == 0, i == len(terms) - 1
                     if part == "open":
-                        st, sp = k == 0, False
+                        st, sp = k == 0 and i == 0, False
                     elif part == "begin":
                         sp = False
                     elif part == "more":
@@ -502,7 +502,9 @@ def schedule(ops, cfg, m):
 ORDER = [int(x) for x in """
 42 55 5 10 38 13 0 1 4 2 3 22 14 15 16 17 8 6 48 23 29 18 20 40 31 43 46 25 24 12 34 30 47 7 19 60 56 57 26 39 21 52 66 41 53 44 27 28 75 54 59 76 101 99 86 100 11 49 87 50 98 33 9 51 108 102 77 106 107 105 103 37 36 109 84 73 32 45 70 68 104 110 35 67 71 69 58 74 81 61 79 88 62 65 72 78 89 85 111 90 91 92 80 82 112 115 113 93 116 63 118 151 119 120 157 121 122 83 94 126 95 117 96 114 150 149 159 153 152 158 160 154 97 127 64 -130 155 125 132 128 131 123 161 163 186 -133 124 129 156 134 164 135 142 165 138 162 136 166 137 167 170 181 143 168 171 144 221 172 140 145 173 184 185 174 175 176 146 177 169 192 194 188 147 141 148 178 187 179 180 139 193 189 190 -196 182 195 191 219 198 222 197 199 223 200 201 205 225 206 202 203 216 207 204 208 183 209 227 210 234 211 212 218 213 214 215 217 224 220 230 226 233 235 228 236 232 231 247 240 238 258 260 259 257 229 248 249 250 261 251 237 274 271 241 243 239 275 252 272 276 277 278 244 310 279 280 316 281 245 246 308 309 253 242 265 254 284 273 255 318 312 311 313 317 319 262 256 286 264 -289 285 290 288 266 282 314 287 291 267 320 322 345 323 -292 268 315 293 324 294 295 321 296 325 263 326 297 283 344 343 301 302 303 329 328 330 331 353 347 351 340 327 380 299 332 304 333 305 334 335 336 298 306 346 337 352 348 338 349 339 307 -355 341 354 357 350 300 381 378 356 358 364 359 382 384 360 361 365 269 375 366 363 270 367 368 369 370 342 386 393 371 377 362 372 373 374 379 376 383 389 390 394 385 387 395 391 406 392 399 388 417 419 416 418 407 408 397 409 420 410 396 400 430 398 433 431 411 402 434 403 435 436 469 437 438 475 439 440 432 401 404 412 405 467 468 413 421 424 477 414 443 471 415 444 441 -448 445 470 476 472 478 449 425 446 473 504 481 447 450 -451 442 426 479 452 423 453 482 460 474 480 483 454 455 427 484 461 422 462 485 456 488 489 490 510 506 512 487 502 503 505 463 499 491 539 492 464 486 493 465 494 495 496 466 458 497 498 511 507 508 457 -514 500 513 509 516 540 537 459 517 518 515 523 428 519 520 524 534 429 525 522 541 526 527 501 528 543 545 552 529 530 536 521 531 532 533 535 538 542 548 544 546 549 553 628 554 565 551 550 558 577 547 578 576 566 575 567 556 568 579 569 555 559 589 592 557 590 570 561 593 562 595 634 594 596 563 597 571 598 599 604 633 632 640 564 560 583 572 584 573 603 574 591 642 636 605 -608 582 602 585 610 580 635 637 641 643 638 644 646 600 609 606 586 607 611 -620 612 613 639 645 581 616 601 668 647 621 653 614 648 615 622 649 623 650 624 666 667 631 664 618 625 651 626 627 629 674 654 670 652 676 669 655 656 657 658 659 660 675 671 677 661 672 662 678 630 680 617 -663 673 679 681 619 587 665 588 682 687 683 688 684 685 698 689 686 690 700 691 692 693 694 695 696 -697 699
 """.split() if x != "30"]
-ORDER = [x - (x > 30) + (x < -30) for x in ORDER]
+ORDER = [int(x) for x in """
+41 54 6 10 5 8 11 37 0 1 2 3 22 14 13 4 15 42 -17 39 18 23 38 16 -20 26 24 55 7 -21 65 56 59 25 85 -28 45 48 46 19 43 29 47 75 49 33 83 86 74 40 50 98 12 105 107 97 51 32 9 100 27 -44 35 58 52 104 76 99 53 72 31 67 60 69 101 30 106 102 66 34 68 70 108 71 87 109 82 103 88 77 80 78 73 89 110 90 36 91 81 79 84 57 114 111 115 112 116 117 92 150 93 118 94 119 113 120 95 121 96 152 156 148 -149 129 157 151 -126 153 158 154 127 130 124 -132 160 125 133 61 134 131 135 155 159 162 161 163 185 169 191 170 164 136 171 168 165 63 166 128 172 122 141 187 183 184 188 186 180 220 173 139 174 123 175 64 176 142 62 143 137 144 177 178 192 193 190 189 194 204 197 145 179 146 167 147 181 195 198 218 199 140 221 196 205 206 203 182 207 200 208 201 209 138 215 233 210 222 211 202 217 212 213 214 224 223 219 225 226 216 234 227 231 235 232 246 228 259 256 247 257 248 258 249 239 237 260 250 261 236 245 270 273 243 240 238 271 274 251 230 229 276 241 244 275 242 315 309 277 252 278 253 279 254 280 255 272 -307 308 317 311 310 312 316 318 288 313 314 319 -285 281 264 283 286 289 266 290 321 328 291 322 287 282 263 346 298 292 284 323 293 265 320 329 330 352 300 324 294 325 295 331 -342 301 327 332 302 333 303 334 304 262 343 350 344 345 353 347 335 336 305 299 267 337 339 379 351 306 338 348 356 349 355 340 380 363 -354 357 377 296 358 268 326 364 365 366 359 362 367 360 368 297 374 369 370 381 269 341 392 376 371 383 385 389 372 373 361 378 375 382 390 384 386 388 393 394 391 405 387 406 417 415 407 416 408 418 396 398 409 429 432 395 400 397 404 399 410 430 433 434 403 435 411 436 431 437 468 474 401 423 412 438 440 413 439 422 414 -467 402 466 447 -444 419 445 448 442 -450 424 420 451 446 452 449 470 476 471 469 477 475 473 472 478 479 453 487 480 481 443 454 482 457 483 441 459 488 489 460 484 425 461 490 421 462 491 426 463 492 485 505 511 509 486 503 502 501 498 538 493 464 494 504 510 495 506 513 -507 512 515 516 496 455 497 465 458 536 517 427 499 539 508 514 522 523 524 518 521 500 519 525 526 456 527 533 428 528 551 535 529 540 530 542 544 531 532 520 534 537 541 547 552 627 543 545 553 549 546 550 548 575 564 576 565 577 566 574 567 568 554 557 555 591 588 560 559 558 556 592 589 -594 563 569 595 570 596 562 597 578 598 561 582 571 581 572 583 573 590 593 579 633 639 632 631 604 -607 602 584 601 608 605 606 -610 599 611 609 641 635 634 637 640 642 643 636 667 645 646 612 600 620 613 647 614 648 638 603 644 580 621 649 618 652 653 654 665 666 619 622 585 623 655 615 624 617 625 656 626 657 675 669 651 673 630 628 586 668 674 670 -677 650 658 616 659 671 676 679 629 672 678 680 686 660 687 681 682 587 688 683 661 684 689 697 685 699 663 690 662 664 691 692 693 694 695 -696 698
+""".split()]
 
 
 def rank_program(g, core, T, topo):

@@ -1,71 +1,67 @@
 from concourse.mybir import AluOpType as A, AxisListType, ActivationFunctionType as F
 
 N, STEP, VISITS = 8, 3, 4
-W, B, L, H = 4096, 1024, 128, 64
-RW = 2 * H
-F16 = "float16"
+W, B, L, H, SP = 4096, 1024, 128, 64, 256
+F16, BF, F32, I32, U16 = "float16", "bfloat16", "float32", "int32", "uint16"
 
-SCRATCH = {
-    "X": ("sbuf", [128, W], "bfloat16"), "X2": ("sbuf", [128, W], "bfloat16"),
-    "tt32": ("sbuf", [128, B], "int32"), "TT": ("sbuf", [128, B + L], "float32"),
-    "trav0": ("sbuf", [128, L], "int32"), "last0": ("sbuf", [128, L], "bfloat16"), "slot0": ("sbuf", [128, 8], "int32"),
-    "mS": ("sbuf", [128, 16 * L], "bfloat16"), "MS": ("sbuf", [128, 16 * L], "bfloat16"),
-    "bB": ("sbuf", [128, L], F16), "eq0": ("sbuf", [128, 256], F16), "eq1": ("sbuf", [128, 512], F16),
-    "es0": ("sbuf", [128, 256], F16), "es1": ("sbuf", [128, 512], F16),
-    "If": ("sbuf", [128, 128], "float32"), "Ig": ("sbuf", [128, 128], "float32"), "Ih": ("sbuf", [128, 128], "bfloat16"),
-    "mh": ("sbuf", [128, 128], "bfloat16"), "xo": ("sbuf", [128, L], "bfloat16"),
-    "Ik": ("sbuf", [128, 128], "bfloat16"), "ui": ("sbuf", [128, 8], "int32"), "uj": ("sbuf", [128, 8], "int32"),
-    "uk": ("sbuf", [128, 8], "int32"), "ju": ("sbuf", [128, 8], "uint16"),
-    "xs": ("sbuf", [128, L], "int32"), "xt": ("sbuf", [128, L], "int32"),
-    "par": ("sbuf", [128, 1], "float32"), "yl": ("sbuf", [128, L], "bfloat16"),
-    "pi": ("sbuf", [128, 1], "int32"), "pj": ("sbuf", [128, 2], "int32"), "col": ("sbuf", [128, 12], "float32"),
-    "BT": ("sbuf", [128, B], "float32"), "i144": ("sbuf", [128, 144], "float32"), "iog": ("sbuf", [128, 128], "float32"),
-    "iom": ("sbuf", [128, H], "float32"), "i16": ("sbuf", [128, 8], "float32"),
-    "id0": ("sbuf", [128, 256], "float32"), "id1": ("sbuf", [128, 512], "float32"),
-    "S1": ("sbuf", [128, 144], "bfloat16"), "S2": ("sbuf", [128, 144], "bfloat16"), "S16": ("sbuf", [128, 144], "bfloat16"),
-    "I1": ("sbuf", [128, 128], "bfloat16"), "In": ("sbuf", [128, 128], "bfloat16"), "I32": ("sbuf", [128, 128], "bfloat16"),
-    "BOf": ("sbuf", [128, 128], "float32"),
-    "lb": ("sbuf", [128, 16 * VISITS], "uint16"), "sb": ("sbuf", [128, 16 * VISITS], "uint16"),
-    "DF": ("sbuf", [128, B], "float32"), "BOh": ("sbuf", [128, 128], F16), "BOm": ("sbuf", [128, 128], "bfloat16"),
-    "MK": ("sbuf", [128, H], "bfloat16"), "PC": ("sbuf", [128, H], "bfloat16"), "ones": ("sbuf", [128, H], "bfloat16"),
-    "RS": ("sbuf", [128, 512], "bfloat16"), "RM": ("sbuf", [128, 512], "bfloat16"), "RK": ("sbuf", [128, H], "float32"),
-    "L32": ("sbuf", [128, 8], "float32"), "DS": ("sbuf", [128, 8], "float32"), "OB": ("sbuf", [128, 4], "uint16"),
-    "D0": ("sbuf", [128, 256], F16), "D1": ("sbuf", [128, 512], F16),
-}
-for _h in range(2):
-    for _n, _w, _d in (("U", H, "uint16"), ("Hu", H, "uint16"), ("dH", H, "float32"), ("A8", H, "float32"),
-                       ("x", 16 * H, "bfloat16"), ("cy", 16 * H, "bfloat16"), ("z", 16 * H, "bfloat16"),
-                       ("e", 16 * H, "bfloat16"), ("cm", 16 * H, "bfloat16"), ("ab", 16 * H, "bfloat16"),
-                       ("Tu", H, "uint16"), ("s", H, "int32"), ("n", H, "int32"), ("nu", H, "uint16"),
-                       ("rel", H, "bfloat16"), ("rdy", H, "bfloat16"), ("td", H, "float32"), ("tk", H, "float32"),
-                       ("kT", H, "float32"), ("kr", H, "float32"), ("qT", H, "bfloat16"), ("oh", H, "bfloat16"),
-                       ("sel", H, F16), ("ex", H, "float32"), ("nm", H, "int32"), ("df", H, "float32"),
-                       ("bl", 4, "float32"), ("of", 4, "float32"), ("ou", 4, "uint16")):
-        SCRATCH["h" + _n] = ("sbuf", [128, 2 * _w], _d)
-    for _v in range(VISITS):
-        SCRATCH["land%d_%d" % (_v, _h)] = ("sbuf", [128, RW], "float32")
-        SCRATCH["send%d_%d" % (_v, _h)] = ("sbuf", [128, RW], "float32")
+SCRATCH = {}
+for _n, _w, _d in (
+        ("X", W, BF), ("X2", W, BF), ("tt32", B, I32), ("TT", SP + B, F32), ("trav0", L, I32), ("slot0", 8, I32), ("last0", L, BF),
+        ("lT", 2 * L * VISITS, F32), ("sT", 2 * L * VISITS, F32), ("lU", 2 * L * VISITS, U16), ("sU", 2 * L * VISITS, U16), ("lb", 16 * VISITS, U16), ("sb", 16 * VISITS, U16),
+        ("mS", 16 * L, BF), ("MS", 16 * L, BF), ("bB", L, F16), ("bF", L, F32), ("bl", 16, F32), ("eq", 4 * L, BF),
+        ("es", 2 * L, F32), ("ou", 16, U16), ("xs", L, I32), ("xt", L, I32), ("xo", L, BF), ("xb", L, BF),
+        ("par", 1, F32), ("ys", 8, F32), ("yl", L, BF),
+        ("pi", 1, I32), ("pj", 2, I32), ("col", 3, F32), ("BT", B, F32), ("DF", B, F32), ("of", 20, F32), ("OF", 20, U16),
+        ("cb", 1, F32), ("hi", 1, F32), ("tV", 1, F32), ("tS", 1, F32), ("uV", 1, F32), ("uS", 1, F32),
+        ("i144", 144, F32), ("iog", L, F32), ("iom", L, F32), ("i32", L, BF),
+        ("S16", 144, BF), ("S32", 144, BF), ("S512", 144, BF),
+        ("I1", L, BF), ("In", L, BF), ("Ik", L, BF), ("Ih", L, BF),
+        ("If", L, F32), ("Ig", L, F32), ("Ihf", L, F32), ("Ifb", L, F32), ("J1", L, F16), ("Jb", L, F16), ("CB", H, F32), ("CH", H, F16), ("CL", H, F16),
+        ("L32", 8, F32), ("p32", 1, F32), ("ui", 8, I32), ("uj", 8, I32), ("uk", 8, I32),
+        ("BOh", L, F16), ("BOn", L, BF), ("BOp", L, BF), ("BOq", L, BF), ("TRn", L, BF),
+        ("CM", L, BF), ("MK", L, BF), ("RD", 2 * L, F32), ("PC", H, BF), ("ones", L, BF),
+        ("kC", L, BF), ("kD", L, BF), ("kh", L, BF), ("kv", H, BF), ("mh", L, BF),
+        ("RS", 1024, BF), ("RM", 1024, BF), ("RK", H, F32)):
+    SCRATCH[_n] = ("sbuf", [128, _w], _d)
+for _n, _w, _d in (("U", H, U16), ("Hu", H, U16), ("dH", H, F32), ("tk", H, BF), ("td", H, F32),
+                   ("x", 16 * H, BF), ("cy", 16 * H, BF), ("z", 16 * H, BF), ("e", 16 * H, BF), ("cm", 16 * H, BF), ("ab", 16 * H, BF),
+                   ("Tu", H, U16), ("q", H, F32), ("s", H, I32), ("n", 2 * H, I32), ("nu", H, U16), ("df", H, F32), ("dg", H, F16),
+                   ("rel", H, BF), ("A8", H, F32), ("D", H, BF), ("rdy", H, BF), ("te", H, F32),
+                   ("kT", H, F32), ("kr", H, F32), ("qT", H, BF), ("oh", H, BF), ("sel", H, F16), ("ex", H, F32)):
+    SCRATCH["h" + _n] = ("sbuf", [128, 2 * _w], _d)
 for _b in range(8):
-    SCRATCH["pb%d" % _b] = ("psum", [128, 512], "float32")
+    SCRATCH["pb%d" % _b] = ("psum", [128, 512], F32)
 
-DMAS = ["slot", "trav", "last", "tt", "clk", "cp", "yclk", "ytt", "ytr0", "ytr1", "ysl0", "ysl1", "yla"]
+DMAS = ["slot", "trav", "last", "tt", "clk", "cp", "yclk", "yc0", "yc1", "cp0", "cp1", "ytt", "ytr", "ysl", "yla"]
 SEMAPHORES = ["cV", "cS", "cP", "cG", "sent"] + ["d" + d for d in DMAS] + \
-             ["arr%d_%d_%d" % (v, h, k) for v in range(1, VISITS) for h in range(2) for k in range(2)]
+             ["arr%d_%d_%s" % (v, h, k) for v in range(1, VISITS) for h in range(2) for k in "Tcb"]
 
-MODEL = {"cyc": 0.83e-3 * 1.25, "pe": 0.6e-3, "g": 1.56, "sc": 3.8, "fix": 0.03, "same": 0.06, "cross": 0.1,
-         "rem": 3.0, "dma0": 2.0, "bw": 250e3}
-CONFIG = {"seed": 0, "noise": 0.0, "bias": 0.3, "slack": 0.1, "pre": True, "split": True, "dh": False, "rel": False, "xs": False, "clk1": True}
+CONFIG = {"V": set(), "S": set(), "W": set(), "tadd": "P", "dh": "S", "rel": "V", "xs": "V", "own": False, "first": "X", "dnm": False, "join": False, "ttf": "G"}
+CONFIG = {'V': {'df0', 'e01', 'e10', 'mC0@0', 'x10@0'}, 'S': {'tk1', 'rdy0', 'bB'}, 'W': {'cy1@0', 'x1@0'}, 'tadd': 'P', 'dh': 'S', 'rel': 'V', 'xs': 'V', 'own': False, 'first': 'X', 'dnm': True, 'join': True, 'ttf': 'G'}
+ORDER = """dmaslot dmatrav .pb70 .iog0 .DF1 dmaclk .sb0 dmatt .pi0 .lb0 .pj0 .pj1 .lb1 .col0 .BOp0 .iom0 .ones0 .par0 .of2 .of0 .kh0 .col1 .lT0 U1 .kC0 .cb0 .BOh0 .kv0 .PC0 .CB0 .i1440 .I10 .If0 .of1 .OF0 .BOn0 .S160 .J10 .Ik0 .Ihf0 .S5120 .Ig0 .BT0 Tpre0 U0 x01 .MK0 .CM0 .DF0 .RD0 .RM0 .RS0 .lb2 bl dmalast Hu0 x00 dH0 cy01 cy00 dH1 Tdh0 .In0 .i320 Tpre1 vote0 .RK0 x11 bB0 .RK1 df0 df1 tk0 td0 .TT0 Hu1 .lT1 Tadd0 Tu0 .BOq0 .Ifb0 Badd0 cy11 .TRn0 Tdh1 bB1 z00 MS00 mS00 vote1 z01 tk1 mS01 td1 q0 Tadd1 premS01 rel0 premS00 s0 Tu1 eq0 n0 z11 MS01 nu0 eq1 e00 nm0 Badd1 preMS01 z10 dup preMS00 e01 MS11 mS11 dn0 MS10 difmS00 mS10 mC0 q1 difmS01 difMS01 cm00 cm01 rel1 crel0 difMS00 u ab00 s1 cnt00 cnt01 es n1 rdy0 nm1 crel1 premS10 ou sco00 te0 nu1 premS11 Tf0 e10 xs ab01 e11 sendT0 npre0 mC1 sco01 srdy0 kT0 xt preMS10 kr0 Tsc01 qT0 oh0 Tsc00 difmS10 preMS11 cm10 difmS11 difMS10 sel0 dn1 cm11 nsel0 ex0 sb0 ab10 difMS11 cnt10 cnt11 Xsc sendb0 ab11 rdy1 te1 Tf1 sco10 sendT1 sco11 srdy1 kT1 kr1 Tsc11 npre1 qT1 oh1 Tpre0 U0 sel1 nsel1 sg Tsc10 x00 ex1 sb1 sendb1 x01 dH0 Tdh0 Hu0 cy00 cy01 U1 par bB0 df0 x11 vote0 tk0 td0 dH1 Tadd0 x10 Hu1 bl Tu0 cy11 Tdh1 z00 Tpre1 Badd0 cy10 MS00 z01 mS00 vote1 bB1 tk1 mS01 td1 df1 q0 rel0 Tadd1 premS00 s0 Tu1 eq0 nm0 premS01 n0 crel0 MS01 Badd1 nu0 mC0 z11 eq1 e00 e01 preMS00 dn0 mS11 MS11 dup preMS01 difmS00 z10 MS10 mS10 q1 cm00 difMS01 rel1 difmS01 cm01 difMS00 u es s1 cnt00 cnt01 ou ab00 premS10 n1 xs rdy0 te0 preMS10 sco00 crel1 ab01 nu1 Tf0 sendT0 e10 npre0 sco01 srdy0 kT0 Tsc01 premS11 e11 difmS10 kr0 nm1 preMS11 mC1 qT0 difmS11 xt oh0 dn1 cm10 difMS10 cm11 sel0 Tsc00 nsel0 difMS11 ex0 sb0 sendb0 Xsc ab10 cnt10 cnt11 ab11 sco10 rdy1 sco11 te1 Tf1 Tsc11 srdy1 npre1 kT1 kr1 U0 sendT1 Tpre0 qT1 oh1 sel1 nsel1 Tsc10 x00 sg ex1 sb1 sendb1 x01 Hu0 cy00 dH0 cy01 Tdh0 U1 df0 vote0 bB0 x11 par tk0 td0 x10 Hu1 Tadd0 bl Tu0 dH1 cy11 Tdh1 z00 Tpre1 Badd0 cy10 mS00 z01 MS00 vote1 df1 tk1 mS01 td1 bB1 mC0 q0 rel0 Tadd1 premS00 premS01 s0 Tu1 eq0 n0 MS01 z11 Badd1 nu0 nm0 crel0 eq1 e00 preMS01 preMS00 dup e01 MS11 mS11 dn0 z10 MS10 difmS00 cm00 mS10 q1 difMS00 difMS01 difmS01 cm01 rel1 u s1 cnt00 cnt01 es premS10 n1 crel1 ab00 ou nu1 premS11 xs preMS10 rdy0 te0 ab01 sco00 e11 mC1 xt Tf0 e10 sco01 preMS11 srdy0 npre0 sendT0 kT0 Tsc01 kr0 nm1 difmS10 cm10 difmS11 qT0 oh0 dn1 difMS10 sel0 cm11 difMS11 Tsc00 nsel0 ex0 sb0 ab10 cnt10 cnt11 sco10 ab11 sco11 rdy1 te1 Tf1 srdy1 Xsc kT1 kr1 Tsc11 sendb0 npre1 qT1 sendT1 Tpre0 U0 oh1 sel1 x01 Tsc10 nsel1 ex1 sb1 sendb1 x00 dH0 sg Hu0 cy01 cy00 bB0 Tdh0 vote0 U1 par df0 tk0 td0 x11 dH1 x10 Hu1 bl Tadd0 Tu0 cy11 Tdh1 z00 Badd0 cy10 Tpre1 MS00 z01 mS00 mS01 bB1 vote1 tk1 td1 Tadd1 rel0 q0 premS00 df1 Tu1 eq1 premS01 s0 z11 eq0 Badd1 dup n0 MS01 nm0 preMS01 z10 crel0 nu0 e00 mS11 preMS00 e01 difmS00 difmS01 yl0 MS10 MS11 mS10 dn0 q1 u rel1 es s1 cm00 cm01 difMS01 difMS00 ou dmacp cnt00 yl1 cnt01 premS11 premS10 n1 xs xt dmayla nu1 npre0 ab01 ab00 preMS11 preMS10 rdy0 sco00 Xsc dmayclk crel1 sco01 e10 srdy0 kT0 nm1 te0 dn1 kr0 qT0 oh0 Tf0 e11 difmS10 cm10 difmS11 cm11 difMS10 difMS11 sel0 Tsc01 Tsc00 ab10 cnt10 cnt11 rdy1 te1 Tf1 Tsc11 Tsc10 nsel0 sco10 ab11 npre1 sco11 srdy1 kT1 kr1 qT1 oh1 sel1 nsel1 ex0 dmaytr ex1 ys0 dmaytt ys1 dmaysl"""
+CONFIG = {'V': {'df0', 'e10', 'mC0@0', 'e01'}, 'S': {'bB'}, 'W': {'cy1@0', 'x1@0'}, 'tadd': 'P', 'dh': 'S', 'rel': 'V', 'xs': 'V', 'own': False, 'first': 'X', 'dnm': True, 'join': True, 'ttf': 'G'}
+ORDER = """.pb70 .i1440 .kC0 .I10 .In0 .Ihf0 .pi0 .lb0 .pj0 .pj1 .col0 .cb0 .RK0 .iom0 dmaslot dmatrav dmaclk .CB0 .iog0 .of1 .BOp0 .J10 .BOh0 .par0 .col1 .of2 .of0 .RK1 .ones0 .OF0 U0 .sb0 .MK0 .CM0 .kh0 dmatt .lT0 .If0 .lb2 .PC0 .BT0 .lb1 bB0 U1 .Ig0 x01 .DF0 bl Tpre1 .RD0 .S160 bB1 eq0 x00 Hu0 dH0 .DF1 .Ifb0 .RS0 .BOn0 .TRn0 .S5120 cy01 cy00 x11 Tdh0 .Ik0 Hu1 df0 .BOq0 dmalast dH1 df1 Tpre0 vote0 tk0 td0 .lT1 Tadd0 Tu0 Badd0 cy11 .i320 Tdh1 z00 .RM0 mS00 z01 MS00 vote1 tk1 mS01 td1 q0 .TT0 Tadd1 premS01 rel0 premS00 s0 Tu1 eq1 crel0 n0 mC0 Badd1 dup nu0 MS01 z11 e01 preMS01 preMS00 MS11 nm0 mS11 e00 difmS00 difMS00 difmS01 difMS01 dn0 z10 MS10 mS10 q1 cm00 rel1 u s1 cm01 cnt00 es cnt01 ab00 premS11 n1 crel1 premS10 ou rdy0 nu1 te0 preMS10 Tf0 e10 sco00 xs ab01 sco01 npre0 srdy0 kT0 Tsc01 e11 kr0 preMS11 difmS10 nm1 qT0 xt oh0 mC1 Tsc00 difmS11 sel0 difMS10 difMS11 cm10 cm11 nsel0 dn1 ab10 ex0 sb0 sendT0 sendb0 cnt10 cnt11 Xsc npre1 rdy1 te1 sco10 ab11 sco11 srdy1 Tf1 kT1 kr1 sendT1 Tsc11 qT1 U0 oh1 sel1 Tsc10 nsel1 x00 Tpre0 ex1 sb1 x01 sg bB0 Hu0 df0 cy00 cy01 dH0 U1 x11 sendb1 Tdh0 vote0 par tk0 td0 x10 Hu1 dH1 Tadd0 bl Tpre1 Tu0 Badd0 cy11 Tdh1 cy10 z00 mS00 MS00 z01 vote1 tk1 mS01 td1 q0 Tadd1 rel0 df1 premS00 premS01 s0 bB1 Tu1 eq1 mC0 nm0 crel0 n0 eq0 nu0 MS01 z11 Badd1 e01 dup e00 MS11 mS11 preMS01 preMS00 dn0 z10 MS10 difmS00 difmS01 difMS00 mS10 q1 difMS01 rel1 cm00 cm01 ab00 u s1 cnt00 cnt01 ab01 es premS11 n1 crel1 ou rdy0 nu1 premS10 preMS10 te0 xs sco00 sco01 Tf0 e10 srdy0 kT0 nm1 kr0 preMS11 Tsc01 e11 qT0 difmS10 difMS10 mC1 dn1 cm10 difmS11 oh0 npre0 sel0 Tsc00 difMS11 cm11 nsel0 ex0 sendT0 xt sb0 cnt10 cnt11 sendb0 ab10 rdy1 te1 sco10 ab11 sco11 srdy1 Tf1 Xsc kT1 npre1 sendT1 Tsc11 kr1 qT1 U0 oh1 sel1 x01 nsel1 sg Tsc10 Tpre0 ex1 sb1 sendb1 x00 Hu0 cy01 bB0 dH0 cy00 U1 x11 Tdh0 df0 vote0 x10 par tk0 td0 Hu1 dH1 Tadd0 bl Tu0 z00 Badd0 Tdh1 cy11 cy10 vote1 mS00 MS00 Tpre1 z01 tk1 mS01 bB1 td1 Tadd1 q0 rel0 df1 premS01 premS00 s0 Tu1 Badd1 eq1 crel0 n0 mC0 MS01 z11 nu0 preMS01 preMS00 eq0 e01 dup nm0 MS11 e00 dn0 mS11 difmS00 difmS01 z10 MS10 difMS00 mS10 difMS01 cm00 q1 cm01 rel1 ab00 s1 u es cnt00 cnt01 premS11 n1 crel1 ou rdy0 nu1 premS10 preMS10 sco00 ab01 sco01 te0 xs Tf0 npre0 e10 srdy0 kT0 xt e11 kr0 preMS11 nm1 qT0 Tsc01 difmS10 oh0 dn1 difMS11 mC1 cm10 difmS11 sel0 difMS10 cm11 Tsc00 nsel0 ab10 cnt10 cnt11 ex0 sb0 sendT0 ab11 sendb0 rdy1 te1 sco10 sco11 srdy1 Tf1 Xsc npre1 kT1 kr1 sendT1 Tsc11 qT1 U0 oh1 sel1 Tsc10 x01 nsel1 sg Tpre0 ex1 sb1 x00 Hu0 cy01 bB0 dH0 cy00 U1 x11 sendb1 Tdh0 vote0 x10 df0 par tk0 td0 Tadd0 Hu1 dH1 bl Tu0 Tpre1 Badd0 cy11 Tdh1 cy10 vote1 z00 mS00 MS00 tk1 td1 z01 Tadd1 df1 mS01 bB1 Tu1 q0 rel0 premS01 premS00 s0 eq1 yl0 crel0 n0 eq0 Badd1 nu0 MS01 z11 e01 dup nm0 MS11 mS11 preMS01 preMS00 e00 z10 difmS00 difMS00 MS10 mS10 cm00 difmS01 u q1 cm01 rel1 es difMS01 ab00 s1 cnt00 cnt01 ou premS11 n1 xs rdy0 premS10 crel1 ab01 sco00 xt nu1 dmacp Xsc yl1 dmayla sco01 e10 dmayclk npre0 srdy0 kT0 dn0 kr0 preMS10 te0 nm1 preMS11 e11 dn1 Tf0 qT0 Tsc01 difmS10 oh0 difMS10 cm10 difmS11 sel0 cm11 Tsc00 difMS11 cnt10 ab10 cnt11 rdy1 te1 sco10 ab11 sco11 srdy1 Tf1 Tsc11 Tsc10 npre1 kT1 kr1 dmaytr dmaytt nsel0 ex0 ys0 qT1 oh1 sel1 nsel1 ex1 ys1 dmaysl"""
+CONFIG.update(mh=False, u="M", acc=False)
+CONFIG = {'V': {'mC1', 'mC0@1', 'df0', 'e01', 'mC0@2', 'cm11', 'e10', 'mC0@0'}, 'S': set(), 'W': set(), 'tadd': 'V', 'dh': 'V', 'rel': 'V', 'xs': 'V', 'own': False, 'first': 'X', 'dnm': False, 'join': True, 'ttf': 'G', 'mh': False, 'u': 'M', 'acc': False}
+ORDER = """dmaslot dmatrav dmaclk dmatt .pi0 .iom0 .pj0 .pj1 .col0 .iog0 .BOp0 .cb0 .i1440 .CB0 .kh0 .lb0 .lb2 .lb1 .of0 bl .CH0 .CL0 .I10 .In0 .kC0 .col1 .S160 .S320 .RK0 .ones0 .of2 .PC0 .BOn0 .BT0 .hi0 .Ihf0 .RK1 .of1 .par0 .pb70 .lT0 .tS0 .sb0 .J10 .OF0 .MK0 .If0 .S5120 U0 .Ik0 .CM0 bB0 .DF1 .BOq0 .DF0 x01 .BOh0 x00 U1 .TRn0 bB1 eq0 .Jb0 dmalast Hu0 cy01 cy00 Hu1 dH0 df0 .RS0 dH1 eq1 vote0 tk0 x11 .lT1 x10 td0 Tadd0 Tu0 cy11 df1 cy10 z00 Badd0 mS00 dup .RM0 z01 mS01 q0 s0 n0 nu0 vote1 tk1 td1 e00 premS00 premS01 Tadd1 MS00 Tu1 rel0 z11 MS01 z10 Badd1 .TT0 crel0 preMS00 e01 nm0 mC0 mS11 dn0 dm0 preMS01 MS11 difmS00 difMS00 difmS01 MS10 mS10 q1 difMS01 .i320 s1 rel1 n1 nm1 dn1 .RD0 u es cm00 nu1 ou cm01 cnt00 cnt01 npre0 premS10 xs ab00 crel1 rdy0 te0 sco00 premS11 Tf0 xt ab01 e10 sco01 srdy0 kT0 Tsc01 dm1 kr0 qT0 oh0 sel0 e11 preMS11 difmS10 cm10 difmS11 preMS10 difMS10 cm11 mC1 ab10 nsel0 difMS11 ex0 Tsc00 sb0 Xsc ab11 cnt10 cnt11 rdy1 te1 Tf1 Tsc11 Tsc10 sco10 sendT0 U0 sco11 srdy1 kT1 kr1 qT1 npre1 oh1 sel1 nsel1 sendb0 Hu0 x00 sendT1 ex1 sb1 x01 cy00 cy01 U1 sg bB0 dH0 df0 vote0 par sendb1 Hu1 bB1 tk0 x11 bl x10 td0 dH1 Tadd0 Tu0 Badd0 cy11 cy10 vote1 z01 eq1 mS01 z00 df1 mS00 q0 s0 tk1 n0 td1 nu0 premS01 premS00 e00 Tadd1 Badd1 Tu1 MS01 rel0 z11 eq0 MS00 z10 e01 crel0 dup preMS00 preMS01 nm0 dn0 dm0 MS11 mS11 difmS00 cm00 difMS00 difmS01 MS10 mS10 mC0 difMS01 u rel1 q1 s1 nm1 n1 premS10 cnt00 cm01 cnt01 npre0 es premS11 nu1 ou dm1 ab00 xs preMS10 dn1 crel1 xt rdy0 te0 Tf0 e10 sco00 ab01 sco01 srdy0 Tsc01 kT0 kr0 qT0 e11 preMS11 difmS10 cm10 difmS11 difMS10 mC1 ab10 oh0 Tsc00 sel0 nsel0 difMS11 cm11 ex0 sb0 Xsc ab11 cnt10 cnt11 rdy1 te1 Tf1 Tsc11 Tsc10 sco10 sendT0 sco11 U0 sendb0 srdy1 kT1 kr1 npre1 qT1 oh1 sel1 Hu0 nsel1 bB0 sendT1 ex1 sb1 x00 x01 cy00 cy01 sg U1 dH0 df0 x10 vote0 sendb1 par Hu1 bB1 bl tk0 td0 Tadd0 Tu0 Badd0 cy10 x11 cy11 vote1 dH1 eq1 z01 z00 mS01 mS00 q0 tk1 df1 s0 n0 td1 premS00 premS01 nu0 e00 Tadd1 Tu1 eq0 rel0 z11 MS01 MS00 Badd1 dup z10 crel0 preMS00 preMS01 e01 nm0 dn0 dm0 MS11 difmS00 difMS00 difmS01 mS11 mC0 MS10 difMS01 cm00 mS10 q1 s1 n1 u nm1 rel1 es ou cm01 xs cnt00 cnt01 npre0 premS10 nu1 ab00 sco00 xt rdy0 te0 premS11 ab01 crel1 sco01 srdy0 e10 Tf0 kT0 dn1 kr0 Tsc01 qT0 dm1 preMS11 preMS10 oh0 e11 difmS10 difmS11 difMS10 cm10 mC1 sel0 nsel0 ab10 Tsc00 difMS11 cm11 ex0 sb0 Xsc cnt10 cnt11 ab11 rdy1 te1 Tf1 Tsc11 Tsc10 sco10 sendT0 U0 sco11 srdy1 sendb0 kT1 kr1 qT1 npre1 oh1 sel1 Hu0 x00 x01 nsel1 ex1 sendT1 sb1 cy00 cy01 U1 sendb1 df0 bB0 dH0 sg vote0 par bB1 Hu1 tk0 x11 bl x10 td0 dH1 Tadd0 Tu0 Badd0 cy11 cy10 vote1 z01 z00 mS01 eq1 df1 mS00 q0 s0 n0 tk1 premS00 premS01 nu0 td1 yl0 e00 MS01 Tadd1 rel0 Tu1 eq0 MS00 z11 z10 Badd1 crel0 preMS00 dup nm0 e01 dn0 dm0 preMS01 MS11 mS11 difmS00 difMS00 difmS01 cm00 MS10 mS10 yl1 dmacp q1 s1 rel1 n1 u cnt00 difMS01 nm1 es premS10 ou cm01 cnt01 npre0 xs crel1 xt Xsc ab00 rdy0 dn1 te0 ab01 sco00 sco01 srdy0 preMS10 premS11 dmayla dmayclk nu1 dm1 Tf0 e10 Tsc01 kT0 kr0 preMS11 qT0 oh0 sel0 e11 difmS10 cm10 difmS11 difMS10 ab10 Tsc00 difMS11 cm11 ab11 cnt10 cnt11 rdy1 te1 Tf1 Tsc11 Tsc10 nsel0 sco10 sco11 srdy1 dmaytr ex0 dmaytt npre1 ys0 kT1 kr1 qT1 oh1 sel1 nsel1 ex1 ys1 dmaysl"""
+CONFIG = {'mh': False, 'u': 'M', 'acc': False, 'V': {'df0', 'mC0@3', 'df1', 'e01', 'e10', 'mC0@0', 'mC1@3'}, 'S': set(), 'W': {'cy1@0', 'mS0', 'x1@0'}, 'tadd': 'P', 'dh': 'V', 'rel': 'V', 'xs': 'V', 'own': False, 'first': 'X', 'dnm': True, 'join': True, 'ttf': 'G'}
+ORDER = """dmaslot .RD0 .BT0 .BT1 .i321 .kh0 .i320 .DF1 .BT2 .BT3 .lb0 .RS0 .pb70 .kC0 .RD1 .pi0 dmatrav dmaclk dmatt .pj0 .iom0 .RK0 .of0 .pj1 .col0 .i1440 .ones0 .par0 .lb2 .cb0 .col1 dmalast .PC0 .MK0 .CB0 .RM0 .lT0 .RM1 .DF0 .CH0 .RK1 .I10 .If0 Tpre0 .iog0 .sb0 .CL0 .lb1 .of1 .CM0 U0 Tpre1 .Ik0 x01 .J10 x00 .S160 .In0 .S5120 .of2 U1 .OF0 .Ihf0 bB1 .BOp0 .RS1 .Jb0 df0 bl Hu0 cy01 cy00 .lT1 .BOn0 bB0 x11 dH0 .BOq0 vote0 Hu1 dH1 .RD2 .TRn0 .TT0 tk0 td0 Tadd0 eq0 Tu0 z00 cy11 Badd0 vote1 MS00 z01 mS01 premS01 tk1 q0 td1 Tadd1 df1 MS01 Tu1 s0 preMS01 z11 eq1 n0 rel0 nu0 mC0 premS00 Badd1 e00 nm0 e01 preMS00 z10 dup MS11 mS11 difmS00 dn0 difmS01 difMS01 .BOh0 MS10 mS10 q1 rel1 s1 crel0 difMS00 cm00 cm01 u es ab00 cnt00 cnt01 premS10 ab01 sco00 n1 premS11 rdy0 sco01 srdy0 te0 nu1 Tf0 npre0 e11 preMS10 e10 mC1 kT0 ou kr0 nm1 sendT0 qT0 crel1 Tsc01 oh0 xs difmS10 cm10 difmS11 preMS11 cm11 difMS10 sel0 dn1 xt ab10 nsel0 ex0 Tsc00 sb0 difMS11 cnt10 Xsc cnt11 ab11 rdy1 sco10 sendb0 sco11 srdy1 te1 Tf1 npre1 Tsc11 kT1 kr1 U0 qT1 oh1 Tsc10 sel1 Tpre0 nsel1 x01 sg Hu0 ex1 sb1 sendT1 cy01 x00 cy00 vote0 U1 par x11 bB0 sendb1 df0 dH0 tk0 bB1 td0 Hu1 bl Tadd0 x10 dH1 eq0 Tu0 z00 Badd0 cy11 cy10 MS00 Tpre1 vote1 z01 mS01 premS01 tk1 q0 td1 mC0 Tadd1 MS01 s0 premS00 Tu1 z11 df1 preMS01 n0 nm0 nu0 Badd1 eq1 dup e00 dn0 z10 e01 MS11 rel0 preMS00 difmS00 mS11 difMS01 difmS01 cm00 crel0 difMS00 MS10 mS10 q1 rel1 cm01 ab00 ab01 s1 u es cnt00 cnt01 n1 ou premS11 premS10 rdy0 sco00 sco01 nu1 crel1 srdy0 te0 e10 Tf0 e11 mC1 kT0 xs sendT0 preMS10 kr0 nm1 qT0 oh0 dn1 difmS10 cm10 npre0 difmS11 sel0 difMS10 xt Tsc01 cm11 preMS11 ab10 nsel0 difMS11 ex0 cnt10 cnt11 Tsc00 sb0 Xsc rdy1 sco10 ab11 sendb0 te1 Tf1 Tsc11 sco11 srdy1 npre1 kT1 Tsc10 kr1 U0 qT1 oh1 sel1 nsel1 Hu0 sg x01 ex1 sb1 x00 Tpre0 cy01 sendT1 cy00 U1 df0 sendb1 x10 x11 par bB0 dH0 vote0 tk0 td0 Tadd0 bl Hu1 dH1 bB1 Tu0 z00 Tpre1 Badd0 cy10 cy11 vote1 MS00 z01 mS01 premS01 tk1 q0 td1 Tadd1 eq0 s0 mC0 Tu1 df1 n0 premS00 nm0 nu0 Badd1 MS01 preMS01 z11 e00 eq1 dup e01 preMS00 z10 dn0 mS11 difmS00 MS11 difmS01 rel0 difMS00 crel0 difMS01 cm00 MS10 mS10 q1 rel1 s1 cm01 ab00 u cnt00 cnt01 es ab01 n1 ou premS10 rdy0 premS11 crel1 sco00 sco01 nu1 srdy0 te0 e11 e10 mC1 Tf0 kT0 xs kr0 nm1 preMS10 xt sendT0 qT0 oh0 difmS11 cm11 difmS10 cm10 npre0 preMS11 sel0 difMS10 dn1 ab10 nsel0 difMS11 Tsc01 ex0 cnt10 cnt11 Tsc00 sb0 Xsc npre1 sendb0 rdy1 te1 Tf1 sco10 ab11 sco11 srdy1 Tsc11 kT1 Tpre0 kr1 qT1 U0 x00 oh1 sendT1 sel1 Tsc10 x01 nsel1 ex1 Hu0 sb1 sg df0 cy00 cy01 sendb1 U1 x10 vote0 Tpre1 dH0 par x11 bB0 tk0 td0 bl Hu1 dH1 Tadd0 bB1 Tu0 z00 Badd0 cy10 cy11 MS00 vote1 z01 mS01 premS01 tk1 q0 td1 Tadd1 s0 yl0 premS00 eq0 Tu1 df1 n0 MS01 nm0 nu0 Badd1 preMS01 z10 eq1 rel0 e00 crel0 z11 e01 preMS00 dup dn0 difmS01 MS10 difMS01 dmacp mS10 difmS00 MS11 u difMS00 mS11 rel1 q1 cm01 cm00 es cnt00 ou cnt01 s1 xs ab00 n1 xt crel1 premS10 rdy0 Xsc nu1 e10 sco00 premS11 yl1 ab01 sco01 srdy0 preMS11 kT0 kr0 nm1 qT0 oh0 sel0 e11 preMS10 difmS10 cm10 te0 Tf0 dmayla difmS11 cm11 difMS10 npre0 dn1 dmayclk ab10 nsel0 ex0 cnt10 cnt11 Tsc01 difMS11 rdy1 ys0 sco10 Tsc00 ab11 sco11 srdy1 te1 Tf1 Tsc11 Tsc10 npre1 dmaytr dmaytt kT1 kr1 qT1 oh1 sel1 nsel1 ex1 ys1 dmaysl"""
+CONFIG = {'mh': False, 'u': 'M', 'acc': False, 'V': {'mC0', 'e10', 'e01', 'x11@0', 'mC1@1', 'x10@0'}, 'S': set(), 'W': {'cy1@1', 'cy1@0', 'cy1@2'}, 'tadd': 'V', 'dh': 'V', 'rel': 'V', 'xs': 'V', 'own': False, 'first': 'X', 'dnm': False, 'join': True, 'ttf': 'G', 'u16': True, 'split': True}
+ORDER = """dmaslot dmatrav dmaclk .pi0 .BT0 .of0 .BT1 .BT2 .BT3 .i321 .DF1 dmatt .kh0 .lb0 .i1440 .RM0 .of2 .pb70 .RK0 .RK1 .RM1 .pj1 .RS0 .I10 .J10 .of1 .lb1 .pj0 .lb2 .OF0 bl bB0 bB1 .iom0 .col0 eq0 .col1 .i320 .DF0 .kC0 df0 .ones0 .In0 .Jb0 .cb0 .PC0 .CB0 .S160 .iog0 .S5120 .MK0 .CM0 .Ik0 .If0 .RD0 .CH0 .par0 U0 .BOp0 .BOn0 .BOq0 .RD1 .RD2 .sb0 .lT0 U1 .Ihf0 .CL0 .RS1 eq1 x01 x00 .BOh0 x10 x11 Hu0 cy01 cy00 dH1 dH0 vote0 Hu1 df1 tk0 td0 dmalast .lT1 Tadd0 Tu0 cy11 z00 mS00 MS00 z01 Badd0 mS01 vote1 tk1 q0 td1 s0 Tadd1 n0 Tu1 premS01 .TRn0 premS00 z11 nu0 Badd1 MS01 dup e00 preMS01 dn0 z10 e01 preMS00 nm0 rel0 mS11 crel0 MS11 difmS00 mC0 MS10 difmS01 cm00 difMS00 difMS01 mS10 dm0 u cnt00 cm01 q1 cnt01 rel1 s1 es crel1 ab00 n1 premS11 premS10 nm1 rdy0 nu1 ou ab01 .TT0 sco00 sco01 e11 e10 te0 srdy0 preMS10 difmS10 difmS11 preMS11 difMS10 difMS11 cm10 kT0 cm11 Tf0 kr0 Uo0 sendT0 xs qT0 dn1 xt oh0 ab10 Tsc01 mC1 cnt10 sel0 npre0 nsel0 Xsc Tsc00 ex0 cnt11 sb0 sco10 ab11 sco11 rdy1 srdy1 sendb0 dm1 te1 Tf1 kT1 Uo1 x00 kr1 npre1 qT1 oh1 Tsc11 sel1 nsel1 Tsc10 ex1 sb1 sendT1 sg x01 U0 Hu0 dH0 df0 x10 cy00 cy01 vote0 sendb1 par bB0 U1 x11 bl bB1 tk0 Hu1 td0 Tadd0 dH1 Tu0 df1 cy11 z00 mS00 z01 MS00 Badd0 mS01 vote1 tk1 q0 td1 s0 Tadd1 nm0 premS00 Tu1 n0 rel0 eq0 premS01 nu0 MS01 Badd1 eq1 z11 e01 crel0 preMS00 dup e00 mS11 dn0 preMS01 MS11 difmS00 mC0 z10 MS10 difmS01 cm00 difMS00 difMS01 mS10 dm0 u q1 cm01 cnt00 cnt01 rel1 s1 es crel1 ab00 n1 premS11 premS10 nm1 ab01 rdy0 nu1 ou sco00 sco01 e11 e10 te0 srdy0 preMS11 difmS10 preMS10 difmS11 dn1 kT0 difMS11 cm10 Tf0 kr0 difMS10 cm11 Uo0 xs qT0 ab10 Tsc01 cnt10 oh0 xt sendT0 sel0 npre0 nsel0 mC1 Xsc ex0 cnt11 rdy1 sb0 te1 Tsc00 Tf1 dm1 ab11 sco10 Uo1 sco11 srdy1 sendb0 kT1 kr1 qT1 Tsc11 x00 oh1 npre1 sel1 nsel1 sendT1 sg Tsc10 ex1 sb1 x01 Hu0 par df0 cy00 cy01 U0 bB0 U1 x10 x11 sendb1 dH0 bl dH1 vote0 tk0 bB1 td0 Hu1 Tadd0 eq0 Tu0 cy11 z00 mS00 z01 MS00 Badd0 mS01 df1 vote1 tk1 q0 td1 s0 Tadd1 n0 Tu1 eq1 premS01 MS01 nu0 z11 premS00 dn0 rel0 Badd1 preMS00 e01 MS11 dup e00 preMS01 mS11 nm0 crel0 difmS00 z10 MS10 cm00 difMS00 difmS01 difMS01 mS10 cm01 u mC0 q1 rel1 s1 cnt00 cnt01 es crel1 ab00 n1 premS11 premS10 nm1 rdy0 ab01 nu1 ou sco00 sco01 te0 srdy0 preMS10 e11 e10 preMS11 difmS10 cm10 difmS11 difMS10 difMS11 Tf0 kT0 cm11 dm0 Uo0 kr0 xs qT0 dn1 ab10 Tsc01 oh0 cnt10 xt mC1 sendT0 Tsc00 sel0 npre0 nsel0 Xsc ex0 cnt11 sb0 sco10 ab11 sco11 rdy1 srdy1 te1 dm1 Tf1 kT1 Uo1 x00 kr1 Tsc11 qT1 sendb0 oh1 npre1 sendT1 sel1 nsel1 Tsc10 sg ex1 sb1 Hu0 U0 x01 df0 cy00 cy01 par sendb1 dH0 bB0 U1 x11 x10 vote0 bl tk0 Hu1 df1 td0 dH1 Tadd0 bB1 Badd0 Tu0 cy11 cy10 vote1 z00 mS00 z01 MS00 eq0 tk1 mS01 td1 q0 yl0 Tadd1 s0 dmacp0 Tu1 eq1 n0 premS00 z10 MS01 premS01 nu0 nm0 rel0 Badd1 e01 u0 dmacp1 dup crel0 dn0 us0 preMS00 mS10 e00 preMS01 difmS00 z11 MS10 ju0 mS11 xs0 difMS00 cm00 q1 xt0 MS11 difmS01 cm01 yl1 dmayla difMS01 Xsc0 cnt00 u1 cnt01 rel1 s1 crel1 ab00 us1 nm1 n1 premS11 premS10 preMS10 es rdy0 ab01 nu1 ju1 sco00 sco01 te0 e11 e10 xs1 dmayc0 Tf0 preMS11 xt1 ou Xsc1 dn1 difmS10 srdy0 cm10 dmayc1 difmS11 difMS10 difMS11 kT0 cm11 dm1 dm0 ab10 Tsc01 cnt10 kr0 Tsc00 qT0 cnt11 rdy1 sco10 ab11 sco11 srdy1 te1 npre0 Tf1 Tsc11 Tsc10 oh0 npre1 kT1 sel0 nsel0 kr1 qT1 ex0 oh1 sel1 nsel1 ex1 ys0 ys1 dmaytr dmaytt dmaysl"""
+CONFIG = {'mh': False, 'u': 'M', 'acc': False, 'V': {'mC0', 'df0', 'e01', 'x11@0', 'e10', 'df1@0'}, 'S': set(), 'W': {'x0@1', 'cy1@1', 'x1', 'mS0@2', 'cy1@2'}, 'tadd': 'P', 'dh': 'V', 'rel': 'V', 'xs': 'V', 'own': False, 'first': 'X', 'dnm': True, 'join': True, 'ttf': 'G', 'u16': True, 'split': True, 'C': {'0@1'}}
+ORDER = """.BT0 .par0 .BT1 .i321 .BT2 .RM0 .kC0 .pi0 .RS0 .RM1 .pj0 .RK0 .lb0 .iog0 .RK1 .BT3 .DF0 .i1440 .of1 .iom0 .RS1 .sb0 .RD0 .pj1 .col0 .I10 .Jb0 .DF1 .cb0 .BOp0 .kh0 .pb70 .BOh0 .ones0 .RD1 .CB0 .CH0 .BOn0 dmaslot .lb1 .lb2 dmatrav .of0 bl df0 .lT0 .Ihf0 dmaclk dmatt .If0 Tpre1 bB1 .of2 .OF0 bB0 .J10 .CL0 .RD2 .BOq0 U0 .col1 .S160 .PC0 .MK0 .i320 .CM0 .Ik0 .In0 U1 eq0 eq1 x00 dmalast x01 .TRn0 x11 Hu0 cy00 cy01 dup .S5120 Tpre0 dH1 dH0 vote0 tk0 td0 Tadd0 Hu1 df1 Tu0 cy10 cy11 .lT1 z00 Badd0 z01 mS00 mS01 mC0 vote1 tk1 .TT0 q0 premS00 td1 MS01 Tadd1 Tu1 z11 s0 premS01 MS00 n0 rel0 Badd1 nu0 preMS00 sendc0 e00 preMS01 e01 nm0 z10 crel0 mS11 MS11 dn0 difmS00 mS10 difMS00 difmS01 difMS01 cm00 cnt00 premS10 cm01 q1 MS10 ab00 s1 ab01 u mC1 cnt01 n1 nm1 nu1 rel1 preMS10 sco00 dn1 es sco01 e10 premS11 rdy0 srdy0 e11 difmS10 difmS11 cm10 ou te0 crel1 cm11 xs Tf0 kT0 difMS10 Uo0 kr0 Tsc01 qT0 preMS11 xt ab10 oh0 sel0 difMS11 npre0 nsel0 cnt10 sendT0 cnt11 ab11 sco10 sco11 Xsc x01 ex0 sb0 rdy1 Tsc00 te1 Tf1 srdy1 sendb0 npre1 kT1 Uo1 kr1 Tsc11 qT1 oh1 U0 sel1 nsel1 sg Tsc10 ex1 Hu0 Tpre0 sb1 cy00 sendT1 cy01 U1 par bB0 df0 x11 dH0 vote0 tk0 sendb1 bl td0 Hu1 Tadd0 Tpre1 bB1 df1 Tu0 cy11 z00 dH1 Badd0 z01 mS00 mS01 vote1 tk1 mC0 premS00 q0 td1 eq1 s0 Tadd1 Tu1 MS00 n0 premS01 z11 Badd1 eq0 dup nu0 MS01 nm0 preMS00 e00 preMS01 z10 e01 dn0 difmS00 cm00 difMS00 difmS01 rel0 crel0 mS11 MS11 difMS01 cm01 cnt00 ab00 mS10 MS10 u q1 premS10 rel1 s1 cnt01 mC1 ab01 n1 nu1 preMS10 nm1 sco00 e10 dn1 rdy0 sco01 srdy0 premS11 e11 difmS11 es difmS10 crel1 te0 ou cm11 difMS10 cm10 Tf0 kT0 xs kr0 Uo0 xt preMS11 qT0 Tsc01 oh0 ab10 sel0 npre0 nsel0 difMS11 cnt10 sendT0 cnt11 ab11 sco10 sco11 Xsc x01 ex0 sb0 rdy1 Tsc00 te1 Tf1 srdy1 npre1 kT1 Uo1 kr1 Tsc11 qT1 U0 oh1 sendb0 sel1 nsel1 Tpre0 Tsc10 ex1 Hu0 x00 sb1 cy01 cy00 sg par sendT1 U1 bB0 dH0 df0 x11 vote0 tk0 sendb1 bl td0 Tadd0 Hu1 dH1 df1 Tu0 cy11 Tpre1 bB1 Badd0 z01 z00 mS01 eq0 vote1 tk1 q0 rel0 premS00 td1 eq1 s0 mC0 premS01 Tadd1 Tu1 dup MS00 n0 z10 Badd1 MS01 preMS00 nu0 e00 preMS01 z11 nm0 e01 dn0 difmS00 cm00 difMS00 difmS01 mS10 MS10 MS11 difMS01 u cm01 crel0 mS11 q1 rel1 s1 ab00 cnt00 premS10 cnt01 sco00 mC1 n1 ab01 preMS10 nm1 nu1 dn1 e10 rdy0 sco01 srdy0 e11 premS11 es te0 ou difmS10 difMS10 difmS11 cm10 preMS11 crel1 ab10 Tf0 kT0 xs kr0 cm11 xt qT0 Uo0 oh0 Tsc01 sel0 Tsc00 npre0 nsel0 difMS11 cnt10 cnt11 ex0 sb0 sendT0 ab11 sendb0 Xsc x01 rdy1 te1 sco10 sco11 srdy1 Tf1 kT1 Uo1 kr1 qT1 Tsc11 npre1 oh1 U0 sel1 nsel1 sg Tsc10 ex1 Hu0 x00 sb1 cy01 cy00 Tpre0 df0 par dH0 bB0 sendT1 U1 vote0 tk0 sendb1 bl td0 Hu1 x11 dmacp0 Tadd0 Tpre1 bB1 df1 Tu0 cy10 cy11 dH1 Badd0 z01 mS01 z00 mS00 yl0 eq0 vote1 tk1 q0 premS00 dmacp1 td1 eq1 s0 rel0 premS01 Tadd1 Tu1 MS01 MS00 n0 dup z10 nm0 Badd1 nu0 e00 preMS01 z11 dn0 e01 u0 us0 preMS00 difmS00 cm00 mS10 ju0 crel0 MS10 xs0 mS11 difMS00 difmS01 xt0 MS11 difMS01 cm01 ab00 cnt00 u1 ab01 Xsc0 q1 rel1 s1 cnt01 premS10 preMS10 us1 n1 ju1 nm1 sco00 rdy0 sco01 srdy0 xs1 nu1 e11 dmayc0 xt1 te0 e10 es difmS10 premS11 Xsc1 difmS11 dn1 ou crel1 Tf0 kT0 kr0 Tsc01 yl1 qT0 Tsc00 difMS10 cm10 cm11 cnt10 dmayla dmayc1 ab10 cnt11 preMS11 difMS11 oh0 rdy1 sel0 npre0 nsel0 ab11 sco10 sco11 srdy1 te1 Tf1 Tsc11 Tsc10 dmaytr npre1 kT1 ex0 kr1 qT1 oh1 sel1 dmaytt ys0 nsel1 ex1 ys1 dmaysl"""
+CONFIG = {'mh': False, 'u': 'M', 'acc': True, 'C': {'0@1'}, 'u16': True, 'split': True, 'V': {'mC0', 'e10', 'e01', 'mC1@1', 'x10@0', 'mC1@0'}, 'S': set(), 'W': {'cy0@3'}, 'tadd': 'V', 'dh': 'V', 'rel': 'V', 'xs': 'V', 'own': False, 'first': 'X', 'dnm': False, 'join': True, 'ttf': 'G'}
+ORDER = """.BT0 .BT1 dmaslot dmatrav dmaclk dmatt .RM0 .lb0 .DF1 .i320 .BT2 .RS0 .pb70 .pi0 .par0 .i321 .pj1 .BT3 .sb0 .of0 .RK0 .RM1 .RS1 .iom0 .kC0 .pj0 .kh0 .col0 .MK0 .RK1 .ones0 .cb0 .CB0 .i1440 .RD0 .CM0 .DF0 .lT0 .RD1 .of2 .I10 .lb2 .Jb0 .CH0 .col1 .In0 .lb1 .J10 .of1 .OF0 bB0 .Ik0 U1 U0 .CL0 bB1 .S160 .PC0 x01 x10 .Ihf0 .S5120 bl x00 df0 .iog0 .BOp0 x11 .BOq0 .RD2 .BOn0 eq0 .TRn0 .If0 Hu0 cy01 cy00 Hu1 dH0 dH1 .TT0 cy10 vote0 tk0 dmalast td0 Tadd0 Tu0 df1 cy11 .lT1 eq1 .BOh0 Badd0 z00 mS00 MS00 z01 mS01 vote1 tk1 q0 td1 mC0 premS01 Tadd1 s0 Tu1 sendc0 n0 z11 nu0 rel0 MS01 e00 e01 z10 premS00 mS11 MS11 D0 dup Badd1 difmS01 nm0 MS10 mS10 difmS00 crel0 dn0 u q1 cm00 mC1 difMS00 dm0 premS11 s1 cm01 D1 n1 es difMS01 cnt00 cnt01 premS10 ab00 ab01 sco00 sco01 nm1 nu1 dn1 ou e10 rdy0 xs dm1 e11 srdy0 te0 rel1 difmS10 xt kT0 cm10 difmS11 Tf0 kr0 Uo0 qT0 Tsc01 crel1 cm11 npre0 difMS10 oh0 cnt10 sel0 Xsc nsel0 difMS11 ex0 Tsc00 cnt11 sb0 ab10 rdy1 ab11 sendT0 sco10 sco11 srdy1 te1 Tf1 Tsc11 kT1 Uo1 x00 sendb0 npre1 x01 kr1 qT1 oh1 sel1 nsel1 sendT1 x11 x10 Tsc10 df0 ex1 sb1 sg Hu0 sendb1 cy00 cy01 U0 bB0 U1 par dH0 vote0 tk0 bB1 td0 Hu1 dH1 Tadd0 bl Tu0 df1 cy11 Badd0 cy10 z00 MS00 mS00 z01 mS01 vote1 tk1 q0 td1 premS00 rel0 premS01 Tadd1 s0 Tu1 eq1 n0 eq0 z11 nu0 MS01 mC0 e00 e01 D0 crel0 mS11 Badd1 MS11 dup difmS00 difmS01 z10 MS10 nm0 mS10 dn0 u q1 dm0 cm00 mC1 difMS00 s1 premS11 cm01 D1 n1 es difMS01 cnt00 cnt01 nm1 nu1 premS10 dn1 ou e10 ab00 ab01 sco00 sco01 rdy0 dm1 xs e11 srdy0 te0 rel1 difmS10 kT0 xt cm10 difmS11 kr0 Tf0 qT0 Tsc01 Uo0 crel1 cm11 npre0 difMS10 cnt10 oh0 ab10 Tsc00 cnt11 sel0 difMS11 Xsc nsel0 rdy1 ab11 sendT0 sco10 sco11 srdy1 ex0 sb0 te1 Tf1 Tsc11 kT1 sendb0 npre1 x01 kr1 Uo1 qT1 oh1 sel1 nsel1 sendT1 x00 x11 x10 df0 Tsc10 ex1 sb1 sendb1 sg Hu0 cy01 cy00 U0 bB0 U1 par dH0 bl bB1 vote0 tk0 Hu1 td0 dH1 Tadd0 Tu0 cy10 df1 cy11 Badd0 z00 MS00 mS00 vote1 z01 mS01 tk1 q0 td1 rel0 premS01 Tadd1 s0 Tu1 n0 eq1 eq0 z11 nu0 premS00 MS01 e00 e01 D0 mS11 MS11 Badd1 dup crel0 mC0 z10 difmS01 MS10 nm0 mS10 dn0 dm0 difmS00 u q1 cm00 premS10 mC1 difMS00 cm01 es difMS01 cnt00 cnt01 premS11 s1 D1 n1 nm1 nu1 dn1 ou e10 ab00 ab01 sco00 sco01 rdy0 dm1 e11 xs srdy0 te0 rel1 kT0 xt difmS10 cm10 difmS11 Tf0 kr0 Uo0 crel1 cm11 npre0 difMS10 cnt10 qT0 oh0 Tsc01 ab10 sel0 Xsc nsel0 ex0 difMS11 Tsc00 cnt11 sb0 rdy1 ab11 sendT0 sco10 sco11 srdy1 te1 Tf1 Tsc11 x00 kT1 Uo1 sendb0 npre1 x01 kr1 qT1 oh1 sel1 nsel1 sendT1 x10 df0 x11 Tsc10 ex1 sb1 sendb1 sg Hu0 bB0 cy01 U0 U1 par dH0 bB1 bl vote0 tk0 Hu1 td0 dH1 Tadd0 Tu0 df1 cy11 cy10 Badd0 z00 mS00 MS00 z01 mS01 vote1 tk1 q0 td1 premS00 rel0 premS01 Tadd1 s0 Tu1 n0 MS01 eq0 nu0 yl0 z11 dmacp0 eq1 D0 e01 z10 e00 mS11 Badd1 dup nm0 u0 dn0 crel0 difmS01 difmS00 mS10 us0 MS10 MS11 dm0 ju0 D1 q1 u1 premS11 xs0 us1 xt0 s1 yl1 ju1 Xsc0 dmacp1 cm01 difMS01 cm00 difMS00 nm1 es cnt00 cnt01 premS10 n1 dm1 nu1 dn1 ab01 ab00 sco00 sco01 ou dmayc0 e10 rdy0 e11 difmS10 xs1 srdy0 te0 rel1 xt1 difmS11 Tf0 Xsc1 dmayla dmayc1 kT0 cm10 Tsc01 kr0 qT0 crel1 cm11 npre0 difMS10 cnt10 oh0 sel0 ab10 Tsc00 cnt11 rdy1 te1 Tf1 Tsc11 difMS11 nsel0 ex0 ab11 sco10 sco11 srdy1 dmaytr npre1 Tsc10 dmaytt kT1 kr1 qT1 oh1 sel1 nsel1 ex1 ys0 ys1 dmaysl"""
+CONFIG = {'mh': True, 'u': 'S', 'acc': False, 'C': {'0@1'}, 'u16': True, 'split': True, 'V': {'df0', 'df1', 'e01', 'e10', 'x10@0'}, 'S': set(), 'W': {'x1@3'}, 'tadd': 'V', 'dh': 'V', 'rel': 'W', 'xs': 'V', 'own': False, 'first': 'X', 'dnm': False, 'join': True, 'ttf': 'G'}
+ORDER = """.pi0 .RK0 .pj1 .RK1 .sb0 .pj0 .i1440 .col0 .RS0 .RS1 .p320 .col1 .RD0 .RD1 .BT0 .i321 .RM0 .L320 .I10 .lb0 .In0 .iom0 .BT1 .PC0 .iog0 .BT2 .BT3 .RM1 .DF1 .J10 dmaslot dmatrav dmaclk .ones0 dmatt .L321 .of1 .cb0 .pb70 .S160 .S5120 .kh0 .MK0 .lb1 .lT0 U1 .kC0 .lb2 .CM0 bB1 .of0 .of2 .par0 .RD2 bl U0 bB0 .OF0 dmalast .BOp0 x01 .i320 x10 Hu0 x00 .BOn0 .TRn0 .TT0 .BOq0 dH0 cy01 cy00 A81 .lT1 .DF0 x11 Hu1 cy10 vote0 tk0 dH1 td0 .BOh0 Tadd0 df1 Tu0 cy11 eq1 .Ik0 vote1 A80 z00 MS00 mS00 z01 mS01 tk1 premS00 premS01 mh0 td1 q0 Tadd1 MS01 Tu1 z11 s0 rel0 n0 df0 preMS01 nu0 e00 mC0 eq0 e01 preMS00 MS11 crel0 dup difmS01 mS11 dn0 difmS00 difMS00 sendc0 nm0 difMS01 z10 mS10 MS10 dm0 u cm00 premS10 cm01 mh1 rel1 q1 cnt00 cnt01 mC1 es npre0 ab00 s1 crel1 sco00 ui preMS10 ab01 premS11 sco01 n1 ou nm1 nu1 uj rdy0 e10 e11 srdy0 difmS10 uk cm10 te0 difmS11 cm11 dn1 ju Tf0 kT0 xs difMS10 kr0 dm1 xt Uo0 qT0 Xsc oh0 preMS11 difMS11 cnt10 cnt11 Tsc01 sendT0 sel0 nsel0 Tsc00 ab10 rdy1 sco10 ex0 te1 sb0 ab11 sco11 srdy1 sendb0 Tf1 Uo1 x01 kT1 kr1 qT1 oh1 npre1 sendT1 sel1 Tsc11 nsel1 ex1 sb1 Tsc10 U0 Hu0 x00 dH0 cy01 cy00 df0 bB0 U1 sendb1 sg par x10 A81 x11 bB1 Hu1 vote0 tk0 dH1 td0 df1 Tadd0 bl Tu0 cy10 cy11 A80 z00 mS00 MS00 eq1 vote1 z01 mS01 tk1 td1 mh0 Tadd1 premS00 q0 Tu1 MS01 premS01 z11 s0 rel0 n0 preMS01 mC0 nm0 nu0 e00 eq0 e01 crel0 preMS00 dup MS11 difmS00 difMS00 difmS01 mS11 dn0 dm0 z10 MS10 difMS01 mS10 cm00 u cm01 premS10 mh1 rel1 q1 cnt00 cnt01 es mC1 ab00 s1 npre0 crel1 sco00 ab01 premS11 sco01 ui preMS10 n1 ou rdy0 nu1 uj e11 srdy0 nm1 e10 difmS10 cm10 uk te0 dn1 ju Tf0 difmS11 kT0 difMS10 xs dm1 kr0 xt Uo0 qT0 Xsc oh0 Tsc01 cm11 preMS11 cnt10 difMS11 sendT0 sel0 cnt11 Tsc00 ab10 nsel0 rdy1 sco10 ex0 te1 sb0 ab11 sco11 srdy1 sendb0 Tf1 Uo1 sendT1 x00 x01 kT1 kr1 qT1 oh1 npre1 sel1 Tsc11 nsel1 ex1 sb1 Tsc10 U0 Hu0 dH0 cy01 cy00 sendb1 sg x10 A81 x11 df0 U1 bB0 par bl Hu1 vote0 bB1 tk0 dH1 td0 df1 Tadd0 Tu0 cy10 cy11 eq1 vote1 A80 z00 MS00 z01 mS00 mS01 tk1 mh0 td1 premS00 q0 Tadd1 MS01 premS01 Tu1 s0 rel0 z11 n0 preMS01 mC0 nm0 nu0 e00 eq0 e01 crel0 preMS00 dup MS11 difmS00 difMS01 dn0 difMS00 difmS01 mS11 dm0 z10 mS10 MS10 cm00 premS10 u cm01 mh1 rel1 q1 cnt00 cnt01 ab00 s1 mC1 npre0 es crel1 n1 nm1 nu1 ui preMS10 ab01 sco00 premS11 sco01 ou e10 uj rdy0 uk te0 e11 srdy0 difmS10 dn1 cm10 ju Tf0 difMS10 difmS11 kT0 xs kr0 dm1 cm11 xt Uo0 preMS11 qT0 Xsc oh0 Tsc01 cnt10 difMS11 sendT0 sel0 cnt11 nsel0 Tsc00 ab10 rdy1 sco10 ab11 ex0 sco11 srdy1 te1 sb0 sendb0 Tf1 x00 x01 Uo1 kT1 kr1 qT1 oh1 npre1 sel1 Tsc11 sendT1 nsel1 ex1 sb1 Tsc10 U0 Hu0 bB0 cy01 cy00 dH0 df0 U1 sendb1 sg par bB1 x11 bl A81 Hu1 vote0 dmacp0 tk0 dH1 td0 df1 Tadd0 Tu0 cy10 cy11 A80 z00 MS00 vote1 mS00 eq1 z01 mS01 tk1 mh0 td1 premS01 premS00 q0 Tadd1 MS01 Tu1 s0 yl0 n0 z11 rel0 u0 preMS01 nu0 e00 eq0 e01 preMS00 crel0 dup MS11 nm0 difmS00 dn0 difMS00 difmS01 mS11 dm0 es us0 difMS01 z10 mS10 MS10 cm00 cm01 premS10 u1 ju0 rel1 xs0 mh1 xt0 q1 cnt00 cnt01 Xsc0 ab00 s1 sco00 ab01 premS11 sco01 us1 n1 crel1 preMS10 nm1 nu1 ju1 rdy0 e10 srdy0 dn1 xs1 yl1 te0 ou kT0 xt1 dmacp1 e11 difmS10 cm10 difmS11 difMS10 kr0 Xsc1 npre0 dmayc0 qT0 Tf0 oh0 preMS11 cm11 Tsc01 cnt10 sel0 cnt11 Tsc00 difMS11 ab10 nsel0 rdy1 te1 dm1 sco10 ab11 Tf1 ex0 sco11 srdy1 dmayla Tsc11 npre1 Tsc10 dmayc1 kT1 kr1 qT1 oh1 sel1 dmaytr nsel1 ex1 ys0 dmaytt ys1 dmaysl"""
 
 
-def build(T, send):
-    ops, now = [], {}
+def build(T, send, cfg):
+    ops, now = [], {"v": 0}
 
     def ap(name, a=0, b=None, step=None):
         b = T[name].shape[1] if b is None else b
         return (name, a, b, T[name][:, a:b] if step is None else T[name][:, a:b:step])
-
-    def slot(name, v, h):
-        return ap(name, 16 * v + 8 * h, 16 * v + 8 * h + 4)
 
     def val(x):
         return x[3] if isinstance(x, tuple) else x
@@ -74,437 +70,512 @@ def build(T, send):
         return [x for x in xs if isinstance(x, tuple)]
 
     def two(*xs):
-        return all(SCRATCH[x[0]][2] in ("bfloat16", "float16", "uint16") for x in xs)
+        return all(SCRATCH[x[0]][2] in (BF, F16, U16) for x in xs)
 
     def cnt(x):
         return x[3].shape[1]
 
-    def add(eng, fn, rd, wr, kind, n, **kw):
-        ops.append(dict(eng=eng, fn=fn, rd=rd, wr=wr, kind=kind, n=n, **kw, **now))
+    def add(name, eng, fn, rd, wr, kind, n, **kw):
+        if not name or name == "TTf":
+            name = "%s%s%d" % (name or ".", wr[0][0], sum(o["wr"][0][0] == wr[0][0] for o in ops))
+        ops.append(dict(name=name, eng=eng, fn=fn, rd=rd, wr=wr, kind=kind, n=n, **kw, **now))
         return ops[-1]
 
-    def ind(win, off):
-        return win[3].indirect(off[3])
+    def named(key, name):
+        return name in cfg[key] or "%s@%d" % (name, now["v"]) in cfg[key]
 
-    def tt(out, a, b, op):
+    def on(name):
+        return "V" if named("V", name) else "S"
+
+    def off(name):
+        return named("S", name)
+
+    def ind(win, o):
+        return win[3].indirect(o[3])
+
+    def tt(name, out, a, b, op):
         both = SCRATCH[a[0]][0] == "sbuf" and SCRATCH[b[0]][0] == "sbuf"
-        return add("V", lambda q, e: [q.tensor_tensor(out[3], a[3], b[3], op)], [a, b], [out], "v", cnt(out) * (2 if both else 1))
+        return add(name, "V", lambda q: [q.tensor_tensor(out[3], a[3], b[3], op)], [a, b], [out], "v", cnt(out) * (2 if both else 1))
 
-    def ts(out, a, s1, s2, op0, op1=None):
-        def fn(q, e):
+    def ts(name, out, a, s1, s2, op0, op1=None):
+        def fn(q):
             if op1 is None:
                 return [q.tensor_scalar(out[3], a[3], val(s1), None, op0)]
             return [q.tensor_scalar(out[3], a[3], val(s1), val(s2), op0, op1)]
-        return add("V", fn, [a] + aps(s1, s2), [out], "v", cnt(out) * (0.5 if two(out, a) else 1))
+        return add(name, "V", fn, [a] + aps(s1, s2), [out], "v", cnt(out) * (0.5 if two(out, a) else 1))
 
-    def cp(out, a):
-        return add("V", lambda q, e: [q.tensor_copy(out[3], a[3])], [a], [out], "v", cnt(out) * (0.5 if two(out, a) else 1))
+    def cp(name, out, a):
+        return add(name, "V", lambda q: [q.tensor_copy(out[3], a[3])], [a], [out], "v", cnt(out) * (0.5 if two(out, a) else 1))
 
-    def aff(out, a, mul, plus, eng="VS"):
-        def fn(q, e):
-            if e == "V":
-                return [q.tensor_scalar(out[3], a[3], float(mul), float(plus), A.mult, A.add)]
-            return [q.activation(out[3], a[3], F.Identity, bias=float(plus), scale=float(mul))]
-        return add(eng, fn, [a], [out], "v", cnt(out))
+    def act(name, out, a, f, bias=0.0, scale=1.0):
+        return add(name, "S", lambda q: [q.activation(out[3], a[3], f, bias=val(bias), scale=scale)], [a] + aps(bias), [out], "v", cnt(out))
+
+    def aff(name, out, a, mul, plus):
+        if name and on(name) == "V" or SCRATCH[out[0]][2] == F16:
+            return ts(name, out, a, float(mul), float(plus), A.mult, A.add)
+        return act(name, out, a, F.Identity, float(plus), float(mul))
+
+    def step(name, out, a, thr, bias, scale):
+        return act(name, out, a, F.Sigmoid, bias, scale) if off(name) else ts(name, out, a, *thr)
 
     def ms(out, c):
-        return add("V", lambda q, e: [q.memset(out[3], c)], [], [out], "v", cnt(out) * (0.5 if two(out) else 1))
+        return add("", "V", lambda q: [q.memset(out[3], c)], [], [out], "v", cnt(out) * (0.5 if two(out) else 1))
 
-    def scan(out, d0, d1, init, op0, op1):
-        return add("V", lambda q, e: [q.tensor_tensor_scan(out[3], d0[3], d1[3], init, op0, op1)], [d0, d1], [out], "v",
+    def scan(name, out, d0, d1, init, op0, op1):
+        return add(name, "V", lambda q: [q.tensor_tensor_scan(out[3], d0[3], d1[3], init, op0, op1)], [d0, d1], [out], "v",
                    cnt(out) * (0.5 if two(out, d0, d1) else 1))
 
-    def vt(out, a):
-        return add("V", lambda q, e: [q.transpose(out[3], a[3])], [a], [out], "v", cnt(out) * (0.5 if two(out, a) else 1))
+    def vt(name, out, a):
+        return add(name, "V", lambda q: [q.transpose(out[3], a[3])], [a], [out], "v", cnt(out) * (0.5 if two(out, a) else 1))
 
-    def gat(out, win, off, eng):
-        def fn(q, e):
-            if e == "V":
-                return [q.tensor_copy(out[3], ind(win, off))]
-            return [q.activation(out[3], ind(win, off), F.Copy)]
-        return add(eng, fn, [win, off], [out], "g", cnt(out))
+    def gat(name, out, win, o, eng=None):
+        eng = eng or on(name)
 
-    def gtt(out, win, off, b, op):
-        return add("V", lambda q, e: [q.tensor_tensor(out[3], ind(win, off), b[3], op)], [win, off, b], [out], "g", cnt(out))
+        def fn(q):
+            if eng == "V":
+                return [q.tensor_copy(out[3], ind(win, o))]
+            return [q.activation(out[3], ind(win, o), F.Copy)]
+        return add(name, eng, fn, [win, o], [out], "g", cnt(out))
 
-    def sct(win, off, a):
-        return add("V", lambda q, e: [q.tensor_copy(ind(win, off), a[3])], [off, a], [win], "sc", cnt(a))
+    def gtt(name, out, win, o, b, op):
+        return add(name, "V", lambda q: [q.tensor_tensor(out[3], ind(win, o), b[3], op)], [win, o, b], [out], "g", cnt(out))
 
-    def mm(groups, part=None):
-        rd, n = [], 0
-        for out, terms in groups:
-            for l, r in terms:
-                rd += (l if isinstance(l, list) else [l]) + [r]
-                n += max(64, cnt(r)) * (4 if SCRATCH[r[0]][2] == "float32" else 1)
-        rd = [x for x in rd if isinstance(x, tuple)]
+    def sct(name, win, o, a):
+        return add(name, "V", lambda q: [q.tensor_copy(ind(win, o), a[3])], [o, a], [win], "sc", cnt(a))
 
-        def fn(q, e):
-            res = []
-            for k, (out, terms) in enumerate(groups):
-                for i, (l, r) in enumerate(terms):
-                    lt = l[l[0]()] if isinstance(l, list) else l
-                    st, sp = i == 0, i == len(terms) - 1
-                    if part == "open":
-                        st, sp = k == 0 and i == 0, False
-                    elif part == "begin":
-                        sp = False
-                    elif part == "more":
-                        st = sp = False
-                    elif part == "end":
-                        st = False
-                    elif part == "close":
-                        st, sp = False, k == len(groups) - 1
-                    ins = q.matmul(out[3], lt[3], r[3], st, sp)
-                res.append(ins)
-            return res
-        return add("P", fn, rd, [o for o, t in groups], "pe", n)
+    def mm(name, terms, part="whole"):
+        n = sum(max(64, cnt(r)) * (4 if SCRATCH[r[0]][2] == F32 else 1) for o, l, r in terms)
+
+        def fn(q):
+            for i, (o, l, r) in enumerate(terms):
+                ins = q.matmul(o[3], l[3], r[3], i == 0 and part in ("whole", "open"), i == len(terms) - 1 and part in ("whole", "close"))
+            return [ins]
+        return add(name, "P", fn, [x for o, l, r in terms for x in (l, r)], [o for o, l, r in terms], "pe", n, part=part)
 
     def iota(out, pattern, base, ch):
-        def fn(q, e):
-            if SCRATCH[out[0]][2] == "int32":
+        def fn(q):
+            if SCRATCH[out[0]][2] == I32:
                 return [q.iota(out[3], pattern, base, ch)]
             return [q.iota(out[3], pattern, base, ch, allow_small_or_imprecise_dtypes=True)]
-        return add("G", fn, [], [out], "io", cnt(out))
+        return add("", "G", fn, [], [out], "io", cnt(out))
+
+    def sel(out, a, pattern, op, ch):
+        return add("", "G", lambda q: [q.affine_select(out[3], a[3], pattern, op, 0.0, 0, ch)], [a], [out], "io", cnt(out) + 24)
 
     def dma(eng, sem, out, a, rd, wr, nbytes):
-        return add(eng, lambda q, e: [q.dma_start(out, a)], rd, wr, "dma", nbytes, sem="d" + sem)
+        return add("dma" + sem, eng, lambda q: [q.dma_start(out, a)], rd, wr, "dma", nbytes, sem="d" + sem)
 
-    dma("S", "slot", T.slot0[:], T.slot[:], [], [ap("slot0")], 4096)
-    dma("S", "trav", T.trav0[:], T.trav[:], [], [ap("trav0")], 65536)
-    if CONFIG["clk1"]:
-        first = dma("Y", "clk", T.X[:], T.clk[:], [], [ap("X")], 1048576)
-        dma("Y", "tt", T.tt32[:], T.ttab[:], [], [ap("tt32")], 1572864)["behind"] = first
-    else:
-        first = dma("Y", "tt", T.tt32[:], T.ttab[:], [], [ap("tt32")], 524288)
-        dma("Y", "clk", T.X[:], T.clk[:], [], [ap("X")], 1572864)["behind"] = first
-    dma("S", "last", T.last0[:], T.last[:], [], [ap("last0")], 1572864)
+    def slot(name, v, h, n=4):
+        return ap(name, 16 * v + 8 * h, 16 * v + 8 * h + n)
+
+    def box(name, v, h, a=0, n=1):
+        stay = v == (0 if name[0] == "l" else VISITS - 1)
+        o = 2 * L * v + (H * (1 - h) + L * a if stay else L * h + H * a)
+        return ap(name, o, o + n * H)
+
+    loads = [("slot", ap("slot0"), T.slot, 4), ("trav", ap("trav0"), T.trav, 4), ("clk", ap("X"), T.clk, 2), ("tt", ap("tt32"), T.ttab, 4),
+             ("last", ap("last0"), T.last, 2)]
+    if cfg["first"] != "X":
+        loads[2:4] = loads[3:1:-1]
+    for k, (name, to, src, size) in enumerate(loads):
+        o = dma("Y", name, to[3], src[:], [], [to], 128 * cnt(to) * size)
+        if k:
+            o["behind"] = ops[-2]
 
     def col(i):
         return ap("col", i, i + 1)
-    P, G, BA, PC, HI, TH = col(0), col(1), col(2), col(3), col(4), 5
+    P, G, PC = col(0), col(1), col(2)
+    wide = 64 if any(x[1] == "S" for x in cfg["W"]) else 32
     iota(ap("pi"), [[0, 1]], 0, 1)
-    iota(ap("i144"), [[1, 144]], 0, -1)
-    iota(ap("BT"), [[1, B]], 0, 0)
+    iota(ap("i144"), [[1, 144]], 1, -1)
     iota(ap("iog"), [[1, 8], [0, 16]], 0, 0)
-    iota(ap("iom"), [[0, 4], [1, 16]], 0, 0)
-    iota(ap("i16"), [[16, 8]], 0, 0)
-    iota(ap("id0"), [[-16, 4], [1, 64]], 0, 0)
-    iota(ap("id1"), [[-16, 4], [1, 128]], -64, 0)
-    ts(ap("pj", 0, 1), ap("pi"), 15, None, A.bitwise_and)
-    ts(ap("pj", 1, 2), ap("pi"), 4, None, A.logical_shift_right)
-    cp(ap("col", 0, 2), ap("pj"))
-    aff(BA, P, 8 * 613, 0)
-    aff(PC, P, -1, 16)
-    ts(HI, P, 8.0, 16.0, A.is_ge, A.mult)
-    ms(col(TH), 56.0)
-    aff(col(TH + 1), HI, 1, 40)
-    aff(col(TH + 2), HI, -1, 56)
-    ms(col(TH + 3), 40.0)
-    ts(ap("S1"), ap("i144"), P, 15.0, A.add, A.is_equal)
-    aff(ap("S2"), ap("S1"), 2, 0)
-    aff(ap("S16"), ap("S1"), 16, 0)
-    ts(ap("I1"), ap("i144", 0, 128), 0.0, None, A.is_equal)
-    aff(ap("In"), ap("I1"), -1, 0)
-    aff(ap("I32"), ap("I1"), 32, 0)
-    ts(ap("BOf"), ap("iog"), G, None, A.is_equal)
-    cp(ap("BOh"), ap("BOf"))
-    iota(ap("DF", 0, B - 97), [[1, B - 97]], 97, 0)
-    iota(ap("DF", B - 97, B), [[1, 97]], 0, 0)
-    aff(ap("BOm"), ap("BOf"), -2, 0)
-    ts(ap("MK"), ap("iom"), P, 16384.0, A.not_equal, A.mult)
-    ts(ap("PC"), ap("iom"), 0.0, PC, A.mult, A.add)
-    ms(ap("ones"), 1.0)
-    ms(ap("RS"), 0.0)
-    ms(ap("RS", 0, 512, 16), 65536.0)
-    ms(ap("RM"), 1.0)
-    ms(ap("RM", 0, 512, 16), 0.0)
+    iota(ap("iom"), [[0, 8], [1, 16]], 0, 0)
+    iota(ap("BT", 0, L), [[1, L]], 0, 0)
+    for w in (L, 2 * L, 4 * L):
+        aff("", ap("BT", w, 2 * w), ap("BT", 0, w), 1, w)
+    aff("", ap("DF", 0, B - 97), ap("BT", 0, B - 97), 1, 97)
+    aff("", ap("DF", B - 97, B), ap("BT", 0, 97), 1, 0)
+    for h in range(2):
+        aff("", ap("i32", H * h, H * h + H), ap("BT", 0, H), 32, 32 * H * (1 - h))
+    iota(ap("of", 0, 8), [[8, 2], [1, 4]], 0, 0)
+    iota(ap("of", 8, 16), [[8, 2], [2, 2], [-4, 2]], 4, 0)
+    iota(ap("of", 16, 20), [[16, 4]], 15, 0)
+    for name, rest, first in (("RS", 0.0, 4096.0), ("RM", 4096.0, 0.0)):
+        ms(ap(name, 0, 16 * wide), rest)
+        ms(ap(name, 0, 16 * wide, 16), first)
+    ms(ap("RD"), 8192.0)
+    ms(ap("RD", L, 2 * L, 16), 0.0)
+    iota(ap("RD", 0, L, 16), [[-16, 8]], SP - 1, -1)
+    ts("", ap("pj", 0, 1), ap("pi"), 15, None, A.bitwise_and)
+    ts("", ap("pj", 1, 2), ap("pi"), 4, None, A.logical_shift_right)
+    cp("", ap("col", 0, 2), ap("pj"))
+    ts("", PC, P, -1.0, 16.0, A.mult, A.add)
+    ts("", ap("cb"), P, 2452.0, -0.25, A.mult, A.add)
+    ts("", ap("hi"), P, 8.0, None, A.is_ge)
+    bound = {"V": 65536.0 + 32 * 12, "S": 65536.0 + 16 * 8}
+    for x, y in ("VS", "SV"):
+        ts("", ap("t" + x), ap("hi"), bound[y] - bound[x], bound[x], A.mult, A.add)
+        ts("", ap("u" + x), ap("t" + x), -8.0, 128.0, A.mult, A.add)
+    if cfg["S"] or cfg["rel"] == "S":
+        act("", ap("ones"), ap("iom"), F.Sigmoid, 128.0)["n"] += 1500
+    else:
+        act("", ap("ones"), ap("iom"), F.Identity, 1.0, 0.0)
+    act("", ap("CB"), ap("iom", 0, H), F.Identity, ap("cb"), 0.0)
+    cp("", ap("CH"), ap("CB"))
+    tt("", ap("CL"), ap("CB"), ap("CH"), A.subtract)
+    act("", ap("PC"), ap("iom", 0, H), F.Identity, PC, 0.0)
+    iota(ap("L32"), [[-32 * H, 2], [512, 4]], 32 * H, 0)
+    ts("", ap("p32"), P, 32.0, None, A.mult)
+    ts("", ap("L32"), ap("L32"), ap("p32"), None, A.add)
+    ts("", ap("S16"), ap("i144"), PC, 16.0, A.is_equal, A.mult)
+    for name, w in (("S32", 2), ("S512", 32)):
+        aff("", ap(name), ap("S16"), w, 0)
+    ts("", ap("I1"), ap("i144", 0, 128), 1.0, None, A.is_equal)
+    for name, w in (("If", 1), ("Ig", -1), ("Ihf", 0.5), ("Ifb", 148), ("Jb", 148), ("J1", 1), ("In", -1), ("Ik", 65536), ("Ih", 0.5)):
+        aff("", ap(name), ap("I1"), w, 0)
+    for name, w in (("kC", 1.5 * 2 ** 28), ("kD", 1.5 * 2 ** 23), ("kh", 15.5), ("kv", 4736.0), ("mh", -0.5), ("par", 256.0), ("sb", 65535)):
+        ms(ap(name), w)
+    ms(ap("pb7", 4 * H, 4 * H + 1), 256.0)
+    ts("", ap("BOp"), ap("iog"), G, None, A.is_equal)
+    for name, w in (("BOh", 1), ("BOn", -4096), ("BOq", -1)):
+        aff("", ap(name), ap("BOp"), w, 0)
+    sel(ap("TRn"), ap("BOn"), [[1, L]], A.is_gt, -1)
+    ts("", ap("MK"), ap("iom"), P, 16384.0, A.not_equal, A.mult)
+    aff("", ap("CM"), ap("MK"), -1, SP)
+    cp("", ap("OF"), ap("of"))
     ms(ap("RK"), 1048576.0)
     ms(ap("RK", 0, H, 16), 65536.0)
-    aff(ap("Ik"), ap("I1"), 65536, 0)
-    aff(ap("If"), ap("I1"), 1, 0)
-    if CONFIG["dh"] or CONFIG["rel"]:
-        aff(ap("Ig"), ap("I1"), -1, 0)
-    if CONFIG["xs"]:
-        aff(ap("Ih"), ap("I1"), 0.5, 0)
-        aff(ap("mh"), ap("I1"), 0, -0.5)
-    ts(ap("L32"), ap("i16"), P, 32.0, A.add, A.mult)
-    aff(ap("DS"), ap("L32"), 2.0 ** -18, 0.125)
-    ts(ap("OB"), ap("i16", 0, 4), 15.0, None, A.add)
+    cp("", ap("lT", 0, L), ap("trav0"))
+    aff("", ap("lT", L, 2 * L), ap("last0"), 1, 0.5 * (cfg["mh"] and not cfg.get("u16")))
+    ms(ap("lb", 0, 16), 65535)
     for h in range(2):
-        d, w = "D%d" % h, H * (h + 1)
-        ts(ap(d), ap("id%d" % h), P, 8191.0, A.is_equal, A.mult)
-        ts(ap(d), ap(d), 1.0, None, A.add)
-        ms(ap(d, 0, 4 * w, w), 0.0)
-    ms(ap("par"), 1.0)
-    for h in range(2):
-        r = "land0_%d" % h
-        cp(ap(r, 0, H), ap("trav0", H * h, H * h + H))
-        cp(slot("lb", 0, h), ap("slot0", 4 * h, 4 * h + 4))
-        aff(ap(r, H, RW), ap("last0", H * h, H * h + H), 2, 1)
-    for q in range(4):
-        cp(ap("TT", 256 * q, 256 * q + 256), ap("tt32", 256 * q, 256 * q + 256))
-
-    X, TT = ap("X"), ap("TT", 0, B)
+        cp("", slot("lb", 0, h), ap("slot0", 4 - 4 * h, 8 - 4 * h))
+    if cfg["ttf"] == "G":
+        sel(ap("TT", SP), ap("tt32"), [[0, B]], A.is_ge, 0)
+    else:
+        for q in range(4):
+            cp("TTf", ap("TT", SP + 256 * q, SP + 256 * q + 256), ap("tt32", 256 * q, 256 * q + 256))
+    X, TT = ap("X"), ap("TT", SP)
 
     def smat(name, k):
         return ap(name, 15 - k, 143 - k)
 
-    for v in range(VISITS):
-        last = v == VISITS - 1
-        now["visit"] = v
+    def b(name, h, a=0, z=None, step=None):
+        w = SCRATCH["h" + name][1][1] // 2
+        return ap("h" + name, w * h + a, w * h + (w if z is None else z), step)
 
-        def b(name, h, a=0, z=None, step=None):
-            w = SCRATCH["h" + name][1][1] // 2
-            return ap("h" + name, w * h + a, w * h + (w if z is None else z), step)
+    def pieces(name, h):
+        return [(name + "%d1" % h, 0, 2)] if named("W", name + str(h)) else [(name + "%d%d" % (h, q), q, q + 1) for q in range(2)]
 
-        def land(h, *r):
-            return ap("land%d_%d" % (v, h), *r)
+    def part(name, h, a, z):
+        w = SCRATCH["h" + name][1][1] // 4
+        return b(name, h, w * a, w * z)
 
-        def snd(h, *r):
-            return ap("send%d_%d" % (v, h), *r)
+    def pb(bank, i, n=1):
+        return ap("pb%d" % bank, H * i, H * (i + n))
 
-        def pv(i):
-            return ap("pb7", H * i, H * i + H)
+    def mrow(name, h):
+        return ap(name, 1024 * h + 15, 1024 * h + 1024, 16)
 
-        def mrow(name, h):
-            return ap(name, 1024 * h + 15, 1024 * h + 1024, 16)
-
-        for h in range(2):
-            if v:
-                for k, r in enumerate((land(h), slot("lb", v, h))):
-                    add("R", None, [], [r], "arr", 0, sem="arr%d_%d_%d" % (v, h, k), after=("send", v - 1, h, k))
-            cp(b("U", h), land(h, 0, H))
-            bo = slot("lb", v, h)
-            tab = ap("tt32") if v == 0 and CONFIG["clk1"] else TT
-            gat(b("Hu", h), tab, bo, "V")
-            for q in range(2):
-                gat(b("x", h, 512 * q, 512 * q + 512), X, b("U", h, 32 * q, 32 * q + 32), "VS")
-                gtt(b("cy", h, 512 * q, 512 * q + 512), X, b("Hu", h, 32 * q, 32 * q + 32), b("x", h, 512 * q, 512 * q + 512), A.is_ge)
-            if CONFIG["dh"]:
-                gat(b("dH", h), TT, bo, "VS")
-                mm([(ap("pb%d" % (4 + h), H, 2 * H), [(ap("If"), b("dH", h)), (ap("Ig"), land(h, 0, H))])])
-            else:
-                gtt(b("dH", h), tab, bo, land(h, 0, H), A.subtract)
-            add("S", lambda q, e, o=b("A8", h), bo=bo: [q.activation(o[3], ind(ap("BT"), bo), F.Identity, bias=BA[3], scale=296.0)],
-                [ap("BT"), bo, BA], [b("A8", h)], "g", H)
-            gat(b("df", h), ap("DF"), bo, "VS")
-            cp(b("bl", h), bo)
-            gat(ap("bB", H * h, H * h + H), ap("BT"), bo, "V")
-        for h in range(2):
-            c1 = ap("pb%d" % (4 + h), 3 * H, 4 * H)
-            mm([(c1, [(smat("S2", k), b("cy", h, k, 1024, 16)) for k in range(16)])])
-            if CONFIG["dh"]:
-                ts(b("tk", h), c1, ap("par"), 19.0, A.add, A.is_ge)
-                tt(pv(5), b("tk", h), ap("pb%d" % (4 + h), H, 2 * H), A.mult)
-            else:
-                ts(pv(4), c1, ap("par"), 19.0, A.add, A.is_ge)
-                tt(pv(5), pv(4), b("dH", h), A.mult)
-            tt(pv(h), pv(5), land(h, 0, H), A.add)
-            cp(b("Tu", h), pv(h))
-        for h in range(2):
-            w = H * (h + 1)
-            for c in range(4):
-                ts(ap("eq%d" % h, w * c, w * c + w), ap("bB", 0, w), b("bl", h, c, c + 1), ap("DS", 4 * h + c, 4 * h + c + 1), A.is_equal, A.mult)
-            scan(ap("es%d" % h), ap("D%d" % h), ap("eq%d" % h), 0.0, A.mult, A.max)
-            tt(b("of", h), ap("es%d" % h, w - 1, 4 * w, w), b("bl", h), A.max)
-            cp(b("ou", h), b("of", h))
-        for h in range(2):
-            for q in range(2):
-                z = b("z", h, 512 * q, 512 * q + 512)
-                gat(z, X, b("Tu", h, 32 * q, 32 * q + 32), "VS")
-                o = 1024 * h + 512 * q
-                scan(ap("mS", o, o + 512), ap("RS"), z, 0.0, A.max, A.min)
-                scan(ap("MS", o, o + 512), ap("RM"), z, 0.0, A.mult, A.max)
-            m2 = snd(h, H, RW)
-            aff(m2, mrow("mS", h), 2, 1)
-            tt(pv(6 + h), pv(h), m2, A.mult)
-            tt(b("s", h), pv(6 + h), b("A8", h), A.add)
-            ts(b("n", h), b("s", h), 3, W - 1, A.logical_shift_right, A.bitwise_and)
-            cp(b("nu", h), b("n", h))
-            ts(b("nm", h), b("s", h), 3, B - 1, A.logical_shift_right, A.bitwise_and)
-            tt(pv(6 + h), b("nm", h), b("df", h), A.subtract)
-            if CONFIG["rel"]:
-                d, o = ap("pb%d" % (4 + h), 7 * H, 8 * H), b("rel", h)
-                mm([(d, [(ap("If"), m2), (ap("Ig"), land(h, H, RW))])])
-                add("S", lambda qq, e, d=d, o=o: [qq.activation(o[3], d[3], F.Sign)], [d], [o], "v", H)
-            else:
-                tt(b("rel", h), m2, land(h, H, RW), A.is_gt)
-            tt(pv(2 + h), b("n", h), pv(h), A.subtract)
-            if last:
-                aff(ap("yl", H * h, H * h + H), mrow("mS", h), 1, 0)
-        mm([(ap("pb5", 6 * H, 6 * H + 8), [(smat("S1", a), ap("MS", 16 * a + 15, 16 * L, 256)) for a in range(16)])])
-        cp(ap("ui"), ap("pb5", 6 * H, 6 * H + 8))
-        ts(ap("uj"), ap("ui"), 31, None, A.bitwise_and)
-        tt(ap("uk"), ap("uj"), ap("L32"), A.add)
-        cp(ap("ju"), ap("uk"))
-        if CONFIG["xs"]:
-            gat(ap("xo"), X, ap("ju"), "VS")
-            mm([(ap("pb5", 4 * H, 6 * H), [(ap("Ih"), ap("xo")), (ap("Ih"), ap("MS", 15, 16 * L, 16)), (ap("Ih"), ap("mh"))])])
-            cp(ap("xt"), ap("pb5", 4 * H, 6 * H))
+    def update(v, last, byM, up, M, xt, ju):
+        mm("u", [(up, ap(l), r) for l, r in [("I1", ap("kh")), ("BOq", M), ("I1", ap("kC")), ("In", ap("kC")), ("I1", ap("i32"))] * byM +
+                 [("BOp", M), ("In", ap("MK"))]])
+        if cfg["join"]:
+            scan("es", ap("es"), ap("RD"), pb(6, 4, 4), 65536.0, A.min, A.max)
+            cp("ou", ap("ou", 0, 8 + 8 * byM), ap("es", 15, L + L * byM, 16))
         else:
-            gtt(ap("xs"), X, ap("ju"), ap("MS", 15, 16 * L, 16), A.add)
-            ts(ap("xt"), ap("xs"), 1, None, A.logical_shift_right)
+            scan("us", ap("es", L), ap("RD", L), up, 65536.0, A.min, A.max)
+            if byM:
+                cp("ju", ju, ap("es", L + 15, 2 * L, 16))
+        if not byM:
+            cp("ui", ap("ui"), ap("es", L + 15, 2 * L, 16))
+            ts("uj", ap("uj"), ap("ui"), 31, None, A.bitwise_and)
+            tt("uk", ap("uk"), ap("uj"), ap("L32"), A.add)
+            cp("ju", ju, ap("uk"))
+        if cfg["xs"] != "V":
+            gat("xo", ap("xo"), X, ju, "S")
+            mm("xp", [(up, ap("Ih"), r) for r in (ap("xo"), M, ap("mh"))] + [(up, ap(l), ap("kD")) for l in ("I1", "In")])
+            xt = ap("xb")
+            act("xt", xt, up, F.Copy)
+        else:
+            gtt("xs", ap("xs"), X, ju, M, A.add)
+            ts("xt", xt, ap("xs"), 1, None, A.logical_shift_right)
         if last:
-            dma("Y", "cp", T.X2[:], T.X[:], [X, land(1, 0, H)], [ap("X2")], 1048576)
-            sct(ap("X2"), ap("ju"), ap("xt"))
+            dma("Y", "cp", T.X2[:], T.X[:], [X, slot("lb", v, 1)], [ap("X2")], 1048576)
+            sct("Xsc", ap("X2"), ju, xt)
             dma("Y", "yclk", T.yclk[:], T.X2[:], [ap("X2")], [], 1048576)
             dma("Y", "yla", T.ylast[:], T.yl[:], [ap("yl")], [], 32768)
+
+    for v in range(VISITS):
+        last = v == VISITS - 1
+        split = last and cfg.get("split")
+        now["v"] = v
+        bname = "bF" if off("bB") else "bB"
+        byP, mh, u16 = cfg["tadd"] == "P", cfg["mh"], cfg.get("u16")
+
+        def post(k, h, src, dst):
+            add("send%s%d" % (k, h), "G", lambda q, sem="arr%d_%d_%s" % (v + 1, h, k): [send(dst[3], src[3], sem)], [src], [], "send",
+                128 * cnt(src) * (4 if src[0] == "sT" else 2), tag=("send", v, h, k), sem="sent")
+
+        def dfb(h):
+            return b("dg" if on("df%d" % h) == "V" else "df", h)
+
+        def one(x):
+            return ap("J1" if SCRATCH[x[0]][2] == F16 else "If")
+
         for h in range(2):
-            for q in range(2):
-                gat(b("e", h, 512 * q, 512 * q + 512), X, b("nu", h, 32 * q, 32 * q + 32), "VS")
-            cmps = []
-            for q in range(2):
-                for bank, name in ((q, "mS"), (2 + q, "MS")):
-                    if CONFIG["pre"]:
-                        mm([(ap("pb%d" % bank, H * j, H * j + H), [(ap("In"), mrow(name, h))]) for j in range(8)], "open")
-                        mm([(ap("pb%d" % bank, H * j, H * j + H), [(ap("I1"), b("e", h, 8 * q + j, 1024, 16))]) for j in range(8)], "close")
-                    else:
-                        mm([(ap("pb%d" % bank, H * j, H * j + H), [(ap("I1"), b("e", h, 8 * q + j, 1024, 16)), (ap("In"), mrow(name, h))])
-                            for j in range(8)])
-                d, o = ap("pb%d" % q), b("cm", h, 512 * q, 512 * q + 512)
-
-                def fn(qq, e, d=d, o=o):
-                    if e == "V":
-                        return [qq.tensor_scalar(o[3], d[3], 0.0, None, A.is_ge)]
-                    return [qq.activation(o[3], d[3], F.Sign, bias=0.5, scale=1.0)]
-                cmps.append(add("VS", fn, [d], [o], "v", 512))
-                d, o = ap("pb%d" % (2 + q)), b("ab", h, 512 * q, 512 * q + 512)
-                add("S", lambda qq, e, d=d, o=o: [qq.activation(o[3], d[3], F.Abs)], [d], [o], "v", 512)
-            c2, zz = ap("pb%d" % (4 + h), 0, H), ap("pb6", H * h, H * h + H)
-            for q in range(2):
-                mm([(c2, [(ap("I32"), b("rel", h))] * (1 - q) +
-                     [([lambda c=cmps[q]: 1 if c["on"] == "V" else 2, smat("S2", p), smat("S1", p)], b("cm", h, H * p, H * p + H))
-                      for p in range(8 * q, 8 * q + 8)])], "end" if q else "begin")
-            rdy = b("rdy", h)
-            add("V", lambda q, e, c2=c2, rdy=rdy, cs=cmps: [q.tensor_scalar(
-                rdy[3], c2[3], col(TH + (cs[0]["on"] == "S") + 2 * (cs[1]["on"] == "S"))[3], None, A.is_ge)],
-                [c2, ap("col", TH, TH + 4)], [rdy], "v", H)
-            tt(b("td", h), rdy, pv(2 + h), A.mult)
-            tt(snd(h, 0, H), b("td", h), pv(h), A.add)
-            sct(ap("TT"), b("ou", h), snd(h, 0, H))
-            nb = ap("pb%d" % (4 + h), 2 * H, 3 * H)
-            mm([(nb, [(ap("If"), b("df", h)), (ap("I1"), ap("MK"))])], "begin")
-            for q in range(2):
-                mm([(zz, [(ap("I1"), ap("PC"))] * (1 - q) + [(smat("S16", p), b("ab", h, H * p, H * p + H)) for p in range(8 * q, 8 * q + 8)])],
-                   "more" if q else "begin")
-            mm([(zz, [(ap("Ik"), rdy)])], "close")
-            vt(b("kT", h), zz)
-            scan(b("kr", h), ap("RK"), b("kT", h), 65536.0, A.min, A.max)
-            gtt(b("qT", h), b("kr", h), ap("OB"), b("kT", h), A.is_equal)
-            vt(b("oh", h), b("qT", h))
-            tt(b("sel", h), b("oh", h), pv(6 + h), A.mult)
-            sg = ap("pb4", 4 * H + H * h, 5 * H + H * h)
-            mm([(nb, [(ap("BOh"), b("sel", h))])], "end")
-            scan(b("ex", h), ap("RS", 0, H), nb, 0.0, A.max, A.min)
-            if not last:
-                cp(slot("sb", v, h), b("ex", h, 15, H, 16))
-                for k, (src, dst) in enumerate(((snd(h), "land%d_%d" % (v + 1, h)), (slot("sb", v, h), "lb"))):
-                    dst = ap(dst) if k == 0 else slot("lb", v + 1, h)
-                    add("G", lambda q, e, s=src, d=dst, sem="arr%d_%d_%d" % (v + 1, h, k): [send(d[3], s[3], sem)], [src], [], "send", 0,
-                        tag=("send", v, h, k), sem="sent")
-                mm([(sg, [(ap("BOm"), b("oh", h)), (ap("I1"), ap("ones"))])])
+            s = str(h)
+            Tl, Cl, bo = box("lT", v, h), box("lT", v, h, 1), slot("lb", v, h)
+            Tp, Fp, Bp, Cp = (pb(4 + h, i) for i in range(4))
+            if v:
+                land = "lU" if u16 else "lT"
+                apart = [("T", box(land, v, h)), ("c", box(land, v, h, 1))] if named("C", s) else [("T", box(land, v, h, 0, 2))]
+                for k, r in apart + [("b", slot("lb", v, h, 8))]:
+                    add("arr", "R", None, [], [r], "arr", 0, sem="arr%d_%d_%s" % (v, h, k), after=("send", v - 1, h, k))
+            if u16 and v:
+                U = box("lU", v, h)
+                cp("U" + s, box("lT", v, h, 0, 2), box("lU", v, h, 0, 2))
             else:
-                aff(b("bl", h), b("ex", h, 15, H, 16), 1, 0)
-                dma("Y", "ytr%d" % h, T.ytrav[:, H * h:H * h + H], snd(h, 0, H)[3], [snd(h, 0, H)], [], 32768)
-                dma("Y", "ysl%d" % h, T.yslot[:, 4 * h:4 * h + 4], b("bl", h)[3], [b("bl", h)], [], 2048)
-        if not last:
-            sct(X, ap("ju"), ap("xt"))
-            sg = ap("pb4", 4 * H, 6 * H)
-            add("V", lambda q, e, sg=sg: [q.tensor_reduce(T.par[:], sg[3], AxisListType.X, A.mult)], [sg], [ap("par")], "v", L)
+                U = b("U", h)
+                cp("U" + s, U, Tl if v else ap("trav0", H - H * h, L - H * h))
+            tab = TT if v else ap("tt32")
+            gat("Hu" + s, b("Hu", h), tab, bo, "V")
+            for name, a, z in pieces("x", h):
+                gat(name, part("x", h, a, z), X, ap(U[0], U[1] + 32 * a, U[1] + 32 * z))
+            for name, a, z in pieces("cy", h):
+                gtt(name, part("cy", h, a, z), X, part("Hu", h, a, z), part("x", h, a, z), A.is_ge)
+            bB = ap(bname, H * h, H * h + H)
+            gat("bB" + s, bB, ap("BT"), bo, "S" if off("bB") else "V")
+            gat("df" + s, dfb(h), ap("DF"), bo)
+            if byP:
+                mm("Tpre" + s, [(Tp, ap("If"), Tl)], "open")
+            c1, Dp, td = pb(6, h), pb(6, 2 + h), b("td", h) if byP else pb(4 + h, 4)
+            mm("vote" + s, [(c1, ap("In"), ap("kv"))] * off("tk" + s) + [(c1, smat("S512", k), b("cy", h, k, 1024, 16)) for k in range(16)])
+            thr = (ap("par"), 4800.0, A.add, A.is_ge)
+            if cfg["dh"] == "V":
+                gtt("dH" + s, b("dH", h), tab, bo, Tl, A.subtract)
+                Dp = b("tk", h) if off("tk" + s) else Dp
+                step("tk" + s, Dp, c1, thr, ap("par"), 1.0)
+                tt("td" + s, td, Dp, b("dH", h), A.mult)
+            else:
+                gat("dH" + s, b("dH", h), tab, bo, "S" if v else "V")
+                mm("Tdh" + s, [(Dp, ap("If"), b("dH", h)), (Dp, ap("Ig"), Tl)])
+                step("tk" + s, b("tk", h), c1, thr, ap("par"), 1.0)
+                tt("td" + s, td, b("tk", h), Dp, A.mult)
+            if byP:
+                mm("Tadd" + s, [(Tp, ap("If"), td)], "close")
+                cp("Tu" + s, b("Tu", h), Tp)
+                terms = [(Bp, ap("Ihf"), Tl), (Bp, ap("Ihf"), td)]
+            elif mh:
+                tt("Tadd" + s, Tp, td, Tl, A.add)
+                cp("Tu" + s, b("Tu", h), Tp)
+            else:
+                tt("Tadd" + s, b("td", h), td, Tl, A.add)
+                cp("Tu" + s, b("Tu", h), b("td", h))
+                terms = [(Tp, ap("If"), b("td", h)), (Bp, ap("Ihf"), b("td", h))]
+            if mh:
+                add("A8" + s, "S", lambda q, o=b("A8", h), bo=bo: [q.activation(o[3], ind(ap("BT"), bo), F.Identity, bias=T.cb[:], scale=148.0)],
+                    [ap("BT"), bo, ap("cb")], [b("A8", h)], "g", H)
+                terms = []
+            else:
+                terms += [(Bp, ap("J1"), ap("CH")), (Bp, ap("J1"), ap("CL")), (Bp, ap("Ifb" if off("bB") else "Jb"), bB)]
+            terms += [(Cp, ap("If"), Cl)] * (cfg["rel"] == "V") + [(Fp, one(dfb(h)), dfb(h))] * cfg["dnm"]
+            if terms:
+                mm("Badd" + s, terms)
+        cp("bl", ap("bl"), slot("lb", v, 0, 16))
+        dp, up = pb(6, 4, 2), pb(6, 6, 2)
+        terms = [(dp, one(ap(bname)), ap(bname)), (dp, ap("I1"), ap("CM"))]
+        h64 = cfg.get("h64")
+        for c in range(8 * bool(h64)):
+            a, z, e = 16 * c, H * (c // 4 + 1), H * c
+            ts("eq%d" % c, ap("eq", e, e + z - a), ap(bname, a, z), ap("bl", c + c // 4 * 4, c + c // 4 * 4 + 1), None, A.is_equal)
+            terms.append((ap("pb6", 4 * H + a, 4 * H + a + 16), ap("TRn"), ap("eq", e, e + 16)))
+            if a + 16 < z:
+                terms.append((ap("pb6", 4 * H + a + 16, 4 * H + z), ap("BOn"), ap("eq", e + 16, e + z - a)))
+        for c, name in enumerate(() if h64 else ("TRn", "BOn")):
+            gtt("eq%d" % c, ap("eq", L * c, L * c + L), ap("bl"), ap("OF", 8 * c, 8 * c + 8), ap(bname), A.is_equal)
+            terms.append((dp, ap(name), ap("eq", L * c, L * c + L)))
+        mm("dup", terms)
+        if not cfg["join"] or split:
+            scan("es", ap("es", 0, L), ap("RD", 0, L), dp, 65536.0, A.min, A.max)
+            cp("ou", ap("ou", 0, 8), ap("es", 15, L, 16))
+        for h in range(2):
+            s = str(h)
+            Tp, Fp, Bp, Cp, dn, dm = (pb(4 + h, i) for i in range(6))
+            for name, a, z in pieces("z", h):
+                gat(name, part("z", h, a, z), X, part("Tu", h, a, z))
+            for m, r, op0, op1 in (("mS", "RS", A.max, A.min), ("MS", "RM", A.min, A.max)):
+                for name, a, z in pieces(m, h):
+                    scan(name, ap(m, 1024 * h + 512 * a, 1024 * h + 512 * z), ap(r, 0, 512 * (z - a)), part("z", h, a, z), 0.0, op0, op1)
+            mc = box("sT", v, h, 1)
+            if u16 and not last:
+                cp("mC" + s, box("sU", v, h, 1), mrow("mS", h))
+            if u16 and mh:
+                ts("mh" + s, mc, mrow("mS", h), 0.5, None, A.add)
+            elif not u16 and (mh or not last):
+                aff("mC" + s, mc, mrow("mS", h), 1, 0.5 * mh)
+            if last:
+                aff("yl" + s, ap("yl", H - H * h, L - H * h), mrow("mS", h), 1, 0)
+            if mh:
+                tt("q" + s, Bp, Tp, mc, A.mult)
+                tt("s" + s, b("s", h), Bp, b("A8", h), A.add)
+            else:
+                mc = mrow("mS", h)
+                tt("q" + s, b("q", h), Tp, mc, A.mult)
+                tt("s" + s, b("s", h), b("q", h), Bp, A.add)
+            if cfg["acc"]:
+                tt("D" + s, b("D", h), mrow("mS", h), mrow("MS", h), A.subtract)
+            n, nm = b("n", h, 0, H), b("n", h, H)
+            ts("n" + s, n, b("s", h), 2, W - 1, A.logical_shift_right, A.bitwise_and)
+            cp("nu" + s, b("nu", h), n)
+            ts("nm" + s, nm, b("s", h), 2, B - 1, A.logical_shift_right, A.bitwise_and)
+            if cfg["dnm"]:
+                tt("dn" + s, pb(4 + h, 4, 2), b("n", h), pb(4 + h, 0, 2), A.subtract)
+            else:
+                tt("dm" + s, dm, nm, dfb(h), A.subtract)
+                tt("dn" + s, dn, n, Tp, A.subtract)
+            if cfg["rel"] == "S":
+                mm("relp" + s, [(Cp, ap("Ig"), box("lT", v, h, 1)), (Cp, ap("I1"), mrow("mS", h))])
+                act("rel" + s, b("rel", h), Cp, F.Sigmoid, -128.0, 256.0)
+            else:
+                tt("rel" + s, b("rel", h), mrow("mS", h) if u16 else mc, Cp if cfg["rel"] == "V" else box("lT", v, h, 1), A.is_gt)
+        M, xt, ju = ap("MS", 15, 16 * L, 16), ap("xt"), ap("ou", 8, 16)
+        byM = cfg["u"] == "M"
+        if split:
+            for h in range(2):
+                s, M, up, a = str(h), mrow("MS", h), pb(6, 6 + h), W // 2 * (1 - h)
+                dma("Y", "cp" + s, T.X2[:, a:a + W // 2], T.X[:, a:a + W // 2], [X, slot("lb", v, 1)], [ap("X2", a, a + W // 2)], 524288)
+                ju, us, xs, xt = ap("ou", 8 + 4 * h, 12 + 4 * h), ap("es", L + H * h, L + H * h + H), ap("xs", H * h, H * h + H), ap("xt", H * h, H * h + H)
+                mm("u" + s, [(up, ap(l), r) for l, r in (("I1", ap("kh", 0, H)), ("BOq", M), ("I1", ap("kC", 0, H)), ("In", ap("kC", 0, H)),
+                                                         ("I1", ap("i32", H)), ("BOp", M), ("In", ap("MK", 0, H)))])
+                scan("us" + s, us, ap("RD", L, L + H), up, 65536.0, A.min, A.max)
+                cp("ju" + s, ju, ap("es", us[1] + 15, us[2], 16))
+                gtt("xs" + s, xs, ap("X", a, a + W // 2), ju, M, A.add)
+                ts("xt" + s, xt, xs, 1, None, A.logical_shift_right)
+                sct("Xsc" + s, ap("X2", a, a + W // 2), ju, xt)
+                dma("Y", "yc" + s, T.yclk[:, a:a + W // 2], T.X2[:, a:a + W // 2], [ap("X2", a, a + W // 2)], [], 524288)
+            dma("Y", "yla", T.ylast[:], T.yl[:], [ap("yl")], [], 32768)
         else:
+            update(v, last, byM, up, M, xt, ju)
+        xt = ap("xt" if cfg["xs"] == "V" else "xb")
+        for h in range(2):
+            s = str(h)
+            Tp, dn, dm, c2, nb, zz = pb(4 + h, 0), pb(4 + h, 4), pb(4 + h, 5), pb(4 + h, 6), pb(4 + h, 7), pb(7, h)
+            for name, a, z in pieces("e", h):
+                gat(name, part("e", h, a, z), X, part("nu", h, a, z))
+            eng = [on("cm%d%d" % (h, q)) for q in range(2)]
+            for name in ("mS", "MS"):
+                for q in range(2):
+                    bank = q + 2 * (h if cfg["own"] or cfg["acc"] else name == "MS")
+                    d = ap("pb%d" % bank)
+                    if cfg["acc"] and name == "MS":
+                        mm("dif%s%d%d" % (name, h, q), [(pb(bank, j), ap("I1"), b("D", h)) for j in range(8)], "close")
+                    else:
+                        mm("pre%s%d%d" % (name, h, q), [(pb(bank, j), ap("In"), mrow(name, h)) for j in range(8)], "open")
+                        mm("dif%s%d%d" % (name, h, q), [(pb(bank, j), ap("I1"), b("e", h, 8 * q + j, 1024, 16)) for j in range(8)], "close")
+                    if name == "MS":
+                        act("ab%d%d" % (h, q), part("ab", h, q, q + 1), d, F.Abs)
+                    elif eng[q] == "V":
+                        ts("cm%d%d" % (h, q), part("cm", h, q, q + 1), d, 0.0, None, A.is_ge)
+                    else:
+                        act("cm%d%d" % (h, q), part("cm", h, q, q + 1), d, F.Sign, 0.5)
+            mm("crel" + s, [(c2, ap("Ik"), b("rel", h))], "open")
+            for q in range(2):
+                mm("cnt%d%d" % (h, q), [(c2, smat("S32" if eng[q] == "V" else "S16", p), b("cm", h, H * p, H * p + H))
+                                        for p in range(8 * q, 8 * q + 8)], "close" if q else "mid")
+            rdy, same = b("rdy", h), eng[0] == eng[1]
+            step("rdy" + s, rdy, c2, (bound[eng[0]] if same else ap("t" + eng[0]), None, A.is_ge),
+                 128 - 8 * bound[eng[0]] if same else ap("u" + eng[0]), 8.0)
+            tt("te" + s, b("te", h), rdy, dn, A.mult)
+            if off("Tf" + s):
+                Fp = pb(4 + h, 2)
+                mm("Tfp" + s, [(Fp, ap("If"), r) for r in [box("lT", v, h)] * byP + [b("td", h), b("te", h)]])
+                act("Tf" + s, box("sT", v, h), Fp, F.Copy)
+            else:
+                tt("Tf" + s, box("sT", v, h), b("te", h), Tp, A.add)
+            if u16 and not last:
+                cp("Uo" + s, box("sU", v, h), box("sT", v, h))
+            if h64:
+                sct("Tsc%d1" % h, ap("TT"), ap("ou", 4 * h, 4 * h + 4), box("sT", v, h))
+            for j in () if h64 else (1, 0):
+                o = box("sT", v, h)[1] + 32 * j
+                sct("Tsc%d%d" % (h, j), ap("TT"), ap("ou", 4 * h + 2 * j, 4 * h + 2 * j + 2), ap("sT", o, o + 32))
+            mm("npre" + s, [(nb, one(dfb(h)), dfb(h)), (nb, ap("I1"), ap("MK", 0, H))], "open")
+            for q in range(2):
+                mm("sco%d%d" % (h, q), [(zz, ap("I1"), ap("PC"))] * (1 - q) +
+                   [(zz, smat("S16", p), b("ab", h, H * p, H * p + H)) for p in range(8 * q, 8 * q + 8)], "mid" if q else "open")
+            mm("srdy" + s, [(zz, ap("Ik"), rdy)], "close")
+            vt("kT" + s, b("kT", h), zz)
+            scan("kr" + s, b("kr", h), ap("RK"), b("kT", h), 65536.0, A.min, A.max)
+            gtt("qT" + s, b("qT", h), b("kr", h), ap("OF", 16), b("kT", h), A.is_equal)
+            vt("oh" + s, b("oh", h), b("qT", h))
+            tt("sel" + s, b("sel", h), b("oh", h), dm, A.mult)
+            mm("nsel" + s, [(nb, ap("BOh"), b("sel", h))], "close")
+            scan("ex" + s, b("ex", h), ap("RS", 0, H), nb, 0.0, A.max, A.min)
+            if not last:
+                cp("sb" + s, slot("sb", v, h), b("ex", h, 15, H, 16))
+                src, dst = ("sU", "lU") if u16 else ("sT", "lT")
+                if "%d@%d" % (h, v + 1) in cfg["C"]:
+                    post("c", h, box(src, v, h, 1), box(dst, v + 1, h, 1))
+                    post("T", h, box(src, v, h), box(dst, v + 1, h))
+                else:
+                    post("T", h, box(src, v, h, 0, 2), box(dst, v + 1, h, 0, 2))
+                post("b", h, slot("sb", v, h, 8), slot("lb", v + 1, h, 8))
+        if last:
+            for h in range(2):
+                aff("ys%d" % h, ap("ys", 4 - 4 * h, 8 - 4 * h), b("ex", h, 15, H, 16), 1, 0)
+            dma("Y", "ytr", T.ytrav[:], box("sT", v, 1, 0, 2)[3], [box("sT", v, 1, 0, 2)], [], 65536)
+            dma("S", "ysl", T.yslot[:], T.ys[:], [ap("ys")], [], 4096)
             dma("Y", "ytt", T.yttab[:], TT[3], [TT], [], 524288)
+        else:
+            sct("Xsc", X, ju, xt)
+            sg = pb(7, 2, 2)
+            mm("sg", [(sg, ap("I1"), ap("ones"))] + [(sg, ap("BOq"), ap("hoh"))] * 2)
+            sg = ap("pb7", 2 * H, 4 * H + 1)
+            add("par", "V", lambda q, sg=sg: [q.tensor_reduce(T.par[:], sg[3], AxisListType.X, A.mult)], [sg], [ap("par")], "v", L + 1)
 
-    hist, tags = {}, {}
+    used, kept = set(), []
+    for o in reversed(ops):
+        if o["name"][0] != "." or o["wr"][0][0] in used:
+            kept.append(o)
+            used.update(x[0] for x in o["rd"] + o["wr"])
+    ops = kept[::-1]
+
+    hist, tags, closed, whole = {}, {}, {}, {}
     for i, o in enumerate(ops):
         dep = set()
-        for acc, isw in [(x, False) for x in o["rd"]] + [(x, True) for x in o["wr"]]:
-            bank = SCRATCH[acc[0]][0] == "psum"
-            for j, a, bb, w in hist.get(acc[0], ()):
-                if j == i:
-                    continue
-                if (isw or w) and a < acc[2] and acc[1] < bb:
+        acc = [(x, False) for x in o["rd"]] + [(x, True) for x in o["wr"]]
+        for x, isw in acc:
+            for j, a, z, w in hist.get(x[0], ()):
+                if (isw or w) and a < x[2] and x[1] < z:
                     dep.add(j)
-                elif bank and (ops[j]["eng"] != o["eng"] or o["eng"] != "V"):
-                    dep.add(j)
-        for acc, isw in [(x, False) for x in o["rd"]] + [(x, True) for x in o["wr"]]:
-            hist.setdefault(acc[0], []).append((i, acc[1], acc[2], isw))
+        for x, isw in acc:
+            old = hist.get(x[0], [])
+            if isw and (x[2] - x[1]) == cnt(x):
+                old = [y for y in old if not (x[1] <= y[1] and y[2] <= x[2])]
+            hist[x[0]] = old + [(i, x[1], x[2], isw)]
+        o["banks"] = sorted({x[0] for x, isw in acc if SCRATCH[x[0]][0] == "psum"})
+        if o["kind"] == "pe":
+            bank = o["banks"][0]
+            if o["part"] in ("whole", "open") and bank in closed:
+                dep.add(closed[bank])
+            if o["part"] == "open":
+                dep.update(whole.pop(bank, []))
+                closed[bank] = i
+            elif o["part"] == "whole":
+                whole.setdefault(bank, []).append(i)
+            else:
+                dep.add(closed[bank])
+                closed[bank] = i
         if o["kind"] == "arr":
             dep = {tags[o["after"]]}
         if "tag" in o:
             tags[o["tag"]] = i
+        if "behind" in o:
+            dep.add(ops.index(o["behind"]))
+        dep.discard(i)
         o["dep"] = sorted(dep)
     return ops
-
-
-def cost(o, e, m):
-    k, n = o["kind"], o["n"]
-    if k == "v":
-        t = max(64, n) * m["cyc"] + m["fix"]
-    elif k == "g":
-        t = (0.05 if e == "V" else 0.065) + n * m["g"] * m["cyc"]
-    elif k == "sc":
-        t = 0.05 + n * m["sc"] * m["cyc"]
-    elif k == "pe":
-        t = n * m["pe"] + m["fix"]
-    elif k == "io":
-        t = 0.13 + 2 * n * m["cyc"]
-    elif k == "dma":
-        return 0.05, m["dma0"] + n / m["bw"]
-    elif k == "send":
-        return 0.5, 0.5
-    else:
-        return 0.0, m["rem"]
-    return t, t
-
-
-def schedule(ops, cfg, m):
-    n = len(ops)
-    rnd = [cfg["seed"] * 7919 + 1]
-
-    def rand():
-        rnd[0] = (rnd[0] * 1103515245 + 12345) % 2147483648
-        return rnd[0] / 2147483648.0
-    succ = [[] for _ in ops]
-    for i, o in enumerate(ops):
-        for j in o["dep"]:
-            succ[j].append(i)
-    prio = [0.0] * n
-    for i in range(n - 1, -1, -1):
-        prio[i] = cost(ops[i], ops[i]["eng"][-1], m)[1] + max([prio[j] + m["cross"] for j in succ[i]] + [0.0])
-    prio = [p + cfg["noise"] * rand() for p in prio]
-    left = [len(o["dep"]) for o in ops]
-    ready = [i for i in range(n) if left[i] == 0]
-    free, done, order = {}, [0.0] * n, []
-    while ready:
-        cand = []
-        for i in ready:
-            o, best = ops[i], None
-            for e in o["eng"]:
-                s = max([free.get(e, 0.0)] + [done[j] + (m["same"] if ops[j]["on"] == e else m["cross"]) for j in o["dep"]])
-                f = s + cost(o, e, m)[0] + (cfg["bias"] if e == "V" and len(o["eng"]) > 1 else 0.0)
-                if best is None or f < best[0]:
-                    best = (f, s, e)
-            cand.append((best[1], i, best[2]))
-        t0 = min(c[0] for c in cand)
-        s, i, e = max([c for c in cand if c[0] <= t0 + cfg["slack"]], key=lambda c: prio[c[1]])
-        hold, lat = cost(ops[i], e, m)
-        ops[i]["on"] = e
-        free[e], done[i] = s + hold, s + lat
-        order.append(i)
-        ready.remove(i)
-        for j in succ[i]:
-            left[j] -= 1
-            if left[j] == 0:
-                ready.append(j)
-    return order, max(done)
-
-
-ORDER = [int(x) for x in """
-42 55 5 10 38 13 0 1 4 2 3 22 14 15 16 17 8 6 48 23 29 18 20 40 31 43 46 25 24 12 34 30 47 7 19 60 56 57 26 39 21 52 66 41 53 44 27 28 75 54 59 76 101 99 86 100 11 49 87 50 98 33 9 51 108 102 77 106 107 105 103 37 36 109 84 73 32 45 70 68 104 110 35 67 71 69 58 74 81 61 79 88 62 65 72 78 89 85 111 90 91 92 80 82 112 115 113 93 116 63 118 151 119 120 157 121 122 83 94 126 95 117 96 114 150 149 159 153 152 158 160 154 97 127 64 -130 155 125 132 128 131 123 161 163 186 -133 124 129 156 134 164 135 142 165 138 162 136 166 137 167 170 181 143 168 171 144 221 172 140 145 173 184 185 174 175 176 146 177 169 192 194 188 147 141 148 178 187 179 180 139 193 189 190 -196 182 195 191 219 198 222 197 199 223 200 201 205 225 206 202 203 216 207 204 208 183 209 227 210 234 211 212 218 213 214 215 217 224 220 230 226 233 235 228 236 232 231 247 240 238 258 260 259 257 229 248 249 250 261 251 237 274 271 241 243 239 275 252 272 276 277 278 244 310 279 280 316 281 245 246 308 309 253 242 265 254 284 273 255 318 312 311 313 317 319 262 256 286 264 -289 285 290 288 266 282 314 287 291 267 320 322 345 323 -292 268 315 293 324 294 295 321 296 325 263 326 297 283 344 343 301 302 303 329 328 330 331 353 347 351 340 327 380 299 332 304 333 305 334 335 336 298 306 346 337 352 348 338 349 339 307 -355 341 354 357 350 300 381 378 356 358 364 359 382 384 360 361 365 269 375 366 363 270 367 368 369 370 342 386 393 371 377 362 372 373 374 379 376 383 389 390 394 385 387 395 391 406 392 399 388 417 419 416 418 407 408 397 409 420 410 396 400 430 398 433 431 411 402 434 403 435 436 469 437 438 475 439 440 432 401 404 412 405 467 468 413 421 424 477 414 443 471 415 444 441 -448 445 470 476 472 478 449 425 446 473 504 481 447 450 -451 442 426 479 452 423 453 482 460 474 480 483 454 455 427 484 461 422 462 485 456 488 489 490 510 506 512 487 502 503 505 463 499 491 539 492 464 486 493 465 494 495 496 466 458 497 498 511 507 508 457 -514 500 513 509 516 540 537 459 517 518 515 523 428 519 520 524 534 429 525 522 541 526 527 501 528 543 545 552 529 530 536 521 531 532 533 535 538 542 548 544 546 549 553 628 554 565 551 550 558 577 547 578 576 566 575 567 556 568 579 569 555 559 589 592 557 590 570 561 593 562 595 634 594 596 563 597 571 598 599 604 633 632 640 564 560 583 572 584 573 603 574 591 642 636 605 -608 582 602 585 610 580 635 637 641 643 638 644 646 600 609 606 586 607 611 -620 612 613 639 645 581 616 601 668 647 621 653 614 648 615 622 649 623 650 624 666 667 631 664 618 625 651 626 627 629 674 654 670 652 676 669 655 656 657 658 659 660 675 671 677 661 672 662 678 630 680 617 -663 673 679 681 619 587 665 588 682 687 683 688 684 685 698 689 686 690 700 691 692 693 694 695 696 -697 699
-""".split() if x != "30"]
-ORDER = [int(x) for x in """
-41 54 6 10 5 8 11 37 0 1 2 3 22 14 13 4 15 42 -17 39 18 23 38 16 -20 26 24 55 7 -21 65 56 59 25 85 -28 45 48 46 19 43 29 47 75 49 33 83 86 74 40 50 98 12 105 107 97 51 32 9 100 27 -44 35 58 52 104 76 99 53 72 31 67 60 69 101 30 106 102 66 34 68 70 108 71 87 109 82 103 88 77 80 78 73 89 110 90 36 91 81 79 84 57 114 111 115 112 116 117 92 150 93 118 94 119 113 120 95 121 96 152 156 148 -149 129 157 151 -126 153 158 154 127 130 124 -132 160 125 133 61 134 131 135 155 159 162 161 163 185 169 191 170 164 136 171 168 165 63 166 128 172 122 141 187 183 184 188 186 180 220 173 139 174 123 175 64 176 142 62 143 137 144 177 178 192 193 190 189 194 204 197 145 179 146 167 147 181 195 198 218 199 140 221 196 205 206 203 182 207 200 208 201 209 138 215 233 210 222 211 202 217 212 213 214 224 223 219 225 226 216 234 227 231 235 232 246 228 259 256 247 257 248 258 249 239 237 260 250 261 236 245 270 273 243 240 238 271 274 251 230 229 276 241 244 275 242 315 309 277 252 278 253 279 254 280 255 272 -307 308 317 311 310 312 316 318 288 313 314 319 -285 281 264 283 286 289 266 290 321 328 291 322 287 282 263 346 298 292 284 323 293 265 320 329 330 352 300 324 294 325 295 331 -342 301 327 332 302 333 303 334 304 262 343 350 344 345 353 347 335 336 305 299 267 337 339 379 351 306 338 348 356 349 355 340 380 363 -354 357 377 296 358 268 326 364 365 366 359 362 367 360 368 297 374 369 370 381 269 341 392 376 371 383 385 389 372 373 361 378 375 382 390 384 386 388 393 394 391 405 387 406 417 415 407 416 408 418 396 398 409 429 432 395 400 397 404 399 410 430 433 434 403 435 411 436 431 437 468 474 401 423 412 438 440 413 439 422 414 -467 402 466 447 -444 419 445 448 442 -450 424 420 451 446 452 449 470 476 471 469 477 475 473 472 478 479 453 487 480 481 443 454 482 457 483 441 459 488 489 460 484 425 461 490 421 462 491 426 463 492 485 505 511 509 486 503 502 501 498 538 493 464 494 504 510 495 506 513 -507 512 515 516 496 455 497 465 458 536 517 427 499 539 508 514 522 523 524 518 521 500 519 525 526 456 527 533 428 528 551 535 529 540 530 542 544 531 532 520 534 537 541 547 552 627 543 545 553 549 546 550 548 575 564 576 565 577 566 574 567 568 554 557 555 591 588 560 559 558 556 592 589 -594 563 569 595 570 596 562 597 578 598 561 582 571 581 572 583 573 590 593 579 633 639 632 631 604 -607 602 584 601 608 605 606 -610 599 611 609 641 635 634 637 640 642 643 636 667 645 646 612 600 620 613 647 614 648 638 603 644 580 621 649 618 652 653 654 665 666 619 622 585 623 655 615 624 617 625 656 626 657 675 669 651 673 630 628 586 668 674 670 -677 650 658 616 659 671 676 679 629 672 678 680 686 660 687 681 682 587 688 683 661 684 689 697 685 699 663 690 662 664 691 692 693 694 695 -696 698
-""".split()]
 
 
 def rank_program(g, core, T, topo):
@@ -516,31 +587,40 @@ def rank_program(g, core, T, topo):
     n_out, n_in = len(topo.engines(core, nxt)), len(topo.engines(prv, core))
 
     def send(dst, src, sem):
-        return g.remote_dma(dst, src, T.sem[sem],
-                            T.sem.sent, pid, rid, topo.mask(core, nxt))
+        return g.remote_dma(dst, src, T.sem[sem], T.sem.sent, pid, rid, topo.mask(core, nxt))
 
-    ops = build(T, send)
-    order = [abs(x) for x in ORDER]
-    for x in ORDER:
-        ops[abs(x)]["on"] = "V" if x < 0 else ops[abs(x)]["eng"][-1]
+    ops = build(T, send, CONFIG)
+    todo, order = {}, []
+    for i, o in enumerate(ops):
+        todo.setdefault(o["name"], []).append(i)
+    for name in ORDER.split():
+        i = todo[name].pop(0)
+        order += [i] + [j for j in todo["arr"] if ops[j]["dep"] == [i]]
+    assert sorted(order) == list(range(len(ops)))
     queue = {"V": g.vector, "S": g.scalar, "P": g.tensor, "G": g, "Y": g.sync}
     total = {}
     known = {e: {} for e in queue}
-    for i in order:
+    bank = {}
+    for pos, i in enumerate(order):
         o = ops[i]
-        e = o["on"]
+        e = o["eng"]
+        o["pos"] = pos
         if o["kind"] == "arr":
             o["sig"], o["seen"] = (o["sem"], n_in), {}
             total[o["sem"]] = n_in
             continue
+        dep = [j for j in o["dep"] if o.get("behind") is not ops[j]]
+        for k in o["banks"]:
+            dep += [j for e2, j in bank.get(k, {}).items() if e2 != e]
+            bank.setdefault(k, {})[e] = i
         need = {}
-        for j in o["dep"]:
-            if e == "P" and ops[j]["on"] == "P":
+        for j in dep:
+            if e == "P" and ops[j]["eng"] == "P":
                 continue
             s, c = ops[j]["sig"]
             if c > need.get(s, (0, 0))[0]:
                 need[s] = (c, j)
-        for s, (c, j) in sorted(need.items(), key=lambda x: -ops[x[1][1]]["pos"] if "pos" in ops[x[1][1]] else 0):
+        for s, (c, j) in sorted(need.items(), key=lambda x: -ops[x[1][1]]["pos"]):
             if known[e].get(s, 0) >= c:
                 continue
             queue[e].wait_ge(T.sem[s], c)
@@ -548,7 +628,7 @@ def rank_program(g, core, T, topo):
             for s2, c2 in ops[j]["seen"].items():
                 if c2 > known[e].get(s2, 0):
                     known[e][s2] = c2
-        ins = o["fn"](queue[e], e)
+        ins = o["fn"](queue[e])
         if o["kind"] == "send":
             total["sent"] = total.get("sent", 0) + n_out
             continue
@@ -556,6 +636,6 @@ def rank_program(g, core, T, topo):
         for x in ins:
             x.then_inc(T.sem[s], step)
             total[s] = total.get(s, 0) + step
-        o["sig"], o["seen"], o["pos"] = (s, total[s]), dict(known[e]), len(total) + sum(total.values())
+        o["sig"], o["seen"] = (s, total[s]), dict(known[e])
     for s, c in total.items():
         g.wait_ge(T.sem[s], c)

from concourse.mybir import AluOpType as A, AxisListType, ActivationFunctionType as F

N, STEP, VISITS = 8, 3, 4
W, B, L, H, SP = 4096, 1024, 128, 64, 256
F16, BF, F32, I32, U16 = "float16", "bfloat16", "float32", "int32", "uint16"

SCRATCH = {}
for _n, _w, _d in (
        ("X", W, BF), ("X2", W, BF), ("tt32", B, I32), ("TT", SP + B, F32), ("trav0", L, I32), ("slot0", 8, I32), ("last0", L, BF),
        ("lT", 2 * L * VISITS, F32), ("sT", 2 * L * VISITS, F32), ("lU", 2 * L * VISITS, U16), ("sU", 2 * L * VISITS, U16), ("lb", 16 * VISITS, U16), ("sb", 16 * VISITS, U16),
        ("mS", 16 * L, BF), ("MS", 16 * L, BF), ("bB", L, F16), ("bF", L, F32), ("bl", 16, F32), ("eq", 4 * L, BF),
        ("es", 2 * L, F32), ("ou", 16, U16), ("xs", L, I32), ("xt", L, I32), ("xo", L, BF), ("xb", L, BF),
        ("par", 1, F32), ("ys", 8, F32), ("yl", L, BF),
        ("pi", 1, I32), ("pj", 2, I32), ("col", 3, F32), ("BT", B, F32), ("DF", B, F32), ("of", 20, F32), ("OF", 20, U16),
        ("cb", 1, F32), ("hi", 1, F32), ("tV", 1, F32), ("tS", 1, F32), ("uV", 1, F32), ("uS", 1, F32),
        ("i144", 144, F32), ("iog", L, F32), ("iom", L, F32), ("i32", L, BF),
        ("S16", 144, BF), ("S32", 144, BF), ("S512", 144, BF),
        ("I1", L, BF), ("In", L, BF), ("Ik", L, BF), ("Ih", L, BF),
        ("If", L, F32), ("Ig", L, F32), ("Ihf", L, F32), ("Ifb", L, F32), ("J1", L, F16), ("Jb", L, F16), ("CB", H, F32), ("CH", H, F16), ("CL", H, F16),
        ("L32", 8, F32), ("p32", 1, F32), ("ui", 8, I32), ("uj", 8, I32), ("uk", 8, I32),
        ("BOh", L, F16), ("BOn", L, BF), ("BOp", L, BF), ("BOq", L, BF), ("TRn", L, BF),
        ("CM", L, BF), ("MK", L, BF), ("RD", 2 * L, F32), ("PC", H, BF), ("ones", L, BF),
        ("kC", L, BF), ("kD", L, BF), ("kh", L, BF), ("kv", H, BF), ("mh", L, BF),
        ("RS", 1024, BF), ("RM", 1024, BF), ("RK", H, F32)):
    SCRATCH[_n] = ("sbuf", [128, _w], _d)
for _n, _w, _d in (("U", H, U16), ("Hu", H, U16), ("dH", H, F32), ("tk", H, BF), ("td", H, F32),
                   ("x", 16 * H, BF), ("cy", 16 * H, BF), ("z", 16 * H, BF), ("e", 16 * H, BF), ("cm", 16 * H, BF), ("ab", 16 * H, BF),
                   ("Tu", H, U16), ("q", H, F32), ("s", H, I32), ("n", 2 * H, I32), ("nu", H, U16), ("df", H, F32), ("dg", H, F16),
                   ("rel", H, BF), ("A8", H, F32), ("D", H, BF), ("rdy", H, BF), ("te", H, F32),
                   ("kT", H, F32), ("kr", H, F32), ("qT", H, BF), ("oh", H, BF), ("sel", H, F16), ("ex", H, F32)):
    SCRATCH["h" + _n] = ("sbuf", [128, 2 * _w], _d)
for _b in range(8):
    SCRATCH["pb%d" % _b] = ("psum", [128, 512], F32)

DMAS = ["slot", "trav", "last", "tt", "clk", "cp", "yclk", "yc0", "yc1", "cp0", "cp1", "ytt", "ytr", "ysl", "yla"]
SEMAPHORES = ["cV", "cS", "cP", "cG", "sent"] + ["d" + d for d in DMAS] + \
             ["arr%d_%d_%s" % (v, h, k) for v in range(1, VISITS) for h in range(2) for k in "Tcb"]

CONFIG = {"V": set(), "S": set(), "W": set(), "tadd": "P", "dh": "S", "rel": "V", "xs": "V", "own": False, "first": "X", "dnm": False, "join": False, "ttf": "G"}
CONFIG = {'V': {'df0', 'e01', 'e10', 'mC0@0', 'x10@0'}, 'S': {'tk1', 'rdy0', 'bB'}, 'W': {'cy1@0', 'x1@0'}, 'tadd': 'P', 'dh': 'S', 'rel': 'V', 'xs': 'V', 'own': False, 'first': 'X', 'dnm': True, 'join': True, 'ttf': 'G'}
ORDER = """dmaslot dmatrav .pb70 .iog0 .DF1 dmaclk .sb0 dmatt .pi0 .lb0 .pj0 .pj1 .lb1 .col0 .BOp0 .iom0 .ones0 .par0 .of2 .of0 .kh0 .col1 .lT0 U1 .kC0 .cb0 .BOh0 .kv0 .PC0 .CB0 .i1440 .I10 .If0 .of1 .OF0 .BOn0 .S160 .J10 .Ik0 .Ihf0 .S5120 .Ig0 .BT0 Tpre0 U0 x01 .MK0 .CM0 .DF0 .RD0 .RM0 .RS0 .lb2 bl dmalast Hu0 x00 dH0 cy01 cy00 dH1 Tdh0 .In0 .i320 Tpre1 vote0 .RK0 x11 bB0 .RK1 df0 df1 tk0 td0 .TT0 Hu1 .lT1 Tadd0 Tu0 .BOq0 .Ifb0 Badd0 cy11 .TRn0 Tdh1 bB1 z00 MS00 mS00 vote1 z01 tk1 mS01 td1 q0 Tadd1 premS01 rel0 premS00 s0 Tu1 eq0 n0 z11 MS01 nu0 eq1 e00 nm0 Badd1 preMS01 z10 dup preMS00 e01 MS11 mS11 dn0 MS10 difmS00 mS10 mC0 q1 difmS01 difMS01 cm00 cm01 rel1 crel0 difMS00 u ab00 s1 cnt00 cnt01 es n1 rdy0 nm1 crel1 premS10 ou sco00 te0 nu1 premS11 Tf0 e10 xs ab01 e11 sendT0 npre0 mC1 sco01 srdy0 kT0 xt preMS10 kr0 Tsc01 qT0 oh0 Tsc00 difmS10 preMS11 cm10 difmS11 difMS10 sel0 dn1 cm11 nsel0 ex0 sb0 ab10 difMS11 cnt10 cnt11 Xsc sendb0 ab11 rdy1 te1 Tf1 sco10 sendT1 sco11 srdy1 kT1 kr1 Tsc11 npre1 qT1 oh1 Tpre0 U0 sel1 nsel1 sg Tsc10 x00 ex1 sb1 sendb1 x01 dH0 Tdh0 Hu0 cy00 cy01 U1 par bB0 df0 x11 vote0 tk0 td0 dH1 Tadd0 x10 Hu1 bl Tu0 cy11 Tdh1 z00 Tpre1 Badd0 cy10 MS00 z01 mS00 vote1 bB1 tk1 mS01 td1 df1 q0 rel0 Tadd1 premS00 s0 Tu1 eq0 nm0 premS01 n0 crel0 MS01 Badd1 nu0 mC0 z11 eq1 e00 e01 preMS00 dn0 mS11 MS11 dup preMS01 difmS00 z10 MS10 mS10 q1 cm00 difMS01 rel1 difmS01 cm01 difMS00 u es s1 cnt00 cnt01 ou ab00 premS10 n1 xs rdy0 te0 preMS10 sco00 crel1 ab01 nu1 Tf0 sendT0 e10 npre0 sco01 srdy0 kT0 Tsc01 premS11 e11 difmS10 kr0 nm1 preMS11 mC1 qT0 difmS11 xt oh0 dn1 cm10 difMS10 cm11 sel0 Tsc00 nsel0 difMS11 ex0 sb0 sendb0 Xsc ab10 cnt10 cnt11 ab11 sco10 rdy1 sco11 te1 Tf1 Tsc11 srdy1 npre1 kT1 kr1 U0 sendT1 Tpre0 qT1 oh1 sel1 nsel1 Tsc10 x00 sg ex1 sb1 sendb1 x01 Hu0 cy00 dH0 cy01 Tdh0 U1 df0 vote0 bB0 x11 par tk0 td0 x10 Hu1 Tadd0 bl Tu0 dH1 cy11 Tdh1 z00 Tpre1 Badd0 cy10 mS00 z01 MS00 vote1 df1 tk1 mS01 td1 bB1 mC0 q0 rel0 Tadd1 premS00 premS01 s0 Tu1 eq0 n0 MS01 z11 Badd1 nu0 nm0 crel0 eq1 e00 preMS01 preMS00 dup e01 MS11 mS11 dn0 z10 MS10 difmS00 cm00 mS10 q1 difMS00 difMS01 difmS01 cm01 rel1 u s1 cnt00 cnt01 es premS10 n1 crel1 ab00 ou nu1 premS11 xs preMS10 rdy0 te0 ab01 sco00 e11 mC1 xt Tf0 e10 sco01 preMS11 srdy0 npre0 sendT0 kT0 Tsc01 kr0 nm1 difmS10 cm10 difmS11 qT0 oh0 dn1 difMS10 sel0 cm11 difMS11 Tsc00 nsel0 ex0 sb0 ab10 cnt10 cnt11 sco10 ab11 sco11 rdy1 te1 Tf1 srdy1 Xsc kT1 kr1 Tsc11 sendb0 npre1 qT1 sendT1 Tpre0 U0 oh1 sel1 x01 Tsc10 nsel1 ex1 sb1 sendb1 x00 dH0 sg Hu0 cy01 cy00 bB0 Tdh0 vote0 U1 par df0 tk0 td0 x11 dH1 x10 Hu1 bl Tadd0 Tu0 cy11 Tdh1 z00 Badd0 cy10 Tpre1 MS00 z01 mS00 mS01 bB1 vote1 tk1 td1 Tadd1 rel0 q0 premS00 df1 Tu1 eq1 premS01 s0 z11 eq0 Badd1 dup n0 MS01 nm0 preMS01 z10 crel0 nu0 e00 mS11 preMS00 e01 difmS00 difmS01 yl0 MS10 MS11 mS10 dn0 q1 u rel1 es s1 cm00 cm01 difMS01 difMS00 ou dmacp cnt00 yl1 cnt01 premS11 premS10 n1 xs xt dmayla nu1 npre0 ab01 ab00 preMS11 preMS10 rdy0 sco00 Xsc dmayclk crel1 sco01 e10 srdy0 kT0 nm1 te0 dn1 kr0 qT0 oh0 Tf0 e11 difmS10 cm10 difmS11 cm11 difMS10 difMS11 sel0 Tsc01 Tsc00 ab10 cnt10 cnt11 rdy1 te1 Tf1 Tsc11 Tsc10 nsel0 sco10 ab11 npre1 sco11 srdy1 kT1 kr1 qT1 oh1 sel1 nsel1 ex0 dmaytr ex1 ys0 dmaytt ys1 dmaysl"""
CONFIG = {'V': {'df0', 'e10', 'mC0@0', 'e01'}, 'S': {'bB'}, 'W': {'cy1@0', 'x1@0'}, 'tadd': 'P', 'dh': 'S', 'rel': 'V', 'xs': 'V', 'own': False, 'first': 'X', 'dnm': True, 'join': True, 'ttf': 'G'}
ORDER = """.pb70 .i1440 .kC0 .I10 .In0 .Ihf0 .pi0 .lb0 .pj0 .pj1 .col0 .cb0 .RK0 .iom0 dmaslot dmatrav dmaclk .CB0 .iog0 .of1 .BOp0 .J10 .BOh0 .par0 .col1 .of2 .of0 .RK1 .ones0 .OF0 U0 .sb0 .MK0 .CM0 .kh0 dmatt .lT0 .If0 .lb2 .PC0 .BT0 .lb1 bB0 U1 .Ig0 x01 .DF0 bl Tpre1 .RD0 .S160 bB1 eq0 x00 Hu0 dH0 .DF1 .Ifb0 .RS0 .BOn0 .TRn0 .S5120 cy01 cy00 x11 Tdh0 .Ik0 Hu1 df0 .BOq0 dmalast dH1 df1 Tpre0 vote0 tk0 td0 .lT1 Tadd0 Tu0 Badd0 cy11 .i320 Tdh1 z00 .RM0 mS00 z01 MS00 vote1 tk1 mS01 td1 q0 .TT0 Tadd1 premS01 rel0 premS00 s0 Tu1 eq1 crel0 n0 mC0 Badd1 dup nu0 MS01 z11 e01 preMS01 preMS00 MS11 nm0 mS11 e00 difmS00 difMS00 difmS01 difMS01 dn0 z10 MS10 mS10 q1 cm00 rel1 u s1 cm01 cnt00 es cnt01 ab00 premS11 n1 crel1 premS10 ou rdy0 nu1 te0 preMS10 Tf0 e10 sco00 xs ab01 sco01 npre0 srdy0 kT0 Tsc01 e11 kr0 preMS11 difmS10 nm1 qT0 xt oh0 mC1 Tsc00 difmS11 sel0 difMS10 difMS11 cm10 cm11 nsel0 dn1 ab10 ex0 sb0 sendT0 sendb0 cnt10 cnt11 Xsc npre1 rdy1 te1 sco10 ab11 sco11 srdy1 Tf1 kT1 kr1 sendT1 Tsc11 qT1 U0 oh1 sel1 Tsc10 nsel1 x00 Tpre0 ex1 sb1 x01 sg bB0 Hu0 df0 cy00 cy01 dH0 U1 x11 sendb1 Tdh0 vote0 par tk0 td0 x10 Hu1 dH1 Tadd0 bl Tpre1 Tu0 Badd0 cy11 Tdh1 cy10 z00 mS00 MS00 z01 vote1 tk1 mS01 td1 q0 Tadd1 rel0 df1 premS00 premS01 s0 bB1 Tu1 eq1 mC0 nm0 crel0 n0 eq0 nu0 MS01 z11 Badd1 e01 dup e00 MS11 mS11 preMS01 preMS00 dn0 z10 MS10 difmS00 difmS01 difMS00 mS10 q1 difMS01 rel1 cm00 cm01 ab00 u s1 cnt00 cnt01 ab01 es premS11 n1 crel1 ou rdy0 nu1 premS10 preMS10 te0 xs sco00 sco01 Tf0 e10 srdy0 kT0 nm1 kr0 preMS11 Tsc01 e11 qT0 difmS10 difMS10 mC1 dn1 cm10 difmS11 oh0 npre0 sel0 Tsc00 difMS11 cm11 nsel0 ex0 sendT0 xt sb0 cnt10 cnt11 sendb0 ab10 rdy1 te1 sco10 ab11 sco11 srdy1 Tf1 Xsc kT1 npre1 sendT1 Tsc11 kr1 qT1 U0 oh1 sel1 x01 nsel1 sg Tsc10 Tpre0 ex1 sb1 sendb1 x00 Hu0 cy01 bB0 dH0 cy00 U1 x11 Tdh0 df0 vote0 x10 par tk0 td0 Hu1 dH1 Tadd0 bl Tu0 z00 Badd0 Tdh1 cy11 cy10 vote1 mS00 MS00 Tpre1 z01 tk1 mS01 bB1 td1 Tadd1 q0 rel0 df1 premS01 premS00 s0 Tu1 Badd1 eq1 crel0 n0 mC0 MS01 z11 nu0 preMS01 preMS00 eq0 e01 dup nm0 MS11 e00 dn0 mS11 difmS00 difmS01 z10 MS10 difMS00 mS10 difMS01 cm00 q1 cm01 rel1 ab00 s1 u es cnt00 cnt01 premS11 n1 crel1 ou rdy0 nu1 premS10 preMS10 sco00 ab01 sco01 te0 xs Tf0 npre0 e10 srdy0 kT0 xt e11 kr0 preMS11 nm1 qT0 Tsc01 difmS10 oh0 dn1 difMS11 mC1 cm10 difmS11 sel0 difMS10 cm11 Tsc00 nsel0 ab10 cnt10 cnt11 ex0 sb0 sendT0 ab11 sendb0 rdy1 te1 sco10 sco11 srdy1 Tf1 Xsc npre1 kT1 kr1 sendT1 Tsc11 qT1 U0 oh1 sel1 Tsc10 x01 nsel1 sg Tpre0 ex1 sb1 x00 Hu0 cy01 bB0 dH0 cy00 U1 x11 sendb1 Tdh0 vote0 x10 df0 par tk0 td0 Tadd0 Hu1 dH1 bl Tu0 Tpre1 Badd0 cy11 Tdh1 cy10 vote1 z00 mS00 MS00 tk1 td1 z01 Tadd1 df1 mS01 bB1 Tu1 q0 rel0 premS01 premS00 s0 eq1 yl0 crel0 n0 eq0 Badd1 nu0 MS01 z11 e01 dup nm0 MS11 mS11 preMS01 preMS00 e00 z10 difmS00 difMS00 MS10 mS10 cm00 difmS01 u q1 cm01 rel1 es difMS01 ab00 s1 cnt00 cnt01 ou premS11 n1 xs rdy0 premS10 crel1 ab01 sco00 xt nu1 dmacp Xsc yl1 dmayla sco01 e10 dmayclk npre0 srdy0 kT0 dn0 kr0 preMS10 te0 nm1 preMS11 e11 dn1 Tf0 qT0 Tsc01 difmS10 oh0 difMS10 cm10 difmS11 sel0 cm11 Tsc00 difMS11 cnt10 ab10 cnt11 rdy1 te1 sco10 ab11 sco11 srdy1 Tf1 Tsc11 Tsc10 npre1 kT1 kr1 dmaytr dmaytt nsel0 ex0 ys0 qT1 oh1 sel1 nsel1 ex1 ys1 dmaysl"""
CONFIG.update(mh=False, u="M", acc=False)
CONFIG = {'V': {'mC1', 'mC0@1', 'df0', 'e01', 'mC0@2', 'cm11', 'e10', 'mC0@0'}, 'S': set(), 'W': set(), 'tadd': 'V', 'dh': 'V', 'rel': 'V', 'xs': 'V', 'own': False, 'first': 'X', 'dnm': False, 'join': True, 'ttf': 'G', 'mh': False, 'u': 'M', 'acc': False}
ORDER = """dmaslot dmatrav dmaclk dmatt .pi0 .iom0 .pj0 .pj1 .col0 .iog0 .BOp0 .cb0 .i1440 .CB0 .kh0 .lb0 .lb2 .lb1 .of0 bl .CH0 .CL0 .I10 .In0 .kC0 .col1 .S160 .S320 .RK0 .ones0 .of2 .PC0 .BOn0 .BT0 .hi0 .Ihf0 .RK1 .of1 .par0 .pb70 .lT0 .tS0 .sb0 .J10 .OF0 .MK0 .If0 .S5120 U0 .Ik0 .CM0 bB0 .DF1 .BOq0 .DF0 x01 .BOh0 x00 U1 .TRn0 bB1 eq0 .Jb0 dmalast Hu0 cy01 cy00 Hu1 dH0 df0 .RS0 dH1 eq1 vote0 tk0 x11 .lT1 x10 td0 Tadd0 Tu0 cy11 df1 cy10 z00 Badd0 mS00 dup .RM0 z01 mS01 q0 s0 n0 nu0 vote1 tk1 td1 e00 premS00 premS01 Tadd1 MS00 Tu1 rel0 z11 MS01 z10 Badd1 .TT0 crel0 preMS00 e01 nm0 mC0 mS11 dn0 dm0 preMS01 MS11 difmS00 difMS00 difmS01 MS10 mS10 q1 difMS01 .i320 s1 rel1 n1 nm1 dn1 .RD0 u es cm00 nu1 ou cm01 cnt00 cnt01 npre0 premS10 xs ab00 crel1 rdy0 te0 sco00 premS11 Tf0 xt ab01 e10 sco01 srdy0 kT0 Tsc01 dm1 kr0 qT0 oh0 sel0 e11 preMS11 difmS10 cm10 difmS11 preMS10 difMS10 cm11 mC1 ab10 nsel0 difMS11 ex0 Tsc00 sb0 Xsc ab11 cnt10 cnt11 rdy1 te1 Tf1 Tsc11 Tsc10 sco10 sendT0 U0 sco11 srdy1 kT1 kr1 qT1 npre1 oh1 sel1 nsel1 sendb0 Hu0 x00 sendT1 ex1 sb1 x01 cy00 cy01 U1 sg bB0 dH0 df0 vote0 par sendb1 Hu1 bB1 tk0 x11 bl x10 td0 dH1 Tadd0 Tu0 Badd0 cy11 cy10 vote1 z01 eq1 mS01 z00 df1 mS00 q0 s0 tk1 n0 td1 nu0 premS01 premS00 e00 Tadd1 Badd1 Tu1 MS01 rel0 z11 eq0 MS00 z10 e01 crel0 dup preMS00 preMS01 nm0 dn0 dm0 MS11 mS11 difmS00 cm00 difMS00 difmS01 MS10 mS10 mC0 difMS01 u rel1 q1 s1 nm1 n1 premS10 cnt00 cm01 cnt01 npre0 es premS11 nu1 ou dm1 ab00 xs preMS10 dn1 crel1 xt rdy0 te0 Tf0 e10 sco00 ab01 sco01 srdy0 Tsc01 kT0 kr0 qT0 e11 preMS11 difmS10 cm10 difmS11 difMS10 mC1 ab10 oh0 Tsc00 sel0 nsel0 difMS11 cm11 ex0 sb0 Xsc ab11 cnt10 cnt11 rdy1 te1 Tf1 Tsc11 Tsc10 sco10 sendT0 sco11 U0 sendb0 srdy1 kT1 kr1 npre1 qT1 oh1 sel1 Hu0 nsel1 bB0 sendT1 ex1 sb1 x00 x01 cy00 cy01 sg U1 dH0 df0 x10 vote0 sendb1 par Hu1 bB1 bl tk0 td0 Tadd0 Tu0 Badd0 cy10 x11 cy11 vote1 dH1 eq1 z01 z00 mS01 mS00 q0 tk1 df1 s0 n0 td1 premS00 premS01 nu0 e00 Tadd1 Tu1 eq0 rel0 z11 MS01 MS00 Badd1 dup z10 crel0 preMS00 preMS01 e01 nm0 dn0 dm0 MS11 difmS00 difMS00 difmS01 mS11 mC0 MS10 difMS01 cm00 mS10 q1 s1 n1 u nm1 rel1 es ou cm01 xs cnt00 cnt01 npre0 premS10 nu1 ab00 sco00 xt rdy0 te0 premS11 ab01 crel1 sco01 srdy0 e10 Tf0 kT0 dn1 kr0 Tsc01 qT0 dm1 preMS11 preMS10 oh0 e11 difmS10 difmS11 difMS10 cm10 mC1 sel0 nsel0 ab10 Tsc00 difMS11 cm11 ex0 sb0 Xsc cnt10 cnt11 ab11 rdy1 te1 Tf1 Tsc11 Tsc10 sco10 sendT0 U0 sco11 srdy1 sendb0 kT1 kr1 qT1 npre1 oh1 sel1 Hu0 x00 x01 nsel1 ex1 sendT1 sb1 cy00 cy01 U1 sendb1 df0 bB0 dH0 sg vote0 par bB1 Hu1 tk0 x11 bl x10 td0 dH1 Tadd0 Tu0 Badd0 cy11 cy10 vote1 z01 z00 mS01 eq1 df1 mS00 q0 s0 n0 tk1 premS00 premS01 nu0 td1 yl0 e00 MS01 Tadd1 rel0 Tu1 eq0 MS00 z11 z10 Badd1 crel0 preMS00 dup nm0 e01 dn0 dm0 preMS01 MS11 mS11 difmS00 difMS00 difmS01 cm00 MS10 mS10 yl1 dmacp q1 s1 rel1 n1 u cnt00 difMS01 nm1 es premS10 ou cm01 cnt01 npre0 xs crel1 xt Xsc ab00 rdy0 dn1 te0 ab01 sco00 sco01 srdy0 preMS10 premS11 dmayla dmayclk nu1 dm1 Tf0 e10 Tsc01 kT0 kr0 preMS11 qT0 oh0 sel0 e11 difmS10 cm10 difmS11 difMS10 ab10 Tsc00 difMS11 cm11 ab11 cnt10 cnt11 rdy1 te1 Tf1 Tsc11 Tsc10 nsel0 sco10 sco11 srdy1 dmaytr ex0 dmaytt npre1 ys0 kT1 kr1 qT1 oh1 sel1 nsel1 ex1 ys1 dmaysl"""
CONFIG = {'mh': False, 'u': 'M', 'acc': False, 'V': {'df0', 'mC0@3', 'df1', 'e01', 'e10', 'mC0@0', 'mC1@3'}, 'S': set(), 'W': {'cy1@0', 'mS0', 'x1@0'}, 'tadd': 'P', 'dh': 'V', 'rel': 'V', 'xs': 'V', 'own': False, 'first': 'X', 'dnm': True, 'join': True, 'ttf': 'G'}
ORDER = """dmaslot .RD0 .BT0 .BT1 .i321 .kh0 .i320 .DF1 .BT2 .BT3 .lb0 .RS0 .pb70 .kC0 .RD1 .pi0 dmatrav dmaclk dmatt .pj0 .iom0 .RK0 .of0 .pj1 .col0 .i1440 .ones0 .par0 .lb2 .cb0 .col1 dmalast .PC0 .MK0 .CB0 .RM0 .lT0 .RM1 .DF0 .CH0 .RK1 .I10 .If0 Tpre0 .iog0 .sb0 .CL0 .lb1 .of1 .CM0 U0 Tpre1 .Ik0 x01 .J10 x00 .S160 .In0 .S5120 .of2 U1 .OF0 .Ihf0 bB1 .BOp0 .RS1 .Jb0 df0 bl Hu0 cy01 cy00 .lT1 .BOn0 bB0 x11 dH0 .BOq0 vote0 Hu1 dH1 .RD2 .TRn0 .TT0 tk0 td0 Tadd0 eq0 Tu0 z00 cy11 Badd0 vote1 MS00 z01 mS01 premS01 tk1 q0 td1 Tadd1 df1 MS01 Tu1 s0 preMS01 z11 eq1 n0 rel0 nu0 mC0 premS00 Badd1 e00 nm0 e01 preMS00 z10 dup MS11 mS11 difmS00 dn0 difmS01 difMS01 .BOh0 MS10 mS10 q1 rel1 s1 crel0 difMS00 cm00 cm01 u es ab00 cnt00 cnt01 premS10 ab01 sco00 n1 premS11 rdy0 sco01 srdy0 te0 nu1 Tf0 npre0 e11 preMS10 e10 mC1 kT0 ou kr0 nm1 sendT0 qT0 crel1 Tsc01 oh0 xs difmS10 cm10 difmS11 preMS11 cm11 difMS10 sel0 dn1 xt ab10 nsel0 ex0 Tsc00 sb0 difMS11 cnt10 Xsc cnt11 ab11 rdy1 sco10 sendb0 sco11 srdy1 te1 Tf1 npre1 Tsc11 kT1 kr1 U0 qT1 oh1 Tsc10 sel1 Tpre0 nsel1 x01 sg Hu0 ex1 sb1 sendT1 cy01 x00 cy00 vote0 U1 par x11 bB0 sendb1 df0 dH0 tk0 bB1 td0 Hu1 bl Tadd0 x10 dH1 eq0 Tu0 z00 Badd0 cy11 cy10 MS00 Tpre1 vote1 z01 mS01 premS01 tk1 q0 td1 mC0 Tadd1 MS01 s0 premS00 Tu1 z11 df1 preMS01 n0 nm0 nu0 Badd1 eq1 dup e00 dn0 z10 e01 MS11 rel0 preMS00 difmS00 mS11 difMS01 difmS01 cm00 crel0 difMS00 MS10 mS10 q1 rel1 cm01 ab00 ab01 s1 u es cnt00 cnt01 n1 ou premS11 premS10 rdy0 sco00 sco01 nu1 crel1 srdy0 te0 e10 Tf0 e11 mC1 kT0 xs sendT0 preMS10 kr0 nm1 qT0 oh0 dn1 difmS10 cm10 npre0 difmS11 sel0 difMS10 xt Tsc01 cm11 preMS11 ab10 nsel0 difMS11 ex0 cnt10 cnt11 Tsc00 sb0 Xsc rdy1 sco10 ab11 sendb0 te1 Tf1 Tsc11 sco11 srdy1 npre1 kT1 Tsc10 kr1 U0 qT1 oh1 sel1 nsel1 Hu0 sg x01 ex1 sb1 x00 Tpre0 cy01 sendT1 cy00 U1 df0 sendb1 x10 x11 par bB0 dH0 vote0 tk0 td0 Tadd0 bl Hu1 dH1 bB1 Tu0 z00 Tpre1 Badd0 cy10 cy11 vote1 MS00 z01 mS01 premS01 tk1 q0 td1 Tadd1 eq0 s0 mC0 Tu1 df1 n0 premS00 nm0 nu0 Badd1 MS01 preMS01 z11 e00 eq1 dup e01 preMS00 z10 dn0 mS11 difmS00 MS11 difmS01 rel0 difMS00 crel0 difMS01 cm00 MS10 mS10 q1 rel1 s1 cm01 ab00 u cnt00 cnt01 es ab01 n1 ou premS10 rdy0 premS11 crel1 sco00 sco01 nu1 srdy0 te0 e11 e10 mC1 Tf0 kT0 xs kr0 nm1 preMS10 xt sendT0 qT0 oh0 difmS11 cm11 difmS10 cm10 npre0 preMS11 sel0 difMS10 dn1 ab10 nsel0 difMS11 Tsc01 ex0 cnt10 cnt11 Tsc00 sb0 Xsc npre1 sendb0 rdy1 te1 Tf1 sco10 ab11 sco11 srdy1 Tsc11 kT1 Tpre0 kr1 qT1 U0 x00 oh1 sendT1 sel1 Tsc10 x01 nsel1 ex1 Hu0 sb1 sg df0 cy00 cy01 sendb1 U1 x10 vote0 Tpre1 dH0 par x11 bB0 tk0 td0 bl Hu1 dH1 Tadd0 bB1 Tu0 z00 Badd0 cy10 cy11 MS00 vote1 z01 mS01 premS01 tk1 q0 td1 Tadd1 s0 yl0 premS00 eq0 Tu1 df1 n0 MS01 nm0 nu0 Badd1 preMS01 z10 eq1 rel0 e00 crel0 z11 e01 preMS00 dup dn0 difmS01 MS10 difMS01 dmacp mS10 difmS00 MS11 u difMS00 mS11 rel1 q1 cm01 cm00 es cnt00 ou cnt01 s1 xs ab00 n1 xt crel1 premS10 rdy0 Xsc nu1 e10 sco00 premS11 yl1 ab01 sco01 srdy0 preMS11 kT0 kr0 nm1 qT0 oh0 sel0 e11 preMS10 difmS10 cm10 te0 Tf0 dmayla difmS11 cm11 difMS10 npre0 dn1 dmayclk ab10 nsel0 ex0 cnt10 cnt11 Tsc01 difMS11 rdy1 ys0 sco10 Tsc00 ab11 sco11 srdy1 te1 Tf1 Tsc11 Tsc10 npre1 dmaytr dmaytt kT1 kr1 qT1 oh1 sel1 nsel1 ex1 ys1 dmaysl"""
CONFIG = {'mh': False, 'u': 'M', 'acc': False, 'V': {'mC0', 'e10', 'e01', 'x11@0', 'mC1@1', 'x10@0'}, 'S': set(), 'W': {'cy1@1', 'cy1@0', 'cy1@2'}, 'tadd': 'V', 'dh': 'V', 'rel': 'V', 'xs': 'V', 'own': False, 'first': 'X', 'dnm': False, 'join': True, 'ttf': 'G', 'u16': True, 'split': True}
ORDER = """dmaslot dmatrav dmaclk .pi0 .BT0 .of0 .BT1 .BT2 .BT3 .i321 .DF1 dmatt .kh0 .lb0 .i1440 .RM0 .of2 .pb70 .RK0 .RK1 .RM1 .pj1 .RS0 .I10 .J10 .of1 .lb1 .pj0 .lb2 .OF0 bl bB0 bB1 .iom0 .col0 eq0 .col1 .i320 .DF0 .kC0 df0 .ones0 .In0 .Jb0 .cb0 .PC0 .CB0 .S160 .iog0 .S5120 .MK0 .CM0 .Ik0 .If0 .RD0 .CH0 .par0 U0 .BOp0 .BOn0 .BOq0 .RD1 .RD2 .sb0 .lT0 U1 .Ihf0 .CL0 .RS1 eq1 x01 x00 .BOh0 x10 x11 Hu0 cy01 cy00 dH1 dH0 vote0 Hu1 df1 tk0 td0 dmalast .lT1 Tadd0 Tu0 cy11 z00 mS00 MS00 z01 Badd0 mS01 vote1 tk1 q0 td1 s0 Tadd1 n0 Tu1 premS01 .TRn0 premS00 z11 nu0 Badd1 MS01 dup e00 preMS01 dn0 z10 e01 preMS00 nm0 rel0 mS11 crel0 MS11 difmS00 mC0 MS10 difmS01 cm00 difMS00 difMS01 mS10 dm0 u cnt00 cm01 q1 cnt01 rel1 s1 es crel1 ab00 n1 premS11 premS10 nm1 rdy0 nu1 ou ab01 .TT0 sco00 sco01 e11 e10 te0 srdy0 preMS10 difmS10 difmS11 preMS11 difMS10 difMS11 cm10 kT0 cm11 Tf0 kr0 Uo0 sendT0 xs qT0 dn1 xt oh0 ab10 Tsc01 mC1 cnt10 sel0 npre0 nsel0 Xsc Tsc00 ex0 cnt11 sb0 sco10 ab11 sco11 rdy1 srdy1 sendb0 dm1 te1 Tf1 kT1 Uo1 x00 kr1 npre1 qT1 oh1 Tsc11 sel1 nsel1 Tsc10 ex1 sb1 sendT1 sg x01 U0 Hu0 dH0 df0 x10 cy00 cy01 vote0 sendb1 par bB0 U1 x11 bl bB1 tk0 Hu1 td0 Tadd0 dH1 Tu0 df1 cy11 z00 mS00 z01 MS00 Badd0 mS01 vote1 tk1 q0 td1 s0 Tadd1 nm0 premS00 Tu1 n0 rel0 eq0 premS01 nu0 MS01 Badd1 eq1 z11 e01 crel0 preMS00 dup e00 mS11 dn0 preMS01 MS11 difmS00 mC0 z10 MS10 difmS01 cm00 difMS00 difMS01 mS10 dm0 u q1 cm01 cnt00 cnt01 rel1 s1 es crel1 ab00 n1 premS11 premS10 nm1 ab01 rdy0 nu1 ou sco00 sco01 e11 e10 te0 srdy0 preMS11 difmS10 preMS10 difmS11 dn1 kT0 difMS11 cm10 Tf0 kr0 difMS10 cm11 Uo0 xs qT0 ab10 Tsc01 cnt10 oh0 xt sendT0 sel0 npre0 nsel0 mC1 Xsc ex0 cnt11 rdy1 sb0 te1 Tsc00 Tf1 dm1 ab11 sco10 Uo1 sco11 srdy1 sendb0 kT1 kr1 qT1 Tsc11 x00 oh1 npre1 sel1 nsel1 sendT1 sg Tsc10 ex1 sb1 x01 Hu0 par df0 cy00 cy01 U0 bB0 U1 x10 x11 sendb1 dH0 bl dH1 vote0 tk0 bB1 td0 Hu1 Tadd0 eq0 Tu0 cy11 z00 mS00 z01 MS00 Badd0 mS01 df1 vote1 tk1 q0 td1 s0 Tadd1 n0 Tu1 eq1 premS01 MS01 nu0 z11 premS00 dn0 rel0 Badd1 preMS00 e01 MS11 dup e00 preMS01 mS11 nm0 crel0 difmS00 z10 MS10 cm00 difMS00 difmS01 difMS01 mS10 cm01 u mC0 q1 rel1 s1 cnt00 cnt01 es crel1 ab00 n1 premS11 premS10 nm1 rdy0 ab01 nu1 ou sco00 sco01 te0 srdy0 preMS10 e11 e10 preMS11 difmS10 cm10 difmS11 difMS10 difMS11 Tf0 kT0 cm11 dm0 Uo0 kr0 xs qT0 dn1 ab10 Tsc01 oh0 cnt10 xt mC1 sendT0 Tsc00 sel0 npre0 nsel0 Xsc ex0 cnt11 sb0 sco10 ab11 sco11 rdy1 srdy1 te1 dm1 Tf1 kT1 Uo1 x00 kr1 Tsc11 qT1 sendb0 oh1 npre1 sendT1 sel1 nsel1 Tsc10 sg ex1 sb1 Hu0 U0 x01 df0 cy00 cy01 par sendb1 dH0 bB0 U1 x11 x10 vote0 bl tk0 Hu1 df1 td0 dH1 Tadd0 bB1 Badd0 Tu0 cy11 cy10 vote1 z00 mS00 z01 MS00 eq0 tk1 mS01 td1 q0 yl0 Tadd1 s0 dmacp0 Tu1 eq1 n0 premS00 z10 MS01 premS01 nu0 nm0 rel0 Badd1 e01 u0 dmacp1 dup crel0 dn0 us0 preMS00 mS10 e00 preMS01 difmS00 z11 MS10 ju0 mS11 xs0 difMS00 cm00 q1 xt0 MS11 difmS01 cm01 yl1 dmayla difMS01 Xsc0 cnt00 u1 cnt01 rel1 s1 crel1 ab00 us1 nm1 n1 premS11 premS10 preMS10 es rdy0 ab01 nu1 ju1 sco00 sco01 te0 e11 e10 xs1 dmayc0 Tf0 preMS11 xt1 ou Xsc1 dn1 difmS10 srdy0 cm10 dmayc1 difmS11 difMS10 difMS11 kT0 cm11 dm1 dm0 ab10 Tsc01 cnt10 kr0 Tsc00 qT0 cnt11 rdy1 sco10 ab11 sco11 srdy1 te1 npre0 Tf1 Tsc11 Tsc10 oh0 npre1 kT1 sel0 nsel0 kr1 qT1 ex0 oh1 sel1 nsel1 ex1 ys0 ys1 dmaytr dmaytt dmaysl"""
CONFIG = {'mh': False, 'u': 'M', 'acc': False, 'V': {'mC0', 'df0', 'e01', 'x11@0', 'e10', 'df1@0'}, 'S': set(), 'W': {'x0@1', 'cy1@1', 'x1', 'mS0@2', 'cy1@2'}, 'tadd': 'P', 'dh': 'V', 'rel': 'V', 'xs': 'V', 'own': False, 'first': 'X', 'dnm': True, 'join': True, 'ttf': 'G', 'u16': True, 'split': True, 'C': {'0@1'}}
ORDER = """.BT0 .par0 .BT1 .i321 .BT2 .RM0 .kC0 .pi0 .RS0 .RM1 .pj0 .RK0 .lb0 .iog0 .RK1 .BT3 .DF0 .i1440 .of1 .iom0 .RS1 .sb0 .RD0 .pj1 .col0 .I10 .Jb0 .DF1 .cb0 .BOp0 .kh0 .pb70 .BOh0 .ones0 .RD1 .CB0 .CH0 .BOn0 dmaslot .lb1 .lb2 dmatrav .of0 bl df0 .lT0 .Ihf0 dmaclk dmatt .If0 Tpre1 bB1 .of2 .OF0 bB0 .J10 .CL0 .RD2 .BOq0 U0 .col1 .S160 .PC0 .MK0 .i320 .CM0 .Ik0 .In0 U1 eq0 eq1 x00 dmalast x01 .TRn0 x11 Hu0 cy00 cy01 dup .S5120 Tpre0 dH1 dH0 vote0 tk0 td0 Tadd0 Hu1 df1 Tu0 cy10 cy11 .lT1 z00 Badd0 z01 mS00 mS01 mC0 vote1 tk1 .TT0 q0 premS00 td1 MS01 Tadd1 Tu1 z11 s0 premS01 MS00 n0 rel0 Badd1 nu0 preMS00 sendc0 e00 preMS01 e01 nm0 z10 crel0 mS11 MS11 dn0 difmS00 mS10 difMS00 difmS01 difMS01 cm00 cnt00 premS10 cm01 q1 MS10 ab00 s1 ab01 u mC1 cnt01 n1 nm1 nu1 rel1 preMS10 sco00 dn1 es sco01 e10 premS11 rdy0 srdy0 e11 difmS10 difmS11 cm10 ou te0 crel1 cm11 xs Tf0 kT0 difMS10 Uo0 kr0 Tsc01 qT0 preMS11 xt ab10 oh0 sel0 difMS11 npre0 nsel0 cnt10 sendT0 cnt11 ab11 sco10 sco11 Xsc x01 ex0 sb0 rdy1 Tsc00 te1 Tf1 srdy1 sendb0 npre1 kT1 Uo1 kr1 Tsc11 qT1 oh1 U0 sel1 nsel1 sg Tsc10 ex1 Hu0 Tpre0 sb1 cy00 sendT1 cy01 U1 par bB0 df0 x11 dH0 vote0 tk0 sendb1 bl td0 Hu1 Tadd0 Tpre1 bB1 df1 Tu0 cy11 z00 dH1 Badd0 z01 mS00 mS01 vote1 tk1 mC0 premS00 q0 td1 eq1 s0 Tadd1 Tu1 MS00 n0 premS01 z11 Badd1 eq0 dup nu0 MS01 nm0 preMS00 e00 preMS01 z10 e01 dn0 difmS00 cm00 difMS00 difmS01 rel0 crel0 mS11 MS11 difMS01 cm01 cnt00 ab00 mS10 MS10 u q1 premS10 rel1 s1 cnt01 mC1 ab01 n1 nu1 preMS10 nm1 sco00 e10 dn1 rdy0 sco01 srdy0 premS11 e11 difmS11 es difmS10 crel1 te0 ou cm11 difMS10 cm10 Tf0 kT0 xs kr0 Uo0 xt preMS11 qT0 Tsc01 oh0 ab10 sel0 npre0 nsel0 difMS11 cnt10 sendT0 cnt11 ab11 sco10 sco11 Xsc x01 ex0 sb0 rdy1 Tsc00 te1 Tf1 srdy1 npre1 kT1 Uo1 kr1 Tsc11 qT1 U0 oh1 sendb0 sel1 nsel1 Tpre0 Tsc10 ex1 Hu0 x00 sb1 cy01 cy00 sg par sendT1 U1 bB0 dH0 df0 x11 vote0 tk0 sendb1 bl td0 Tadd0 Hu1 dH1 df1 Tu0 cy11 Tpre1 bB1 Badd0 z01 z00 mS01 eq0 vote1 tk1 q0 rel0 premS00 td1 eq1 s0 mC0 premS01 Tadd1 Tu1 dup MS00 n0 z10 Badd1 MS01 preMS00 nu0 e00 preMS01 z11 nm0 e01 dn0 difmS00 cm00 difMS00 difmS01 mS10 MS10 MS11 difMS01 u cm01 crel0 mS11 q1 rel1 s1 ab00 cnt00 premS10 cnt01 sco00 mC1 n1 ab01 preMS10 nm1 nu1 dn1 e10 rdy0 sco01 srdy0 e11 premS11 es te0 ou difmS10 difMS10 difmS11 cm10 preMS11 crel1 ab10 Tf0 kT0 xs kr0 cm11 xt qT0 Uo0 oh0 Tsc01 sel0 Tsc00 npre0 nsel0 difMS11 cnt10 cnt11 ex0 sb0 sendT0 ab11 sendb0 Xsc x01 rdy1 te1 sco10 sco11 srdy1 Tf1 kT1 Uo1 kr1 qT1 Tsc11 npre1 oh1 U0 sel1 nsel1 sg Tsc10 ex1 Hu0 x00 sb1 cy01 cy00 Tpre0 df0 par dH0 bB0 sendT1 U1 vote0 tk0 sendb1 bl td0 Hu1 x11 dmacp0 Tadd0 Tpre1 bB1 df1 Tu0 cy10 cy11 dH1 Badd0 z01 mS01 z00 mS00 yl0 eq0 vote1 tk1 q0 premS00 dmacp1 td1 eq1 s0 rel0 premS01 Tadd1 Tu1 MS01 MS00 n0 dup z10 nm0 Badd1 nu0 e00 preMS01 z11 dn0 e01 u0 us0 preMS00 difmS00 cm00 mS10 ju0 crel0 MS10 xs0 mS11 difMS00 difmS01 xt0 MS11 difMS01 cm01 ab00 cnt00 u1 ab01 Xsc0 q1 rel1 s1 cnt01 premS10 preMS10 us1 n1 ju1 nm1 sco00 rdy0 sco01 srdy0 xs1 nu1 e11 dmayc0 xt1 te0 e10 es difmS10 premS11 Xsc1 difmS11 dn1 ou crel1 Tf0 kT0 kr0 Tsc01 yl1 qT0 Tsc00 difMS10 cm10 cm11 cnt10 dmayla dmayc1 ab10 cnt11 preMS11 difMS11 oh0 rdy1 sel0 npre0 nsel0 ab11 sco10 sco11 srdy1 te1 Tf1 Tsc11 Tsc10 dmaytr npre1 kT1 ex0 kr1 qT1 oh1 sel1 dmaytt ys0 nsel1 ex1 ys1 dmaysl"""
CONFIG = {'mh': False, 'u': 'M', 'acc': True, 'C': {'0@1'}, 'u16': True, 'split': True, 'V': {'mC0', 'e10', 'e01', 'mC1@1', 'x10@0', 'mC1@0'}, 'S': set(), 'W': {'cy0@3'}, 'tadd': 'V', 'dh': 'V', 'rel': 'V', 'xs': 'V', 'own': False, 'first': 'X', 'dnm': False, 'join': True, 'ttf': 'G'}
ORDER = """.BT0 .BT1 dmaslot dmatrav dmaclk dmatt .RM0 .lb0 .DF1 .i320 .BT2 .RS0 .pb70 .pi0 .par0 .i321 .pj1 .BT3 .sb0 .of0 .RK0 .RM1 .RS1 .iom0 .kC0 .pj0 .kh0 .col0 .MK0 .RK1 .ones0 .cb0 .CB0 .i1440 .RD0 .CM0 .DF0 .lT0 .RD1 .of2 .I10 .lb2 .Jb0 .CH0 .col1 .In0 .lb1 .J10 .of1 .OF0 bB0 .Ik0 U1 U0 .CL0 bB1 .S160 .PC0 x01 x10 .Ihf0 .S5120 bl x00 df0 .iog0 .BOp0 x11 .BOq0 .RD2 .BOn0 eq0 .TRn0 .If0 Hu0 cy01 cy00 Hu1 dH0 dH1 .TT0 cy10 vote0 tk0 dmalast td0 Tadd0 Tu0 df1 cy11 .lT1 eq1 .BOh0 Badd0 z00 mS00 MS00 z01 mS01 vote1 tk1 q0 td1 mC0 premS01 Tadd1 s0 Tu1 sendc0 n0 z11 nu0 rel0 MS01 e00 e01 z10 premS00 mS11 MS11 D0 dup Badd1 difmS01 nm0 MS10 mS10 difmS00 crel0 dn0 u q1 cm00 mC1 difMS00 dm0 premS11 s1 cm01 D1 n1 es difMS01 cnt00 cnt01 premS10 ab00 ab01 sco00 sco01 nm1 nu1 dn1 ou e10 rdy0 xs dm1 e11 srdy0 te0 rel1 difmS10 xt kT0 cm10 difmS11 Tf0 kr0 Uo0 qT0 Tsc01 crel1 cm11 npre0 difMS10 oh0 cnt10 sel0 Xsc nsel0 difMS11 ex0 Tsc00 cnt11 sb0 ab10 rdy1 ab11 sendT0 sco10 sco11 srdy1 te1 Tf1 Tsc11 kT1 Uo1 x00 sendb0 npre1 x01 kr1 qT1 oh1 sel1 nsel1 sendT1 x11 x10 Tsc10 df0 ex1 sb1 sg Hu0 sendb1 cy00 cy01 U0 bB0 U1 par dH0 vote0 tk0 bB1 td0 Hu1 dH1 Tadd0 bl Tu0 df1 cy11 Badd0 cy10 z00 MS00 mS00 z01 mS01 vote1 tk1 q0 td1 premS00 rel0 premS01 Tadd1 s0 Tu1 eq1 n0 eq0 z11 nu0 MS01 mC0 e00 e01 D0 crel0 mS11 Badd1 MS11 dup difmS00 difmS01 z10 MS10 nm0 mS10 dn0 u q1 dm0 cm00 mC1 difMS00 s1 premS11 cm01 D1 n1 es difMS01 cnt00 cnt01 nm1 nu1 premS10 dn1 ou e10 ab00 ab01 sco00 sco01 rdy0 dm1 xs e11 srdy0 te0 rel1 difmS10 kT0 xt cm10 difmS11 kr0 Tf0 qT0 Tsc01 Uo0 crel1 cm11 npre0 difMS10 cnt10 oh0 ab10 Tsc00 cnt11 sel0 difMS11 Xsc nsel0 rdy1 ab11 sendT0 sco10 sco11 srdy1 ex0 sb0 te1 Tf1 Tsc11 kT1 sendb0 npre1 x01 kr1 Uo1 qT1 oh1 sel1 nsel1 sendT1 x00 x11 x10 df0 Tsc10 ex1 sb1 sendb1 sg Hu0 cy01 cy00 U0 bB0 U1 par dH0 bl bB1 vote0 tk0 Hu1 td0 dH1 Tadd0 Tu0 cy10 df1 cy11 Badd0 z00 MS00 mS00 vote1 z01 mS01 tk1 q0 td1 rel0 premS01 Tadd1 s0 Tu1 n0 eq1 eq0 z11 nu0 premS00 MS01 e00 e01 D0 mS11 MS11 Badd1 dup crel0 mC0 z10 difmS01 MS10 nm0 mS10 dn0 dm0 difmS00 u q1 cm00 premS10 mC1 difMS00 cm01 es difMS01 cnt00 cnt01 premS11 s1 D1 n1 nm1 nu1 dn1 ou e10 ab00 ab01 sco00 sco01 rdy0 dm1 e11 xs srdy0 te0 rel1 kT0 xt difmS10 cm10 difmS11 Tf0 kr0 Uo0 crel1 cm11 npre0 difMS10 cnt10 qT0 oh0 Tsc01 ab10 sel0 Xsc nsel0 ex0 difMS11 Tsc00 cnt11 sb0 rdy1 ab11 sendT0 sco10 sco11 srdy1 te1 Tf1 Tsc11 x00 kT1 Uo1 sendb0 npre1 x01 kr1 qT1 oh1 sel1 nsel1 sendT1 x10 df0 x11 Tsc10 ex1 sb1 sendb1 sg Hu0 bB0 cy01 U0 U1 par dH0 bB1 bl vote0 tk0 Hu1 td0 dH1 Tadd0 Tu0 df1 cy11 cy10 Badd0 z00 mS00 MS00 z01 mS01 vote1 tk1 q0 td1 premS00 rel0 premS01 Tadd1 s0 Tu1 n0 MS01 eq0 nu0 yl0 z11 dmacp0 eq1 D0 e01 z10 e00 mS11 Badd1 dup nm0 u0 dn0 crel0 difmS01 difmS00 mS10 us0 MS10 MS11 dm0 ju0 D1 q1 u1 premS11 xs0 us1 xt0 s1 yl1 ju1 Xsc0 dmacp1 cm01 difMS01 cm00 difMS00 nm1 es cnt00 cnt01 premS10 n1 dm1 nu1 dn1 ab01 ab00 sco00 sco01 ou dmayc0 e10 rdy0 e11 difmS10 xs1 srdy0 te0 rel1 xt1 difmS11 Tf0 Xsc1 dmayla dmayc1 kT0 cm10 Tsc01 kr0 qT0 crel1 cm11 npre0 difMS10 cnt10 oh0 sel0 ab10 Tsc00 cnt11 rdy1 te1 Tf1 Tsc11 difMS11 nsel0 ex0 ab11 sco10 sco11 srdy1 dmaytr npre1 Tsc10 dmaytt kT1 kr1 qT1 oh1 sel1 nsel1 ex1 ys0 ys1 dmaysl"""
CONFIG = {'mh': True, 'u': 'S', 'acc': False, 'C': {'0@1'}, 'u16': True, 'split': True, 'V': {'df0', 'df1', 'e01', 'e10', 'x10@0'}, 'S': set(), 'W': {'x1@3'}, 'tadd': 'V', 'dh': 'V', 'rel': 'W', 'xs': 'V', 'own': False, 'first': 'X', 'dnm': False, 'join': True, 'ttf': 'G'}
ORDER = """.pi0 .RK0 .pj1 .RK1 .sb0 .pj0 .i1440 .col0 .RS0 .RS1 .p320 .col1 .RD0 .RD1 .BT0 .i321 .RM0 .L320 .I10 .lb0 .In0 .iom0 .BT1 .PC0 .iog0 .BT2 .BT3 .RM1 .DF1 .J10 dmaslot dmatrav dmaclk .ones0 dmatt .L321 .of1 .cb0 .pb70 .S160 .S5120 .kh0 .MK0 .lb1 .lT0 U1 .kC0 .lb2 .CM0 bB1 .of0 .of2 .par0 .RD2 bl U0 bB0 .OF0 dmalast .BOp0 x01 .i320 x10 Hu0 x00 .BOn0 .TRn0 .TT0 .BOq0 dH0 cy01 cy00 A81 .lT1 .DF0 x11 Hu1 cy10 vote0 tk0 dH1 td0 .BOh0 Tadd0 df1 Tu0 cy11 eq1 .Ik0 vote1 A80 z00 MS00 mS00 z01 mS01 tk1 premS00 premS01 mh0 td1 q0 Tadd1 MS01 Tu1 z11 s0 rel0 n0 df0 preMS01 nu0 e00 mC0 eq0 e01 preMS00 MS11 crel0 dup difmS01 mS11 dn0 difmS00 difMS00 sendc0 nm0 difMS01 z10 mS10 MS10 dm0 u cm00 premS10 cm01 mh1 rel1 q1 cnt00 cnt01 mC1 es npre0 ab00 s1 crel1 sco00 ui preMS10 ab01 premS11 sco01 n1 ou nm1 nu1 uj rdy0 e10 e11 srdy0 difmS10 uk cm10 te0 difmS11 cm11 dn1 ju Tf0 kT0 xs difMS10 kr0 dm1 xt Uo0 qT0 Xsc oh0 preMS11 difMS11 cnt10 cnt11 Tsc01 sendT0 sel0 nsel0 Tsc00 ab10 rdy1 sco10 ex0 te1 sb0 ab11 sco11 srdy1 sendb0 Tf1 Uo1 x01 kT1 kr1 qT1 oh1 npre1 sendT1 sel1 Tsc11 nsel1 ex1 sb1 Tsc10 U0 Hu0 x00 dH0 cy01 cy00 df0 bB0 U1 sendb1 sg par x10 A81 x11 bB1 Hu1 vote0 tk0 dH1 td0 df1 Tadd0 bl Tu0 cy10 cy11 A80 z00 mS00 MS00 eq1 vote1 z01 mS01 tk1 td1 mh0 Tadd1 premS00 q0 Tu1 MS01 premS01 z11 s0 rel0 n0 preMS01 mC0 nm0 nu0 e00 eq0 e01 crel0 preMS00 dup MS11 difmS00 difMS00 difmS01 mS11 dn0 dm0 z10 MS10 difMS01 mS10 cm00 u cm01 premS10 mh1 rel1 q1 cnt00 cnt01 es mC1 ab00 s1 npre0 crel1 sco00 ab01 premS11 sco01 ui preMS10 n1 ou rdy0 nu1 uj e11 srdy0 nm1 e10 difmS10 cm10 uk te0 dn1 ju Tf0 difmS11 kT0 difMS10 xs dm1 kr0 xt Uo0 qT0 Xsc oh0 Tsc01 cm11 preMS11 cnt10 difMS11 sendT0 sel0 cnt11 Tsc00 ab10 nsel0 rdy1 sco10 ex0 te1 sb0 ab11 sco11 srdy1 sendb0 Tf1 Uo1 sendT1 x00 x01 kT1 kr1 qT1 oh1 npre1 sel1 Tsc11 nsel1 ex1 sb1 Tsc10 U0 Hu0 dH0 cy01 cy00 sendb1 sg x10 A81 x11 df0 U1 bB0 par bl Hu1 vote0 bB1 tk0 dH1 td0 df1 Tadd0 Tu0 cy10 cy11 eq1 vote1 A80 z00 MS00 z01 mS00 mS01 tk1 mh0 td1 premS00 q0 Tadd1 MS01 premS01 Tu1 s0 rel0 z11 n0 preMS01 mC0 nm0 nu0 e00 eq0 e01 crel0 preMS00 dup MS11 difmS00 difMS01 dn0 difMS00 difmS01 mS11 dm0 z10 mS10 MS10 cm00 premS10 u cm01 mh1 rel1 q1 cnt00 cnt01 ab00 s1 mC1 npre0 es crel1 n1 nm1 nu1 ui preMS10 ab01 sco00 premS11 sco01 ou e10 uj rdy0 uk te0 e11 srdy0 difmS10 dn1 cm10 ju Tf0 difMS10 difmS11 kT0 xs kr0 dm1 cm11 xt Uo0 preMS11 qT0 Xsc oh0 Tsc01 cnt10 difMS11 sendT0 sel0 cnt11 nsel0 Tsc00 ab10 rdy1 sco10 ab11 ex0 sco11 srdy1 te1 sb0 sendb0 Tf1 x00 x01 Uo1 kT1 kr1 qT1 oh1 npre1 sel1 Tsc11 sendT1 nsel1 ex1 sb1 Tsc10 U0 Hu0 bB0 cy01 cy00 dH0 df0 U1 sendb1 sg par bB1 x11 bl A81 Hu1 vote0 dmacp0 tk0 dH1 td0 df1 Tadd0 Tu0 cy10 cy11 A80 z00 MS00 vote1 mS00 eq1 z01 mS01 tk1 mh0 td1 premS01 premS00 q0 Tadd1 MS01 Tu1 s0 yl0 n0 z11 rel0 u0 preMS01 nu0 e00 eq0 e01 preMS00 crel0 dup MS11 nm0 difmS00 dn0 difMS00 difmS01 mS11 dm0 es us0 difMS01 z10 mS10 MS10 cm00 cm01 premS10 u1 ju0 rel1 xs0 mh1 xt0 q1 cnt00 cnt01 Xsc0 ab00 s1 sco00 ab01 premS11 sco01 us1 n1 crel1 preMS10 nm1 nu1 ju1 rdy0 e10 srdy0 dn1 xs1 yl1 te0 ou kT0 xt1 dmacp1 e11 difmS10 cm10 difmS11 difMS10 kr0 Xsc1 npre0 dmayc0 qT0 Tf0 oh0 preMS11 cm11 Tsc01 cnt10 sel0 cnt11 Tsc00 difMS11 ab10 nsel0 rdy1 te1 dm1 sco10 ab11 Tf1 ex0 sco11 srdy1 dmayla Tsc11 npre1 Tsc10 dmayc1 kT1 kr1 qT1 oh1 sel1 dmaytr nsel1 ex1 ys0 dmaytt ys1 dmaysl"""


def build(T, send, cfg):
    ops, now = [], {"v": 0}

    def ap(name, a=0, b=None, step=None):
        b = T[name].shape[1] if b is None else b
        return (name, a, b, T[name][:, a:b] if step is None else T[name][:, a:b:step])

    def val(x):
        return x[3] if isinstance(x, tuple) else x

    def aps(*xs):
        return [x for x in xs if isinstance(x, tuple)]

    def two(*xs):
        return all(SCRATCH[x[0]][2] in (BF, F16, U16) for x in xs)

    def cnt(x):
        return x[3].shape[1]

    def add(name, eng, fn, rd, wr, kind, n, **kw):
        if not name or name == "TTf":
            name = "%s%s%d" % (name or ".", wr[0][0], sum(o["wr"][0][0] == wr[0][0] for o in ops))
        ops.append(dict(name=name, eng=eng, fn=fn, rd=rd, wr=wr, kind=kind, n=n, **kw, **now))
        return ops[-1]

    def named(key, name):
        return name in cfg[key] or "%s@%d" % (name, now["v"]) in cfg[key]

    def on(name):
        return "V" if named("V", name) else "S"

    def off(name):
        return named("S", name)

    def ind(win, o):
        return win[3].indirect(o[3])

    def tt(name, out, a, b, op):
        both = SCRATCH[a[0]][0] == "sbuf" and SCRATCH[b[0]][0] == "sbuf"
        return add(name, "V", lambda q: [q.tensor_tensor(out[3], a[3], b[3], op)], [a, b], [out], "v", cnt(out) * (2 if both else 1))

    def ts(name, out, a, s1, s2, op0, op1=None):
        def fn(q):
            if op1 is None:
                return [q.tensor_scalar(out[3], a[3], val(s1), None, op0)]
            return [q.tensor_scalar(out[3], a[3], val(s1), val(s2), op0, op1)]
        return add(name, "V", fn, [a] + aps(s1, s2), [out], "v", cnt(out) * (0.5 if two(out, a) else 1))

    def cp(name, out, a):
        return add(name, "V", lambda q: [q.tensor_copy(out[3], a[3])], [a], [out], "v", cnt(out) * (0.5 if two(out, a) else 1))

    def act(name, out, a, f, bias=0.0, scale=1.0):
        return add(name, "S", lambda q: [q.activation(out[3], a[3], f, bias=val(bias), scale=scale)], [a] + aps(bias), [out], "v", cnt(out))

    def aff(name, out, a, mul, plus):
        if name and on(name) == "V" or SCRATCH[out[0]][2] == F16:
            return ts(name, out, a, float(mul), float(plus), A.mult, A.add)
        return act(name, out, a, F.Identity, float(plus), float(mul))

    def step(name, out, a, thr, bias, scale):
        return act(name, out, a, F.Sigmoid, bias, scale) if off(name) else ts(name, out, a, *thr)

    def ms(out, c):
        return add("", "V", lambda q: [q.memset(out[3], c)], [], [out], "v", cnt(out) * (0.5 if two(out) else 1))

    def scan(name, out, d0, d1, init, op0, op1):
        return add(name, "V", lambda q: [q.tensor_tensor_scan(out[3], d0[3], d1[3], init, op0, op1)], [d0, d1], [out], "v",
                   cnt(out) * (0.5 if two(out, d0, d1) else 1))

    def vt(name, out, a):
        return add(name, "V", lambda q: [q.transpose(out[3], a[3])], [a], [out], "v", cnt(out) * (0.5 if two(out, a) else 1))

    def gat(name, out, win, o, eng=None):
        eng = eng or on(name)

        def fn(q):
            if eng == "V":
                return [q.tensor_copy(out[3], ind(win, o))]
            return [q.activation(out[3], ind(win, o), F.Copy)]
        return add(name, eng, fn, [win, o], [out], "g", cnt(out))

    def gtt(name, out, win, o, b, op):
        return add(name, "V", lambda q: [q.tensor_tensor(out[3], ind(win, o), b[3], op)], [win, o, b], [out], "g", cnt(out))

    def sct(name, win, o, a):
        return add(name, "V", lambda q: [q.tensor_copy(ind(win, o), a[3])], [o, a], [win], "sc", cnt(a))

    def mm(name, terms, part="whole"):
        n = sum(max(64, cnt(r)) * (4 if SCRATCH[r[0]][2] == F32 else 1) for o, l, r in terms)

        def fn(q):
            for i, (o, l, r) in enumerate(terms):
                ins = q.matmul(o[3], l[3], r[3], i == 0 and part in ("whole", "open"), i == len(terms) - 1 and part in ("whole", "close"))
            return [ins]
        return add(name, "P", fn, [x for o, l, r in terms for x in (l, r)], [o for o, l, r in terms], "pe", n, part=part)

    def iota(out, pattern, base, ch):
        def fn(q):
            if SCRATCH[out[0]][2] == I32:
                return [q.iota(out[3], pattern, base, ch)]
            return [q.iota(out[3], pattern, base, ch, allow_small_or_imprecise_dtypes=True)]
        return add("", "G", fn, [], [out], "io", cnt(out))

    def sel(out, a, pattern, op, ch):
        return add("", "G", lambda q: [q.affine_select(out[3], a[3], pattern, op, 0.0, 0, ch)], [a], [out], "io", cnt(out) + 24)

    def dma(eng, sem, out, a, rd, wr, nbytes):
        return add("dma" + sem, eng, lambda q: [q.dma_start(out, a)], rd, wr, "dma", nbytes, sem="d" + sem)

    def slot(name, v, h, n=4):
        return ap(name, 16 * v + 8 * h, 16 * v + 8 * h + n)

    def box(name, v, h, a=0, n=1):
        stay = v == (0 if name[0] == "l" else VISITS - 1)
        o = 2 * L * v + (H * (1 - h) + L * a if stay else L * h + H * a)
        return ap(name, o, o + n * H)

    loads = [("slot", ap("slot0"), T.slot, 4), ("trav", ap("trav0"), T.trav, 4), ("clk", ap("X"), T.clk, 2), ("tt", ap("tt32"), T.ttab, 4),
             ("last", ap("last0"), T.last, 2)]
    if cfg["first"] != "X":
        loads[2:4] = loads[3:1:-1]
    for k, (name, to, src, size) in enumerate(loads):
        o = dma("Y", name, to[3], src[:], [], [to], 128 * cnt(to) * size)
        if k:
            o["behind"] = ops[-2]

    def col(i):
        return ap("col", i, i + 1)
    P, G, PC = col(0), col(1), col(2)
    wide = 64 if any(x[1] == "S" for x in cfg["W"]) else 32
    iota(ap("pi"), [[0, 1]], 0, 1)
    iota(ap("i144"), [[1, 144]], 1, -1)
    iota(ap("iog"), [[1, 8], [0, 16]], 0, 0)
    iota(ap("iom"), [[0, 8], [1, 16]], 0, 0)
    iota(ap("BT", 0, L), [[1, L]], 0, 0)
    for w in (L, 2 * L, 4 * L):
        aff("", ap("BT", w, 2 * w), ap("BT", 0, w), 1, w)
    aff("", ap("DF", 0, B - 97), ap("BT", 0, B - 97), 1, 97)
    aff("", ap("DF", B - 97, B), ap("BT", 0, 97), 1, 0)
    for h in range(2):
        aff("", ap("i32", H * h, H * h + H), ap("BT", 0, H), 32, 32 * H * (1 - h))
    iota(ap("of", 0, 8), [[8, 2], [1, 4]], 0, 0)
    iota(ap("of", 8, 16), [[8, 2], [2, 2], [-4, 2]], 4, 0)
    iota(ap("of", 16, 20), [[16, 4]], 15, 0)
    for name, rest, first in (("RS", 0.0, 4096.0), ("RM", 4096.0, 0.0)):
        ms(ap(name, 0, 16 * wide), rest)
        ms(ap(name, 0, 16 * wide, 16), first)
    ms(ap("RD"), 8192.0)
    ms(ap("RD", L, 2 * L, 16), 0.0)
    iota(ap("RD", 0, L, 16), [[-16, 8]], SP - 1, -1)
    ts("", ap("pj", 0, 1), ap("pi"), 15, None, A.bitwise_and)
    ts("", ap("pj", 1, 2), ap("pi"), 4, None, A.logical_shift_right)
    cp("", ap("col", 0, 2), ap("pj"))
    ts("", PC, P, -1.0, 16.0, A.mult, A.add)
    ts("", ap("cb"), P, 2452.0, -0.25, A.mult, A.add)
    ts("", ap("hi"), P, 8.0, None, A.is_ge)
    bound = {"V": 65536.0 + 32 * 12, "S": 65536.0 + 16 * 8}
    for x, y in ("VS", "SV"):
        ts("", ap("t" + x), ap("hi"), bound[y] - bound[x], bound[x], A.mult, A.add)
        ts("", ap("u" + x), ap("t" + x), -8.0, 128.0, A.mult, A.add)
    if cfg["S"] or cfg["rel"] == "S":
        act("", ap("ones"), ap("iom"), F.Sigmoid, 128.0)["n"] += 1500
    else:
        act("", ap("ones"), ap("iom"), F.Identity, 1.0, 0.0)
    act("", ap("CB"), ap("iom", 0, H), F.Identity, ap("cb"), 0.0)
    cp("", ap("CH"), ap("CB"))
    tt("", ap("CL"), ap("CB"), ap("CH"), A.subtract)
    act("", ap("PC"), ap("iom", 0, H), F.Identity, PC, 0.0)
    iota(ap("L32"), [[-32 * H, 2], [512, 4]], 32 * H, 0)
    ts("", ap("p32"), P, 32.0, None, A.mult)
    ts("", ap("L32"), ap("L32"), ap("p32"), None, A.add)
    ts("", ap("S16"), ap("i144"), PC, 16.0, A.is_equal, A.mult)
    for name, w in (("S32", 2), ("S512", 32)):
        aff("", ap(name), ap("S16"), w, 0)
    ts("", ap("I1"), ap("i144", 0, 128), 1.0, None, A.is_equal)
    for name, w in (("If", 1), ("Ig", -1), ("Ihf", 0.5), ("Ifb", 148), ("Jb", 148), ("J1", 1), ("In", -1), ("Ik", 65536), ("Ih", 0.5)):
        aff("", ap(name), ap("I1"), w, 0)
    for name, w in (("kC", 1.5 * 2 ** 28), ("kD", 1.5 * 2 ** 23), ("kh", 15.5), ("kv", 4736.0), ("mh", -0.5), ("par", 256.0), ("sb", 65535)):
        ms(ap(name), w)
    ms(ap("pb7", 4 * H, 4 * H + 1), 256.0)
    ts("", ap("BOp"), ap("iog"), G, None, A.is_equal)
    for name, w in (("BOh", 1), ("BOn", -4096), ("BOq", -1)):
        aff("", ap(name), ap("BOp"), w, 0)
    sel(ap("TRn"), ap("BOn"), [[1, L]], A.is_gt, -1)
    ts("", ap("MK"), ap("iom"), P, 16384.0, A.not_equal, A.mult)
    aff("", ap("CM"), ap("MK"), -1, SP)
    cp("", ap("OF"), ap("of"))
    ms(ap("RK"), 1048576.0)
    ms(ap("RK", 0, H, 16), 65536.0)
    cp("", ap("lT", 0, L), ap("trav0"))
    aff("", ap("lT", L, 2 * L), ap("last0"), 1, 0.5 * (cfg["mh"] and not cfg.get("u16")))
    ms(ap("lb", 0, 16), 65535)
    for h in range(2):
        cp("", slot("lb", 0, h), ap("slot0", 4 - 4 * h, 8 - 4 * h))
    if cfg["ttf"] == "G":
        sel(ap("TT", SP), ap("tt32"), [[0, B]], A.is_ge, 0)
    else:
        for q in range(4):
            cp("TTf", ap("TT", SP + 256 * q, SP + 256 * q + 256), ap("tt32", 256 * q, 256 * q + 256))
    X, TT = ap("X"), ap("TT", SP)

    def smat(name, k):
        return ap(name, 15 - k, 143 - k)

    def b(name, h, a=0, z=None, step=None):
        w = SCRATCH["h" + name][1][1] // 2
        return ap("h" + name, w * h + a, w * h + (w if z is None else z), step)

    def pieces(name, h):
        return [(name + "%d1" % h, 0, 2)] if named("W", name + str(h)) else [(name + "%d%d" % (h, q), q, q + 1) for q in range(2)]

    def part(name, h, a, z):
        w = SCRATCH["h" + name][1][1] // 4
        return b(name, h, w * a, w * z)

    def pb(bank, i, n=1):
        return ap("pb%d" % bank, H * i, H * (i + n))

    def mrow(name, h):
        return ap(name, 1024 * h + 15, 1024 * h + 1024, 16)

    def update(v, last, byM, up, M, xt, ju):
        mm("u", [(up, ap(l), r) for l, r in [("I1", ap("kh")), ("BOq", M), ("I1", ap("kC")), ("In", ap("kC")), ("I1", ap("i32"))] * byM +
                 [("BOp", M), ("In", ap("MK"))]])
        if cfg["join"]:
            scan("es", ap("es"), ap("RD"), pb(6, 4, 4), 65536.0, A.min, A.max)
            cp("ou", ap("ou", 0, 8 + 8 * byM), ap("es", 15, L + L * byM, 16))
        else:
            scan("us", ap("es", L), ap("RD", L), up, 65536.0, A.min, A.max)
            if byM:
                cp("ju", ju, ap("es", L + 15, 2 * L, 16))
        if not byM:
            cp("ui", ap("ui"), ap("es", L + 15, 2 * L, 16))
            ts("uj", ap("uj"), ap("ui"), 31, None, A.bitwise_and)
            tt("uk", ap("uk"), ap("uj"), ap("L32"), A.add)
            cp("ju", ju, ap("uk"))
        if cfg["xs"] != "V":
            gat("xo", ap("xo"), X, ju, "S")
            mm("xp", [(up, ap("Ih"), r) for r in (ap("xo"), M, ap("mh"))] + [(up, ap(l), ap("kD")) for l in ("I1", "In")])
            xt = ap("xb")
            act("xt", xt, up, F.Copy)
        else:
            gtt("xs", ap("xs"), X, ju, M, A.add)
            ts("xt", xt, ap("xs"), 1, None, A.logical_shift_right)
        if last:
            dma("Y", "cp", T.X2[:], T.X[:], [X, slot("lb", v, 1)], [ap("X2")], 1048576)
            sct("Xsc", ap("X2"), ju, xt)
            dma("Y", "yclk", T.yclk[:], T.X2[:], [ap("X2")], [], 1048576)
            dma("Y", "yla", T.ylast[:], T.yl[:], [ap("yl")], [], 32768)

    for v in range(VISITS):
        last = v == VISITS - 1
        split = last and cfg.get("split")
        now["v"] = v
        bname = "bF" if off("bB") else "bB"
        byP, mh, u16 = cfg["tadd"] == "P", cfg["mh"], cfg.get("u16")

        def post(k, h, src, dst):
            add("send%s%d" % (k, h), "G", lambda q, sem="arr%d_%d_%s" % (v + 1, h, k): [send(dst[3], src[3], sem)], [src], [], "send",
                128 * cnt(src) * (4 if src[0] == "sT" else 2), tag=("send", v, h, k), sem="sent")

        def dfb(h):
            return b("dg" if on("df%d" % h) == "V" else "df", h)

        def one(x):
            return ap("J1" if SCRATCH[x[0]][2] == F16 else "If")

        for h in range(2):
            s = str(h)
            Tl, Cl, bo = box("lT", v, h), box("lT", v, h, 1), slot("lb", v, h)
            Tp, Fp, Bp, Cp = (pb(4 + h, i) for i in range(4))
            if v:
                land = "lU" if u16 else "lT"
                apart = [("T", box(land, v, h)), ("c", box(land, v, h, 1))] if named("C", s) else [("T", box(land, v, h, 0, 2))]
                for k, r in apart + [("b", slot("lb", v, h, 8))]:
                    add("arr", "R", None, [], [r], "arr", 0, sem="arr%d_%d_%s" % (v, h, k), after=("send", v - 1, h, k))
            if u16 and v:
                U = box("lU", v, h)
                cp("U" + s, box("lT", v, h, 0, 2), box("lU", v, h, 0, 2))
            else:
                U = b("U", h)
                cp("U" + s, U, Tl if v else ap("trav0", H - H * h, L - H * h))
            tab = TT if v else ap("tt32")
            gat("Hu" + s, b("Hu", h), tab, bo, "V")
            for name, a, z in pieces("x", h):
                gat(name, part("x", h, a, z), X, ap(U[0], U[1] + 32 * a, U[1] + 32 * z))
            for name, a, z in pieces("cy", h):
                gtt(name, part("cy", h, a, z), X, part("Hu", h, a, z), part("x", h, a, z), A.is_ge)
            bB = ap(bname, H * h, H * h + H)
            gat("bB" + s, bB, ap("BT"), bo, "S" if off("bB") else "V")
            gat("df" + s, dfb(h), ap("DF"), bo)
            if byP:
                mm("Tpre" + s, [(Tp, ap("If"), Tl)], "open")
            c1, Dp, td = pb(6, h), pb(6, 2 + h), b("td", h) if byP else pb(4 + h, 4)
            mm("vote" + s, [(c1, ap("In"), ap("kv"))] * off("tk" + s) + [(c1, smat("S512", k), b("cy", h, k, 1024, 16)) for k in range(16)])
            thr = (ap("par"), 4800.0, A.add, A.is_ge)
            if cfg["dh"] == "V":
                gtt("dH" + s, b("dH", h), tab, bo, Tl, A.subtract)
                Dp = b("tk", h) if off("tk" + s) else Dp
                step("tk" + s, Dp, c1, thr, ap("par"), 1.0)
                tt("td" + s, td, Dp, b("dH", h), A.mult)
            else:
                gat("dH" + s, b("dH", h), tab, bo, "S" if v else "V")
                mm("Tdh" + s, [(Dp, ap("If"), b("dH", h)), (Dp, ap("Ig"), Tl)])
                step("tk" + s, b("tk", h), c1, thr, ap("par"), 1.0)
                tt("td" + s, td, b("tk", h), Dp, A.mult)
            if byP:
                mm("Tadd" + s, [(Tp, ap("If"), td)], "close")
                cp("Tu" + s, b("Tu", h), Tp)
                terms = [(Bp, ap("Ihf"), Tl), (Bp, ap("Ihf"), td)]
            elif mh:
                tt("Tadd" + s, Tp, td, Tl, A.add)
                cp("Tu" + s, b("Tu", h), Tp)
            else:
                tt("Tadd" + s, b("td", h), td, Tl, A.add)
                cp("Tu" + s, b("Tu", h), b("td", h))
                terms = [(Tp, ap("If"), b("td", h)), (Bp, ap("Ihf"), b("td", h))]
            if mh:
                add("A8" + s, "S", lambda q, o=b("A8", h), bo=bo: [q.activation(o[3], ind(ap("BT"), bo), F.Identity, bias=T.cb[:], scale=148.0)],
                    [ap("BT"), bo, ap("cb")], [b("A8", h)], "g", H)
                terms = []
            else:
                terms += [(Bp, ap("J1"), ap("CH")), (Bp, ap("J1"), ap("CL")), (Bp, ap("Ifb" if off("bB") else "Jb"), bB)]
            terms += [(Cp, ap("If"), Cl)] * (cfg["rel"] == "V") + [(Fp, one(dfb(h)), dfb(h))] * cfg["dnm"]
            if terms:
                mm("Badd" + s, terms)
        cp("bl", ap("bl"), slot("lb", v, 0, 16))
        dp, up = pb(6, 4, 2), pb(6, 6, 2)
        terms = [(dp, one(ap(bname)), ap(bname)), (dp, ap("I1"), ap("CM"))]
        h64 = cfg.get("h64")
        for c in range(8 * bool(h64)):
            a, z, e = 16 * c, H * (c // 4 + 1), H * c
            ts("eq%d" % c, ap("eq", e, e + z - a), ap(bname, a, z), ap("bl", c + c // 4 * 4, c + c // 4 * 4 + 1), None, A.is_equal)
            terms.append((ap("pb6", 4 * H + a, 4 * H + a + 16), ap("TRn"), ap("eq", e, e + 16)))
            if a + 16 < z:
                terms.append((ap("pb6", 4 * H + a + 16, 4 * H + z), ap("BOn"), ap("eq", e + 16, e + z - a)))
        for c, name in enumerate(() if h64 else ("TRn", "BOn")):
            gtt("eq%d" % c, ap("eq", L * c, L * c + L), ap("bl"), ap("OF", 8 * c, 8 * c + 8), ap(bname), A.is_equal)
            terms.append((dp, ap(name), ap("eq", L * c, L * c + L)))
        mm("dup", terms)
        if not cfg["join"] or split:
            scan("es", ap("es", 0, L), ap("RD", 0, L), dp, 65536.0, A.min, A.max)
            cp("ou", ap("ou", 0, 8), ap("es", 15, L, 16))
        for h in range(2):
            s = str(h)
            Tp, Fp, Bp, Cp, dn, dm = (pb(4 + h, i) for i in range(6))
            for name, a, z in pieces("z", h):
                gat(name, part("z", h, a, z), X, part("Tu", h, a, z))
            for m, r, op0, op1 in (("mS", "RS", A.max, A.min), ("MS", "RM", A.min, A.max)):
                for name, a, z in pieces(m, h):
                    scan(name, ap(m, 1024 * h + 512 * a, 1024 * h + 512 * z), ap(r, 0, 512 * (z - a)), part("z", h, a, z), 0.0, op0, op1)
            mc = box("sT", v, h, 1)
            if u16 and not last:
                cp("mC" + s, box("sU", v, h, 1), mrow("mS", h))
            if u16 and mh:
                ts("mh" + s, mc, mrow("mS", h), 0.5, None, A.add)
            elif not u16 and (mh or not last):
                aff("mC" + s, mc, mrow("mS", h), 1, 0.5 * mh)
            if last:
                aff("yl" + s, ap("yl", H - H * h, L - H * h), mrow("mS", h), 1, 0)
            if mh:
                tt("q" + s, Bp, Tp, mc, A.mult)
                tt("s" + s, b("s", h), Bp, b("A8", h), A.add)
            else:
                mc = mrow("mS", h)
                tt("q" + s, b("q", h), Tp, mc, A.mult)
                tt("s" + s, b("s", h), b("q", h), Bp, A.add)
            if cfg["acc"]:
                tt("D" + s, b("D", h), mrow("mS", h), mrow("MS", h), A.subtract)
            n, nm = b("n", h, 0, H), b("n", h, H)
            ts("n" + s, n, b("s", h), 2, W - 1, A.logical_shift_right, A.bitwise_and)
            cp("nu" + s, b("nu", h), n)
            ts("nm" + s, nm, b("s", h), 2, B - 1, A.logical_shift_right, A.bitwise_and)
            if cfg["dnm"]:
                tt("dn" + s, pb(4 + h, 4, 2), b("n", h), pb(4 + h, 0, 2), A.subtract)
            else:
                tt("dm" + s, dm, nm, dfb(h), A.subtract)
                tt("dn" + s, dn, n, Tp, A.subtract)
            if cfg["rel"] == "S":
                mm("relp" + s, [(Cp, ap("Ig"), box("lT", v, h, 1)), (Cp, ap("I1"), mrow("mS", h))])
                act("rel" + s, b("rel", h), Cp, F.Sigmoid, -128.0, 256.0)
            else:
                tt("rel" + s, b("rel", h), mrow("mS", h) if u16 else mc, Cp if cfg["rel"] == "V" else box("lT", v, h, 1), A.is_gt)
        M, xt, ju = ap("MS", 15, 16 * L, 16), ap("xt"), ap("ou", 8, 16)
        byM = cfg["u"] == "M"
        if split:
            for h in range(2):
                s, M, up, a = str(h), mrow("MS", h), pb(6, 6 + h), W // 2 * (1 - h)
                dma("Y", "cp" + s, T.X2[:, a:a + W // 2], T.X[:, a:a + W // 2], [X, slot("lb", v, 1)], [ap("X2", a, a + W // 2)], 524288)
                ju, us, xs, xt = ap("ou", 8 + 4 * h, 12 + 4 * h), ap("es", L + H * h, L + H * h + H), ap("xs", H * h, H * h + H), ap("xt", H * h, H * h + H)
                mm("u" + s, [(up, ap(l), r) for l, r in (("I1", ap("kh", 0, H)), ("BOq", M), ("I1", ap("kC", 0, H)), ("In", ap("kC", 0, H)),
                                                         ("I1", ap("i32", H)), ("BOp", M), ("In", ap("MK", 0, H)))])
                scan("us" + s, us, ap("RD", L, L + H), up, 65536.0, A.min, A.max)
                cp("ju" + s, ju, ap("es", us[1] + 15, us[2], 16))
                gtt("xs" + s, xs, ap("X", a, a + W // 2), ju, M, A.add)
                ts("xt" + s, xt, xs, 1, None, A.logical_shift_right)
                sct("Xsc" + s, ap("X2", a, a + W // 2), ju, xt)
                dma("Y", "yc" + s, T.yclk[:, a:a + W // 2], T.X2[:, a:a + W // 2], [ap("X2", a, a + W // 2)], [], 524288)
            dma("Y", "yla", T.ylast[:], T.yl[:], [ap("yl")], [], 32768)
        else:
            update(v, last, byM, up, M, xt, ju)
        xt = ap("xt" if cfg["xs"] == "V" else "xb")
        for h in range(2):
            s = str(h)
            Tp, dn, dm, c2, nb, zz = pb(4 + h, 0), pb(4 + h, 4), pb(4 + h, 5), pb(4 + h, 6), pb(4 + h, 7), pb(7, h)
            for name, a, z in pieces("e", h):
                gat(name, part("e", h, a, z), X, part("nu", h, a, z))
            eng = [on("cm%d%d" % (h, q)) for q in range(2)]
            for name in ("mS", "MS"):
                for q in range(2):
                    bank = q + 2 * (h if cfg["own"] or cfg["acc"] else name == "MS")
                    d = ap("pb%d" % bank)
                    if cfg["acc"] and name == "MS":
                        mm("dif%s%d%d" % (name, h, q), [(pb(bank, j), ap("I1"), b("D", h)) for j in range(8)], "close")
                    else:
                        mm("pre%s%d%d" % (name, h, q), [(pb(bank, j), ap("In"), mrow(name, h)) for j in range(8)], "open")
                        mm("dif%s%d%d" % (name, h, q), [(pb(bank, j), ap("I1"), b("e", h, 8 * q + j, 1024, 16)) for j in range(8)], "close")
                    if name == "MS":
                        act("ab%d%d" % (h, q), part("ab", h, q, q + 1), d, F.Abs)
                    elif eng[q] == "V":
                        ts("cm%d%d" % (h, q), part("cm", h, q, q + 1), d, 0.0, None, A.is_ge)
                    else:
                        act("cm%d%d" % (h, q), part("cm", h, q, q + 1), d, F.Sign, 0.5)
            mm("crel" + s, [(c2, ap("Ik"), b("rel", h))], "open")
            for q in range(2):
                mm("cnt%d%d" % (h, q), [(c2, smat("S32" if eng[q] == "V" else "S16", p), b("cm", h, H * p, H * p + H))
                                        for p in range(8 * q, 8 * q + 8)], "close" if q else "mid")
            rdy, same = b("rdy", h), eng[0] == eng[1]
            step("rdy" + s, rdy, c2, (bound[eng[0]] if same else ap("t" + eng[0]), None, A.is_ge),
                 128 - 8 * bound[eng[0]] if same else ap("u" + eng[0]), 8.0)
            tt("te" + s, b("te", h), rdy, dn, A.mult)
            if off("Tf" + s):
                Fp = pb(4 + h, 2)
                mm("Tfp" + s, [(Fp, ap("If"), r) for r in [box("lT", v, h)] * byP + [b("td", h), b("te", h)]])
                act("Tf" + s, box("sT", v, h), Fp, F.Copy)
            else:
                tt("Tf" + s, box("sT", v, h), b("te", h), Tp, A.add)
            if u16 and not last:
                cp("Uo" + s, box("sU", v, h), box("sT", v, h))
            if h64:
                sct("Tsc%d1" % h, ap("TT"), ap("ou", 4 * h, 4 * h + 4), box("sT", v, h))
            for j in () if h64 else (1, 0):
                o = box("sT", v, h)[1] + 32 * j
                sct("Tsc%d%d" % (h, j), ap("TT"), ap("ou", 4 * h + 2 * j, 4 * h + 2 * j + 2), ap("sT", o, o + 32))
            mm("npre" + s, [(nb, one(dfb(h)), dfb(h)), (nb, ap("I1"), ap("MK", 0, H))], "open")
            for q in range(2):
                mm("sco%d%d" % (h, q), [(zz, ap("I1"), ap("PC"))] * (1 - q) +
                   [(zz, smat("S16", p), b("ab", h, H * p, H * p + H)) for p in range(8 * q, 8 * q + 8)], "mid" if q else "open")
            mm("srdy" + s, [(zz, ap("Ik"), rdy)], "close")
            vt("kT" + s, b("kT", h), zz)
            scan("kr" + s, b("kr", h), ap("RK"), b("kT", h), 65536.0, A.min, A.max)
            gtt("qT" + s, b("qT", h), b("kr", h), ap("OF", 16), b("kT", h), A.is_equal)
            vt("oh" + s, b("oh", h), b("qT", h))
            tt("sel" + s, b("sel", h), b("oh", h), dm, A.mult)
            mm("nsel" + s, [(nb, ap("BOh"), b("sel", h))], "close")
            scan("ex" + s, b("ex", h), ap("RS", 0, H), nb, 0.0, A.max, A.min)
            if not last:
                cp("sb" + s, slot("sb", v, h), b("ex", h, 15, H, 16))
                src, dst = ("sU", "lU") if u16 else ("sT", "lT")
                if "%d@%d" % (h, v + 1) in cfg["C"]:
                    post("c", h, box(src, v, h, 1), box(dst, v + 1, h, 1))
                    post("T", h, box(src, v, h), box(dst, v + 1, h))
                else:
                    post("T", h, box(src, v, h, 0, 2), box(dst, v + 1, h, 0, 2))
                post("b", h, slot("sb", v, h, 8), slot("lb", v + 1, h, 8))
        if last:
            for h in range(2):
                aff("ys%d" % h, ap("ys", 4 - 4 * h, 8 - 4 * h), b("ex", h, 15, H, 16), 1, 0)
            dma("Y", "ytr", T.ytrav[:], box("sT", v, 1, 0, 2)[3], [box("sT", v, 1, 0, 2)], [], 65536)
            dma("S", "ysl", T.yslot[:], T.ys[:], [ap("ys")], [], 4096)
            dma("Y", "ytt", T.yttab[:], TT[3], [TT], [], 524288)
        else:
            sct("Xsc", X, ju, xt)
            sg = pb(7, 2, 2)
            mm("sg", [(sg, ap("I1"), ap("ones"))] + [(sg, ap("BOq"), ap("hoh"))] * 2)
            sg = ap("pb7", 2 * H, 4 * H + 1)
            add("par", "V", lambda q, sg=sg: [q.tensor_reduce(T.par[:], sg[3], AxisListType.X, A.mult)], [sg], [ap("par")], "v", L + 1)

    used, kept = set(), []
    for o in reversed(ops):
        if o["name"][0] != "." or o["wr"][0][0] in used:
            kept.append(o)
            used.update(x[0] for x in o["rd"] + o["wr"])
    ops = kept[::-1]

    hist, tags, closed, whole = {}, {}, {}, {}
    for i, o in enumerate(ops):
        dep = set()
        acc = [(x, False) for x in o["rd"]] + [(x, True) for x in o["wr"]]
        for x, isw in acc:
            for j, a, z, w in hist.get(x[0], ()):
                if (isw or w) and a < x[2] and x[1] < z:
                    dep.add(j)
        for x, isw in acc:
            old = hist.get(x[0], [])
            if isw and (x[2] - x[1]) == cnt(x):
                old = [y for y in old if not (x[1] <= y[1] and y[2] <= x[2])]
            hist[x[0]] = old + [(i, x[1], x[2], isw)]
        o["banks"] = sorted({x[0] for x, isw in acc if SCRATCH[x[0]][0] == "psum"})
        if o["kind"] == "pe":
            bank = o["banks"][0]
            if o["part"] in ("whole", "open") and bank in closed:
                dep.add(closed[bank])
            if o["part"] == "open":
                dep.update(whole.pop(bank, []))
                closed[bank] = i
            elif o["part"] == "whole":
                whole.setdefault(bank, []).append(i)
            else:
                dep.add(closed[bank])
                closed[bank] = i
        if o["kind"] == "arr":
            dep = {tags[o["after"]]}
        if "tag" in o:
            tags[o["tag"]] = i
        if "behind" in o:
            dep.add(ops.index(o["behind"]))
        dep.discard(i)
        o["dep"] = sorted(dep)
    return ops


def rank_program(g, core, T, topo):
    rank = T.rank_of(core)
    if rank is None:
        return
    nxt, prv = T.cores[(rank + STEP) % N], T.cores[(rank - STEP) % N]
    rid, pid, _ = topo.addr(nxt)
    n_out, n_in = len(topo.engines(core, nxt)), len(topo.engines(prv, core))

    def send(dst, src, sem):
        return g.remote_dma(dst, src, T.sem[sem], T.sem.sent, pid, rid, topo.mask(core, nxt))

    ops = build(T, send, CONFIG)
    todo, order = {}, []
    for i, o in enumerate(ops):
        todo.setdefault(o["name"], []).append(i)
    for name in ORDER.split():
        i = todo[name].pop(0)
        order += [i] + [j for j in todo["arr"] if ops[j]["dep"] == [i]]
    assert sorted(order) == list(range(len(ops)))
    queue = {"V": g.vector, "S": g.scalar, "P": g.tensor, "G": g, "Y": g.sync}
    total = {}
    known = {e: {} for e in queue}
    bank = {}
    for pos, i in enumerate(order):
        o = ops[i]
        e = o["eng"]
        o["pos"] = pos
        if o["kind"] == "arr":
            o["sig"], o["seen"] = (o["sem"], n_in), {}
            total[o["sem"]] = n_in
            continue
        dep = [j for j in o["dep"] if o.get("behind") is not ops[j]]
        for k in o["banks"]:
            dep += [j for e2, j in bank.get(k, {}).items() if e2 != e]
            bank.setdefault(k, {})[e] = i
        need = {}
        for j in dep:
            if e == "P" and ops[j]["eng"] == "P":
                continue
            s, c = ops[j]["sig"]
            if c > need.get(s, (0, 0))[0]:
                need[s] = (c, j)
        for s, (c, j) in sorted(need.items(), key=lambda x: -ops[x[1][1]]["pos"]):
            if known[e].get(s, 0) >= c:
                continue
            queue[e].wait_ge(T.sem[s], c)
            known[e][s] = c
            for s2, c2 in ops[j]["seen"].items():
                if c2 > known[e].get(s2, 0):
                    known[e][s2] = c2
        ins = o["fn"](queue[e])
        if o["kind"] == "send":
            total["sent"] = total.get("sent", 0) + n_out
            continue
        s, step = (o["sem"], 16) if o["kind"] == "dma" else ("c" + e, 1)
        for x in ins:
            x.then_inc(T.sem[s], step)
            total[s] = total.get(s, 0) + step
        o["sig"], o["seen"] = (s, total[s]), dict(known[e])
    for s, c in total.items():
        g.wait_ge(T.sem[s], c)
